import numpy as np
import ml_dtypes


def mxq(x, axis, fmt="e4m3"):
    dtype, down = {"e4m3": (ml_dtypes.float8_e4m3fn, 7), "e5m2": (ml_dtypes.float8_e5m2, 14)}[fmt]
    v = np.moveaxis(np.asarray(x, np.float32).astype(ml_dtypes.bfloat16).astype(np.float64), axis, -1)
    blocks = v.reshape(v.shape[:-1] + (-1, 32))
    amax = np.abs(blocks).max(-1, keepdims=True)
    byte = np.maximum(np.where(amax > 0, np.frexp(amax)[1] - 1 + 127, 0) - down, 1)
    scale = np.exp2(byte - 127.0)
    codes = (blocks / scale).astype(np.float32).astype(dtype).astype(np.float64)
    return np.moveaxis((codes * scale).reshape(v.shape), -1, axis)


WIDE = False


def mx_kscale(k):
    if not WIDE:
        return np.ones(k)
    levels = np.array([10, -10, 5, -5, 0])
    if k % 512:
        return np.exp2(np.random.permutation(np.resize(levels, k // 32))).repeat(32)
    a = np.empty((k // 512, 16))
    for p in range(k // 512):
        a[p, :8] = np.random.permutation(np.resize(levels, 8))
        for g in range(8):
            far = levels[np.abs(levels - a[p, g]) >= 10]
            a[p, g + 8] = far[np.random.randint(len(far))]
    return np.exp2(a.ravel()).repeat(32)


BF16 = ml_dtypes.bfloat16


def bf(x):
    return np.asarray(x, np.float32).astype(BF16)


def f64(x):
    return np.asarray(x).astype(np.float64)


E2M1 = np.array([0.0, 0.5, 1.0, 1.5, 2.0, 3.0, 4.0, 6.0, -0.0, -0.5, -1.0, -1.5, -2.0, -3.0, -4.0, -6.0])


def pack_weight(w, fmt):
    k, n = w.shape
    w = f64(bf(w)).reshape(k // 32, 32, n)
    amax = np.abs(w).max(1)
    if fmt == "e4m3":
        byte = np.frexp(amax)[1] - 1 + 127 - 7
    else:
        mant, ex = np.frexp(amax / 6.0)
        byte = np.where(mant > 0.5, ex, ex - 1) + 127
    byte = np.clip(np.where(amax > 0, byte, 1), 1, 254)
    scaled = (w * np.exp2(127.0 - byte)[:, None, :]).reshape(k, n).astype(np.float32)
    by_word = np.ascontiguousarray(scaled.reshape(k // 512, 128, 4, n).transpose(0, 1, 3, 2))
    if fmt == "e4m3":
        words = by_word.astype(ml_dtypes.float8_e4m3fn).view(np.uint8)
    else:
        c = by_word.astype(ml_dtypes.float4_e2m1fn).view(np.uint8) & 0xF
        words = c[..., 0::2] | (c[..., 1::2] << 4)
    return np.ascontiguousarray(words), np.ascontiguousarray(byte.astype(np.uint8).reshape(k // 512, 16, n))


def unpack_weight(words, scales, fmt):
    g, p, n, _ = words.shape
    if fmt == "e4m3":
        vals = np.ascontiguousarray(words).view(ml_dtypes.float8_e4m3fn).astype(np.float64)
    else:
        nib = np.empty((g, p, n, 4), np.uint8)
        nib[..., 0::2] = words & 0xF
        nib[..., 1::2] = words >> 4
        vals = E2M1[nib]
    vals = vals * np.repeat(np.exp2(scales.astype(np.float64) - 127.0), 8, axis=1)[..., None]
    return vals.transpose(0, 1, 3, 2).reshape(g * 512, n)
def pack4(w):
    words, scales = pack_weight(w, "e2m1")
    return words.reshape(words.shape[0], 128, -1), scales


def unpack4(words, scales):
    return unpack_weight(words.reshape(words.shape[0], 128, -1, 2), scales, "e2m1")


def planes(Y):
    n, m = Y.shape
    b = f64(bf(Y)).reshape(n // 32, 32, m)
    amax = np.abs(b).max(1)
    byte = np.clip(np.where(amax > 0, np.frexp(amax)[1] - 1 + 127 - 7, 1), 1, 254)
    codes = (b * np.exp2(127.0 - byte)[:, None, :]).reshape(n, m).astype(np.float32).astype(ml_dtypes.float8_e4m3fn).view(np.uint8)
    words = codes.reshape(n // 512, 128, 4, m).transpose(0, 1, 3, 2)
    return np.ascontiguousarray(words), np.ascontiguousarray(byte.astype(np.uint8).reshape(n // 512, 16, m))


B, T, D, F, R = 2, 1024, 512, 512, 512


def setup_inputs():
    sf, sr = mx_kscale(D), mx_kscale(D)
    t = mx_kscale(T)
    xf = bf(np.random.standard_normal((B, T, D)) * sf * t[None, :, None])
    xr = bf(np.random.standard_normal((B, T, D)) * sr)
    wf_words, wf_scales = pack4(np.random.standard_normal((D, F)) / np.sqrt(D) / sf[:, None])
    wr_words, wr_scales = pack4(np.random.standard_normal((D, R)) / np.sqrt(D) / sr[:, None])
    return {
        "xf": xf,
        "xr": xr,
        "wf_words": wf_words,
        "wf_scales": wf_scales,
        "wr_words": wr_words,
        "wr_scales": wr_scales,
        "g": bf((1.0 + 0.1 * np.random.standard_normal((B, T))) / t[None, :]),
        "m0": bf(np.random.standard_normal((B, F, R))),
        "decay": bf(np.random.uniform(0.5, 0.95, R)),
    }


def core(xf, xr, wf_words, wf_scales, wr_words, wr_scales, g, m0, decay):
    fil = mxq(f64(xf), 2, "e4m3") @ unpack4(wf_words, wf_scales)
    rol = np.tanh(mxq(f64(xr), 2, "e4m3") @ unpack4(wr_words, wr_scales)) * f64(g)[:, :, None]
    bind = mxq(fil, 1, "e4m3").transpose(0, 2, 1) @ mxq(rol, 1, "e4m3")
    return f64(decay)[None, None, :] * f64(m0) + bind / np.sqrt(T)


def reference(xf, xr, wf_words, wf_scales, wr_words, wr_scales, g, m0, decay):
    R_out = core(xf, xr, wf_words, wf_scales, wr_words, wr_scales, g, m0, decay)
    words, scales = planes(np.moveaxis(R_out, 1, 0).reshape(512, -1))
    return R_out, words, scales

@@ -1,0 +1,314 @@
+from contextlib import ExitStack
+
+import concourse.mybir as mybir
+from concourse.masks import make_identity
+
+B, T, D, F, R = 2, 1024, 512, 512, 512
+FLOPS = 2 * B * T * D * (F + R) + 2 * B * T * F * R
+
+F32 = mybir.dt.float32
+BF16 = mybir.dt.bfloat16
+U32 = mybir.dt.uint32
+I32 = mybir.dt.int32
+U8 = mybir.dt.uint8
+FP8X4 = mybir.dt.float8_e4m3fn_x4
+FP4X4 = mybir.dt.float4_e2m1fn_x4
+ACT = mybir.ActivationFunctionType
+ALU = mybir.AluOpType
+
+P = 128
+PACK = 4
+KP = P * PACK
+CH = 128
+NCH = 4
+NG = 8
+BANKS = 8
+WARM = 0
+VEC_X = ((0, 1), (2, 0), (3, 0), (4, 0))
+VEC_F = ()
+
+
+def tile_tensorproductrolefillerwrite_x2_kernel(
+    tc, xf, xr, wf_words, wf_scales, wr_words, wr_scales, g, m0, decay, out_0, out_1, out_2
+):
+    nc = tc.nc
+    with ExitStack() as ctx:
+        sb = ctx.enter_context(tc.tile_pool(name="sb", bufs=1))
+        ps = ctx.enter_context(tc.psum_pool(name="ps", bufs=1))
+        ctx.enter_context(tc.manual_schedule())
+
+        def sbt(name, shape, dtype, tag=None):
+            return sb.tile(shape, dtype, name=name, tag=tag or name, align_bytes=64)
+
+        banks_taken = []
+
+        def bank(kind, shape):
+            n = len(banks_taken)
+            banks_taken.append(kind)
+            return ps.tile(shape, F32, name="%s%d" % (kind, n), tag="bank%d" % (n % BANKS))
+
+        def group(i):
+            return i % 2, i // 4, (i // 2) % 2
+
+        x_raw, x_t, x_q, x_s, y_bf, y_q, y_s, tp, mm, th = {}, {}, {}, {}, {}, {}, {}, {}, {}, {}
+        m_raw, dm, res, res_bf = {}, {}, {}, {}
+
+        ident = sbt("ident", [P, P], F32)
+        w_words = [sbt("ww%d" % o, [P, 2 * F], U8) for o in range(2)]
+        w_scale = [sbt("ws%d" % o, [P, F], U8) for o in range(2)]
+        g_sb = sbt("g_sb", [P, B * 2, PACK], BF16)
+        d_col = sbt("d_col", [P, PACK], BF16)
+        d_row = sbt("d_row", [P, R], BF16)
+        warm = sbt("warm", [P, 1], F32)
+        o_q = sbt("o_q", [P, B * R], U32)
+        o_s = sbt("o_s", [P, B * R], U8)
+
+        def load_x(i, h):
+            role, b, half = group(i)
+            src = (xr if role else xf)[b, half * KP:(half + 1) * KP, :].rearrange("(p j) d -> p j d", j=PACK)
+            x_raw[i, h] = sbt("xraw%d_%d" % (i, h), [P, 2, D], BF16)
+            nc.sync.dma_start(out=x_raw[i, h][:], in_=src[:, 2 * h:2 * h + 2, :])
+
+        def load_w(o):
+            nc.sync.dma_start(out=w_words[o][:].bitcast(I32), in_=(wf_words, wr_words)[o][0].bitcast(I32))
+
+        def load_ws(o):
+            src = (wf_scales, wr_scales)[o][0].bitcast(I32)
+            for q in range(4):
+                nc.scalar.dma_start(out=w_scale[o][:].bitcast(I32)[32 * q:32 * q + 4, :], in_=src[4 * q:4 * q + 4, :])
+
+        def load_m(b, h):
+            m_raw[b, h] = sbt("m%d_%d" % (b, h), [P, 2, R], BF16)
+            nc.sync.dma_start(out=m_raw[b, h][:], in_=m0[b].rearrange("(p j) r -> p j r", j=PACK)[:, 2 * h:2 * h + 2, :])
+
+        def transp(i, h):
+            tp[i, h] = bank("tp", [P, 2, 2, P])
+            words = x_raw[i, h][:].rearrange("p j d -> p (j d)").bitcast(F32)
+            for j in range(2):
+                for u in range(2):
+                    nc.tensor.transpose(tp[i, h][:, j, u, :], words[:, 256 * j + u:256 * (j + 1):2], ident[:])
+
+        def xcopy(i, h):
+            on_vector = (i, h) in VEC_X
+            if h == 0:
+                x_t[i] = sbt("xt%d" % i, [P, PACK * P * PACK], BF16, tag="xt%d" % (i % 3))
+            dst = x_t[i][:].bitcast(F32)[:, 512 * h:512 * (h + 1)].rearrange("p (j m u) -> p j m u", j=2, u=2)
+            src = tp[i, h][:].rearrange("p j u m -> p j m u")
+            if on_vector:
+                nc.vector.tensor_copy(out=dst, in_=src)
+            else:
+                nc.scalar.copy(out=dst, in_=src)
+
+        def xquant(i, h0=0, h1=2):
+            if h0 == 0:
+                x_q[i] = sbt("xq%d" % i, [P, KP], U32, tag="xq%d" % (i % 3))
+                x_s[i] = sbt("xs%d" % i, [P, KP], U8, tag="xs%d" % (i % 3))
+            nc.vector.quantize_mx(out=x_q[i][:, 256 * h0:256 * h1].bitcast(FP8X4), scales=x_s[i][:, 256 * h0:256 * h1], in_=x_t[i][:, 1024 * h0:1024 * h1])
+
+        def mm1(i, c):
+            o = group(i)[0]
+            mm[i, c] = bank("mm", [P, PACK, CH])
+            for j in range(PACK):
+                nc.tensor.matmul_mx(
+                    out=mm[i, c][:, j, :],
+                    lhsT=x_q[i][:, P * j:P * (j + 1)].bitcast(FP8X4), lhsT_scale=x_s[i][:, P * j:P * (j + 1)],
+                    rhs=w_words[o][:, 2 * CH * c:2 * CH * (c + 1)].bitcast(FP4X4), rhs_scale=w_scale[o][:, CH * c:CH * (c + 1)],
+                    start=True, stop=True)
+
+        def new_y(i):
+            y_bf[i] = sbt("y%d" % i, [P, F * PACK], BF16, tag="y%d" % (i % 3))
+            y_q[i] = sbt("yq%d" % i, [P, F], U32)
+            y_s[i] = sbt("ys%d" % i, [P, F], U8)
+
+        def fil_out(i, c):
+            on_vector = (i, c) in VEC_F
+            if c == 0:
+                new_y(i)
+            dst = y_bf[i][:].rearrange("p (a m t) -> p a m t", a=PACK, t=PACK)[:, :, 32 * c:32 * (c + 1), :]
+            src = mm[i, c][:].rearrange("p t (m a) -> p a m t", a=PACK)
+            if on_vector:
+                nc.vector.tensor_copy(out=dst, in_=src)
+            else:
+                nc.scalar.copy(out=dst, in_=src)
+
+        def tanh_out(i, c):
+            if c == 0:
+                th[i] = sbt("th%d" % i, [P, R, PACK], F32, tag="th%d" % ((i // 2) % 2))
+            nc.scalar.activation(out=th[i][:, CH * c:CH * (c + 1), :], in_=mm[i, c][:].rearrange("p t n -> p n t"), func=ACT.Tanh)
+
+        def gmul(i, c0, c1):
+            if c0 == 0:
+                new_y(i)
+            dst = y_bf[i][:, CH * PACK * c0:CH * PACK * c1].rearrange("p (n t) -> p n t", t=PACK)
+            gate = g_sb[:, i // 2, :].unsqueeze(1).to_broadcast([P, CH * (c1 - c0), PACK])
+            nc.vector.tensor_tensor(out=dst, in0=th[i][:, CH * c0:CH * c1, :], in1=gate, op=ALU.mult)
+
+        def yquant(i, c0, c1):
+            nc.vector.quantize_mx(out=y_q[i][:, CH * c0:CH * c1].bitcast(FP8X4), scales=y_s[i][:, CH * c0:CH * c1],
+                                  in_=y_bf[i][:, CH * PACK * c0:CH * PACK * c1])
+
+        def decay_mul(b, h):
+            if h == 0:
+                dm[b] = sbt("dm%d" % b, [P, PACK, R], F32)
+            row = d_row[:].unsqueeze(1).to_broadcast([P, 2, R])
+            nc.vector.tensor_tensor(out=dm[b][:, 2 * h:2 * h + 2, :], in0=m_raw[b, h][:], in1=row, op=ALU.mult)
+
+        def mm2_pass(out, b, a, half, cols):
+            fi = 4 * b + 2 * half
+            nc.tensor.matmul_mx(
+                out=out,
+                lhsT=y_q[fi][:, P * a:P * (a + 1)].bitcast(FP8X4), lhsT_scale=y_s[fi][:, P * a:P * (a + 1)],
+                rhs=y_q[fi + 1][:, cols].bitcast(FP8X4), rhs_scale=y_s[fi + 1][:, cols],
+                start=(half == 0), stop=(half == 1))
+
+        def mm2_rows(b, a):
+            mm["o", b, a] = bank("mm", [P, R])
+            for half in range(2):
+                mm2_pass(mm["o", b, a][:], b, a, half, slice(0, R))
+
+        def finish_rows(b, a):
+            if a == 0:
+                res[b] = sbt("res%d" % b, [P, PACK, R], F32)
+            nc.vector.scalar_tensor_tensor(out=res[b][:, a, :], in0=mm["o", b, a][:], scalar=1.0 / 32.0, in1=dm[b][:, a, :], op0=ALU.mult, op1=ALU.add)
+            if a == PACK - 1:
+                nc.sync.dma_start(out=out_0[b].rearrange("(p a) r -> p a r", a=PACK), in_=res[b][:])
+
+        def mm2_cols(b, c):
+            mm["o", b, c] = bank("mm", [P, PACK, CH])
+            for a in range(PACK):
+                for half in range(2):
+                    mm2_pass(mm["o", b, c][:, a, :], b, a, half, slice(CH * c, CH * (c + 1)))
+
+        def finish_cols(b, c):
+            res[b, c] = sbt("res%d_%d" % (b, c), [P, PACK, CH], F32)
+            nc.vector.scalar_tensor_tensor(out=res[b, c][:], in0=mm["o", b, c][:], scalar=1.0 / 32.0, in1=dm[b][:, :, CH * c:CH * (c + 1)],
+                                           op0=ALU.mult, op1=ALU.add)
+            nc.sync.dma_start(out=out_0[b].rearrange("(p a) r -> p a r", a=PACK)[:, :, CH * c:CH * (c + 1)], in_=res[b, c][:])
+
+        def round_out(key, src, on_vector=False):
+            res_bf[key] = sbt("rb%d_%d" % key, [P, src.shape[2] * PACK], BF16)
+            dst = res_bf[key][:].rearrange("p (n i a) -> p n a i", a=PACK, i=4)
+            src = src.rearrange("p a (n i) -> p n a i", i=4)
+            if on_vector:
+                nc.vector.tensor_copy(out=dst, in_=src)
+            else:
+                nc.scalar.copy(out=dst, in_=src)
+
+        def oquant(key, c0, c1):
+            nc.vector.quantize_mx(out=o_q[:, c0:c1].bitcast(FP8X4), scales=o_s[:, c0:c1], in_=res_bf[key][:])
+
+        def store_words(c0, c1):
+            dst = out_1[0].rearrange("p m t -> p (m t)").bitcast(I32)
+            nc.sync.dma_start(out=dst[:, c0:c1], in_=o_q[:].bitcast(I32)[:, c0:c1])
+
+        def store_scales():
+            for q in range(4):
+                eng = nc.scalar if q % 2 else nc.sync
+                eng.dma_start(out=out_2[0].bitcast(I32)[4 * q:4 * q + 4, :], in_=o_s[:].bitcast(I32)[32 * q:32 * q + 4, :])
+
+        load_x(0, 0)
+        nc.scalar.dma_start(out=d_col[:], in_=decay.rearrange("(p j) -> p j", j=PACK))
+        make_identity(nc, ident[:])
+        for o in range(2):
+            nc.vector.memset(w_scale[o][:].bitcast(I32), 0)
+        nc.vector.memset(warm[:], 0.0)
+        if WARM:
+            z_bf = sbt("z_bf", [P, KP], BF16)
+            z_q = sbt("z_q", [P, P], U32)
+            z_s = sbt("z_s", [P, P], U8)
+            nc.gpsimd.memset(z_bf[:].bitcast(I32), 0)
+            nc.vector.quantize_mx(out=z_q[:].bitcast(FP8X4), scales=z_s[:], in_=z_bf[:])
+            z_ps = bank("mm", [P, PACK, P])
+            for n in range(WARM):
+                nc.tensor.matmul_mx(out=z_ps[:, n % PACK, :], lhsT=z_q[:].bitcast(FP8X4), lhsT_scale=z_s[:], rhs=z_q[:].bitcast(FP8X4), rhs_scale=z_s[:], start=True, stop=True)
+        load_ws(0)
+        nc.scalar.activation(out=warm[:], in_=warm[:], func=ACT.Tanh)
+        load_x(0, 1)
+        load_x(1, 0)
+        load_w(0)
+        load_x(1, 1)
+        load_m(0, 0)
+        load_m(0, 1)
+        load_w(1)
+        load_ws(1)
+        nc.sync.dma_start(out=g_sb[:], in_=g.rearrange("b (h p t) -> p (b h) t", h=2, t=PACK))
+        load_x(2, 0)
+        load_x(2, 1)
+        load_m(1, 0)
+        load_m(1, 1)
+        for i in range(3, NG):
+            load_x(i, 0)
+            load_x(i, 1)
+
+        transp(0, 0)
+        transp(0, 1)
+        d_ps = bank("mm", [P, 2, P])
+        for u in range(2):
+            nc.tensor.transpose(d_ps[:, u, :], d_col[:].bitcast(F32)[:, u:u + 1].to_broadcast([P, P]), ident[:])
+        transp(1, 0)
+        transp(1, 1)
+        xcopy(0, 0)
+        xcopy(0, 1)
+        xquant(0, 0, 1)
+        nc.vector.tensor_copy(out=d_row[:].bitcast(F32).rearrange("p (m u) -> p m u", u=2), in_=d_ps[:].rearrange("p u m -> p m u"))
+        xquant(0, 1, 2)
+        decay_mul(0, 0)
+        for c in range(NCH):
+            mm1(0, c)
+
+        for i in range(NG):
+            role = group(i)[0]
+            last = i == NG - 1
+            if not last:
+                xcopy(i + 1, 0)
+                xcopy(i + 1, 1)
+            if i > 0 and not role:
+                gmul(i - 1, 2, 4)
+            if not last:
+                xquant(i + 1)
+            if i > 0:
+                yquant(i - 1, 0, NCH)
+            if i + 2 < NG:
+                transp(i + 2, 0)
+                transp(i + 2, 1)
+            if i == 0:
+                decay_mul(0, 1)
+                decay_mul(1, 0)
+            if i == 2:
+                decay_mul(1, 1)
+            if i in (4, 6):
+                for a in (i - 4, i - 3):
+                    mm2_rows(0, a)
+                for a in (i - 4, i - 3):
+                    finish_rows(0, a)
+            for c in range(NCH):
+                if role:
+                    tanh_out(i, c)
+                    if not last and c == 1:
+                        gmul(i, 0, 2)
+                else:
+                    fil_out(i, c)
+                if not last:
+                    mm1(i + 1, c)
+
+        i = NG - 1
+        round_out((0, 0), res[0][:])
+        gmul(i, 0, 1)
+        for s in range(NCH + 2):
+            if s + 1 < NCH:
+                gmul(i, s + 1, s + 2)
+            if s < NCH:
+                yquant(i, s, s + 1)
+                mm2_cols(1, s)
+            if s == NCH - 1:
+                oquant((0, 0), 0, R)
+                store_words(0, R)
+            if 0 <= s - 1 < NCH:
+                finish_cols(1, s - 1)
+            if 0 <= s - 2 < NCH - 1:
+                oquant((1, s - 2), R + CH * (s - 2), R + CH * (s - 1))
+            if 0 <= s - 1 < NCH:
+                round_out((1, s - 1), res[1, s - 1][:], on_vector=(s == NCH))
+        oquant((1, NCH - 1), R + CH * (NCH - 1), 2 * R)
+        store_words(R, 2 * R)
+        store_scales()

@@ -23,9 +23,18 @@ CH = 128
 NCH = 4
 NG = 8
 BANKS = 8
-WARM = 0
-VEC_X = ((0, 1), (2, 0), (3, 0), (4, 0))
-VEC_F = ()
+WARM = 10
+ORDER = """
+D DC U00 T00 X00 Q00 T01 T10 X01 Q01 T11 X10 M00 X11 U01 F00 M01 M02
+Q1 U10 U11 M03 F01 M10 T20 T21 F02 F03 H10 X20 M11 M12 H11 T30 T31 X21v
+Y0 H12 Q2 X30 X31 G10 M13 M20 H13 F20 T40 T41 Q3 X40 M21 M22 F21 G12
+M23 M30 X41v T50 F22 F23 M31 Y1 H30 H31 M32 M33 T51 Q4 M40 M41 X50v H32
+H33 F40 Y2 T60 T61 G30 G32 M42 M43 X51 X60 X61 F41v T70 F42 F43 Y3 T71
+X70 A0 Q5 Q6 M50 A1 X71 M51 M52 M53 Y4 S0 S1 H50 Q7 M60 A2 H51
+H52 G50 H53 G52 A3 S2 F60 M61 F61 M62 M63 Y5 F62 F63 M70 M71 M72 H70
+S3 G70 Y6 Y70 M73 H71 H72 G71 G72 Y71 R00 B0 B1 Z0 H73 Y72 B2 R10
+G73 R01 Z1 Y73 Z2 O00 O01 R11 B3 Z3 R12v R13 O10 O11 O12 O13
+"""
 
 
 def tile_tensorproductrolefillerwrite_x2_kernel(
@@ -40,12 +49,16 @@ def tile_tensorproductrolefillerwrite_x2_kernel(
         def sbt(name, shape, dtype, tag=None):
             return sb.tile(shape, dtype, name=name, tag=tag or name, align_bytes=64)
 
-        banks_taken = []
+        free_banks = list(range(BANKS))
+        held = {}
 
-        def bank(kind, shape):
-            n = len(banks_taken)
-            banks_taken.append(kind)
-            return ps.tile(shape, F32, name="%s%d" % (kind, n), tag="bank%d" % (n % BANKS))
+        def take_bank(key, shape):
+            held[key] = free_banks[0]
+            free_banks.remove(held[key])
+            return ps.tile(shape, F32, name="ps_%s" % key, tag="bank%d" % held[key])
+
+        def give_bank(key):
+            free_banks.append(held[key])
 
         def group(i):
             return i % 2, i // 4, (i // 2) % 2
@@ -72,26 +85,26 @@ def tile_tensorproductrolefillerwrite_x2_kernel(
         def load_w(o):
             nc.sync.dma_start(out=w_words[o][:].bitcast(I32), in_=(wf_words, wr_words)[o][0].bitcast(I32))
 
-        def load_ws(o):
+        def load_ws(o, queues):
             src = (wf_scales, wr_scales)[o][0].bitcast(I32)
             for q in range(4):
-                nc.scalar.dma_start(out=w_scale[o][:].bitcast(I32)[32 * q:32 * q + 4, :], in_=src[4 * q:4 * q + 4, :])
+                queues[q].dma_start(out=w_scale[o][:].bitcast(I32)[32 * q:32 * q + 4, :], in_=src[4 * q:4 * q + 4, :])
 
         def load_m(b, h):
             m_raw[b, h] = sbt("m%d_%d" % (b, h), [P, 2, R], BF16)
             nc.sync.dma_start(out=m_raw[b, h][:], in_=m0[b].rearrange("(p j) r -> p j r", j=PACK)[:, 2 * h:2 * h + 2, :])
 
         def transp(i, h):
-            tp[i, h] = bank("tp", [P, 2, 2, P])
+            tp[i, h] = take_bank("T%d%d" % (i, h), [P, 2, 2, P])
             words = x_raw[i, h][:].rearrange("p j d -> p (j d)").bitcast(F32)
             for j in range(2):
                 for u in range(2):
                     nc.tensor.transpose(tp[i, h][:, j, u, :], words[:, 256 * j + u:256 * (j + 1):2], ident[:])
 
-        def xcopy(i, h):
-            on_vector = (i, h) in VEC_X
+        def xcopy(i, h, on_vector):
+            give_bank("T%d%d" % (i, h))
             if h == 0:
-                x_t[i] = sbt("xt%d" % i, [P, PACK * P * PACK], BF16, tag="xt%d" % (i % 3))
+                x_t[i] = sbt("xt%d" % i, [P, PACK * P * PACK], BF16)
             dst = x_t[i][:].bitcast(F32)[:, 512 * h:512 * (h + 1)].rearrange("p (j m u) -> p j m u", j=2, u=2)
             src = tp[i, h][:].rearrange("p j u m -> p j m u")
             if on_vector:
@@ -101,13 +114,13 @@ def tile_tensorproductrolefillerwrite_x2_kernel(
 
         def xquant(i, h0=0, h1=2):
             if h0 == 0:
-                x_q[i] = sbt("xq%d" % i, [P, KP], U32, tag="xq%d" % (i % 3))
-                x_s[i] = sbt("xs%d" % i, [P, KP], U8, tag="xs%d" % (i % 3))
+                x_q[i] = sbt("xq%d" % i, [P, KP], U32)
+                x_s[i] = sbt("xs%d" % i, [P, KP], U8)
             nc.vector.quantize_mx(out=x_q[i][:, 256 * h0:256 * h1].bitcast(FP8X4), scales=x_s[i][:, 256 * h0:256 * h1], in_=x_t[i][:, 1024 * h0:1024 * h1])
 
         def mm1(i, c):
             o = group(i)[0]
-            mm[i, c] = bank("mm", [P, PACK, CH])
+            mm[i, c] = take_bank("M%d%d" % (i, c), [P, PACK, CH])
             for j in range(PACK):
                 nc.tensor.matmul_mx(
                     out=mm[i, c][:, j, :],
@@ -116,12 +129,12 @@ def tile_tensorproductrolefillerwrite_x2_kernel(
                     start=True, stop=True)
 
         def new_y(i):
-            y_bf[i] = sbt("y%d" % i, [P, F * PACK], BF16, tag="y%d" % (i % 3))
+            y_bf[i] = sbt("y%d" % i, [P, F * PACK], BF16)
             y_q[i] = sbt("yq%d" % i, [P, F], U32)
             y_s[i] = sbt("ys%d" % i, [P, F], U8)
 
-        def fil_out(i, c):
-            on_vector = (i, c) in VEC_F
+        def fil_out(i, c, on_vector):
+            give_bank("M%d%d" % (i, c))
             if c == 0:
                 new_y(i)
             dst = y_bf[i][:].rearrange("p (a m t) -> p a m t", a=PACK, t=PACK)[:, :, 32 * c:32 * (c + 1), :]
@@ -132,6 +145,7 @@ def tile_tensorproductrolefillerwrite_x2_kernel(
                 nc.scalar.copy(out=dst, in_=src)
 
         def tanh_out(i, c):
+            give_bank("M%d%d" % (i, c))
             if c == 0:
                 th[i] = sbt("th%d" % i, [P, R, PACK], F32, tag="th%d" % ((i // 2) % 2))
             nc.scalar.activation(out=th[i][:, CH * c:CH * (c + 1), :], in_=mm[i, c][:].rearrange("p t n -> p n t"), func=ACT.Tanh)
@@ -162,11 +176,12 @@ def tile_tensorproductrolefillerwrite_x2_kernel(
                 start=(half == 0), stop=(half == 1))
 
         def mm2_rows(b, a):
-            mm["o", b, a] = bank("mm", [P, R])
+            mm["o", b, a] = take_bank("A%d" % a, [P, R])
             for half in range(2):
                 mm2_pass(mm["o", b, a][:], b, a, half, slice(0, R))
 
         def finish_rows(b, a):
+            give_bank("A%d" % a)
             if a == 0:
                 res[b] = sbt("res%d" % b, [P, PACK, R], F32)
             nc.vector.scalar_tensor_tensor(out=res[b][:, a, :], in0=mm["o", b, a][:], scalar=1.0 / 32.0, in1=dm[b][:, a, :], op0=ALU.mult, op1=ALU.add)
@@ -174,12 +189,13 @@ def tile_tensorproductrolefillerwrite_x2_kernel(
                 nc.sync.dma_start(out=out_0[b].rearrange("(p a) r -> p a r", a=PACK), in_=res[b][:])
 
         def mm2_cols(b, c):
-            mm["o", b, c] = bank("mm", [P, PACK, CH])
+            mm["o", b, c] = take_bank("B%d" % c, [P, PACK, CH])
             for a in range(PACK):
                 for half in range(2):
                     mm2_pass(mm["o", b, c][:, a, :], b, a, half, slice(CH * c, CH * (c + 1)))
 
         def finish_cols(b, c):
+            give_bank("B%d" % c)
             res[b, c] = sbt("res%d_%d" % (b, c), [P, PACK, CH], F32)
             nc.vector.scalar_tensor_tensor(out=res[b, c][:], in0=mm["o", b, c][:], scalar=1.0 / 32.0, in1=dm[b][:, :, CH * c:CH * (c + 1)],
                                            op0=ALU.mult, op1=ALU.add)
@@ -206,32 +222,46 @@ def tile_tensorproductrolefillerwrite_x2_kernel(
                 eng = nc.scalar if q % 2 else nc.sync
                 eng.dma_start(out=out_2[0].bitcast(I32)[4 * q:4 * q + 4, :], in_=o_s[:].bitcast(I32)[32 * q:32 * q + 4, :])
 
-        load_x(0, 0)
+        def spread_decay():
+            mm["d"] = take_bank("D", [P, 2, P])
+            for u in range(2):
+                nc.tensor.transpose(mm["d"][:, u, :], d_col[:].bitcast(F32)[:, u:u + 1].to_broadcast([P, P]), ident[:])
+
+        def copy_decay(on_vector):
+            give_bank("D")
+            dst = d_row[:].bitcast(F32).rearrange("p (m u) -> p m u", u=2)
+            src = mm["d"][:].rearrange("p u m -> p m u")
+            if on_vector:
+                nc.vector.tensor_copy(out=dst, in_=src)
+            else:
+                nc.scalar.copy(out=dst, in_=src)
+
         nc.scalar.dma_start(out=d_col[:], in_=decay.rearrange("(p j) -> p j", j=PACK))
-        make_identity(nc, ident[:])
-        for o in range(2):
-            nc.vector.memset(w_scale[o][:].bitcast(I32), 0)
-        nc.vector.memset(warm[:], 0.0)
-        if WARM:
-            z_bf = sbt("z_bf", [P, KP], BF16)
-            z_q = sbt("z_q", [P, P], U32)
-            z_s = sbt("z_s", [P, P], U8)
-            nc.gpsimd.memset(z_bf[:].bitcast(I32), 0)
-            nc.vector.quantize_mx(out=z_q[:].bitcast(FP8X4), scales=z_s[:], in_=z_bf[:])
-            z_ps = bank("mm", [P, PACK, P])
-            for n in range(WARM):
-                nc.tensor.matmul_mx(out=z_ps[:, n % PACK, :], lhsT=z_q[:].bitcast(FP8X4), lhsT_scale=z_s[:], rhs=z_q[:].bitcast(FP8X4), rhs_scale=z_s[:], start=True, stop=True)
-        load_ws(0)
-        nc.scalar.activation(out=warm[:], in_=warm[:], func=ACT.Tanh)
-        load_x(0, 1)
-        load_x(1, 0)
-        load_w(0)
-        load_x(1, 1)
+        load_x(0, 0)
         load_m(0, 0)
+        load_x(0, 1)
+        make_identity(nc, ident[:])
+        z_bf = sbt("z_bf", [P, KP], BF16)
+        z_q = sbt("z_q", [P, P], U32)
+        z_s = sbt("z_s", [P, P], U8)
+        nc.vector.memset(w_scale[0][:].bitcast(I32), 0)
+        nc.vector.memset(z_bf[:].bitcast(I32), 0)
+        nc.vector.memset(warm[:], 0.0)
+        nc.vector.memset(w_scale[1][:].bitcast(I32), 0)
+        nc.vector.quantize_mx(out=z_q[:].bitcast(FP8X4), scales=z_s[:], in_=z_bf[:])
+        z_ps = take_bank("Z", [P, PACK, P])
+        for n in range(WARM):
+            nc.tensor.matmul_mx(out=z_ps[:, n % PACK, :], lhsT=z_q[:].bitcast(FP8X4), lhsT_scale=z_s[:], rhs=z_q[:].bitcast(FP8X4), rhs_scale=z_s[:], start=True, stop=True)
+        give_bank("Z")
+        load_ws(0, (nc.scalar, nc.scalar, nc.gpsimd, nc.gpsimd))
+        nc.scalar.activation(out=warm[:], in_=warm[:], func=ACT.Tanh)
+        load_w(0)
+        load_x(1, 0)
+        load_x(1, 1)
+        load_ws(1, (nc.sync, nc.sync, nc.gpsimd, nc.gpsimd))
+        nc.gpsimd.dma_start(out=g_sb[:], in_=g.rearrange("b (h p t) -> p (b h) t", h=2, t=PACK))
         load_m(0, 1)
         load_w(1)
-        load_ws(1)
-        nc.sync.dma_start(out=g_sb[:], in_=g.rearrange("b (h p t) -> p (b h) t", h=2, t=PACK))
         load_x(2, 0)
         load_x(2, 1)
         load_m(1, 0)
@@ -240,75 +270,55 @@ def tile_tensorproductrolefillerwrite_x2_kernel(
             load_x(i, 0)
             load_x(i, 1)
 
-        transp(0, 0)
-        transp(0, 1)
-        d_ps = bank("mm", [P, 2, P])
-        for u in range(2):
-            nc.tensor.transpose(d_ps[:, u, :], d_col[:].bitcast(F32)[:, u:u + 1].to_broadcast([P, P]), ident[:])
-        transp(1, 0)
-        transp(1, 1)
-        xcopy(0, 0)
-        xcopy(0, 1)
-        xquant(0, 0, 1)
-        nc.vector.tensor_copy(out=d_row[:].bitcast(F32).rearrange("p (m u) -> p m u", u=2), in_=d_ps[:].rearrange("p u m -> p m u"))
-        xquant(0, 1, 2)
-        decay_mul(0, 0)
-        for c in range(NCH):
-            mm1(0, c)
-
-        for i in range(NG):
-            role = group(i)[0]
-            last = i == NG - 1
-            if not last:
-                xcopy(i + 1, 0)
-                xcopy(i + 1, 1)
-            if i > 0 and not role:
-                gmul(i - 1, 2, 4)
-            if not last:
-                xquant(i + 1)
-            if i > 0:
-                yquant(i - 1, 0, NCH)
-            if i + 2 < NG:
-                transp(i + 2, 0)
-                transp(i + 2, 1)
-            if i == 0:
-                decay_mul(0, 1)
-                decay_mul(1, 0)
-            if i == 2:
-                decay_mul(1, 1)
-            if i in (4, 6):
-                for a in (i - 4, i - 3):
-                    mm2_rows(0, a)
-                for a in (i - 4, i - 3):
-                    finish_rows(0, a)
-            for c in range(NCH):
-                if role:
-                    tanh_out(i, c)
-                    if not last and c == 1:
-                        gmul(i, 0, 2)
+        for step in ORDER.split():
+            vec = step[-1] == "v"
+            name = step[:-1] if vec else step
+            kind = name[0]
+            n = [int(ch) for ch in name[1:]] if name != "DC" else []
+            if name == "D":
+                spread_decay()
+            elif name == "DC":
+                copy_decay(vec)
+            elif kind == "T":
+                transp(*n)
+            elif kind == "X":
+                xcopy(n[0], n[1], vec)
+            elif kind == "Q":
+                if len(n) == 2:
+                    xquant(n[0], n[1], n[1] + 1)
                 else:
-                    fil_out(i, c)
-                if not last:
-                    mm1(i + 1, c)
-
-        i = NG - 1
-        round_out((0, 0), res[0][:])
-        gmul(i, 0, 1)
-        for s in range(NCH + 2):
-            if s + 1 < NCH:
-                gmul(i, s + 1, s + 2)
-            if s < NCH:
-                yquant(i, s, s + 1)
-                mm2_cols(1, s)
-            if s == NCH - 1:
-                oquant((0, 0), 0, R)
-                store_words(0, R)
-            if 0 <= s - 1 < NCH:
-                finish_cols(1, s - 1)
-            if 0 <= s - 2 < NCH - 1:
-                oquant((1, s - 2), R + CH * (s - 2), R + CH * (s - 1))
-            if 0 <= s - 1 < NCH:
-                round_out((1, s - 1), res[1, s - 1][:], on_vector=(s == NCH))
-        oquant((1, NCH - 1), R + CH * (NCH - 1), 2 * R)
-        store_words(R, 2 * R)
+                    xquant(n[0])
+            elif kind == "M":
+                mm1(*n)
+            elif kind == "F":
+                fil_out(n[0], n[1], vec)
+            elif kind == "H":
+                tanh_out(*n)
+            elif kind == "G":
+                gmul(n[0], n[1], n[1] + (1 if n[0] == NG - 1 else 2))
+            elif kind == "Y":
+                if len(n) == 2:
+                    yquant(n[0], n[1], n[1] + 1)
+                else:
+                    yquant(n[0], 0, NCH)
+            elif kind == "U":
+                decay_mul(*n)
+            elif kind == "A":
+                mm2_rows(0, n[0])
+            elif kind == "S":
+                finish_rows(0, n[0])
+            elif kind == "B":
+                mm2_cols(1, n[0])
+            elif kind == "Z":
+                finish_cols(1, n[0])
+            elif kind == "R":
+                round_out(tuple(n), res[0][:, :, 256 * n[1]:256 * (n[1] + 1)] if n[0] == 0 else res[1, n[1]][:], vec)
+            else:
+                width = 256 if n[0] == 0 else CH
+                oquant(tuple(n), R * n[0] + width * n[1], R * n[0] + width * (n[1] + 1))
+                if n == [0, 1]:
+                    store_words(0, R)
+                if n == [1, 2]:
+                    store_words(R, R + 3 * CH)
+        store_words(R + 3 * CH, 2 * R)
         store_scales()

@@ -23,17 +23,17 @@ CH = 128
 NCH = 4
 NG = 8
 BANKS = 8
-WARM = 10
+WARM = 13
 ORDER = """
-D DC U00 T00 X00 Q00 T01 T10 X01 Q01 T11 X10 M00 X11 U01 F00 M01 M02
-Q1 U10 U11 M03 F01 M10 T20 T21 F02 F03 H10 X20 M11 M12 H11 T30 T31 X21v
-Y0 H12 Q2 X30 X31 G10 M13 M20 H13 F20 T40 T41 Q3 X40 M21 M22 F21 G12
-M23 M30 X41v T50 F22 F23 M31 Y1 H30 H31 M32 M33 T51 Q4 M40 M41 X50v H32
-H33 F40 Y2 T60 T61 G30 G32 M42 M43 X51 X60 X61 F41v T70 F42 F43 Y3 T71
-X70 A0 Q5 Q6 M50 A1 X71 M51 M52 M53 Y4 S0 S1 H50 Q7 M60 A2 H51
-H52 G50 H53 G52 A3 S2 F60 M61 F61 M62 M63 Y5 F62 F63 M70 M71 M72 H70
-S3 G70 Y6 Y70 M73 H71 H72 G71 G72 Y71 R00 B0 B1 Z0 H73 Y72 B2 R10
-G73 R01 Z1 Y73 Z2 O00 O01 R11 B3 Z3 R12v R13 O10 O11 O12 O13
+T00 T01 D T10 T11 X00v X01 Q00 DC Q01 M00 U00 U01 X10 X11 M01 Q1 M02
+U10 M03 U11 T20 T21 M10 F00 F01 F02 F03 Y0 M11 T30 X20 X21 T31 Q2 M12
+H10 M13 M20 M21 H11 M22 X30v X31 G10 Q3 H12 H13 M23 T40 T41 M30 F20 F21v
+M31 T50 G12 F22 X40v F23 X41 H30 T51 H31 Y1 Q4 M32 T60 Y2 X50 M33 X51
+M40 H32 H33 M41 F40 G30 T61 Q5 X60 F41 G32 X61 M42 M43 F42v F43 T70 Y3
+Q6 Y4 M50 M51 H50 H51 A0 M52 M53 S0 H52 H53 M60 T71 X70 X71 F60 M61
+G50 G52 A1 M62 S1 Q7 M63 F61 A2 M70 F62 M71 F63 H70 Y5 A3 M72 S2
+Y6 M73 G70 S3 Y70 H71 H72 B0 R00 H73 G71 G72 Y71 B1 Z0 Y72 G73 Z1
+B2 Y73 B3 R10 Z2 R01 O00 R11 O01 Z3 O10 O11 R12 R13v O12 O13
 """
 
 
@@ -238,17 +238,17 @@ def tile_tensorproductrolefillerwrite_x2_kernel(
 
         nc.scalar.dma_start(out=d_col[:], in_=decay.rearrange("(p j) -> p j", j=PACK))
         load_x(0, 0)
-        load_m(0, 0)
         load_x(0, 1)
+        load_x(1, 0)
         make_identity(nc, ident[:])
         z_bf = sbt("z_bf", [P, KP], BF16)
         z_q = sbt("z_q", [P, P], U32)
         z_s = sbt("z_s", [P, P], U8)
-        nc.vector.memset(w_scale[0][:].bitcast(I32), 0)
         nc.vector.memset(z_bf[:].bitcast(I32), 0)
+        nc.vector.memset(w_scale[0][:].bitcast(I32), 0)
+        nc.vector.quantize_mx(out=z_q[:].bitcast(FP8X4), scales=z_s[:], in_=z_bf[:])
         nc.vector.memset(warm[:], 0.0)
         nc.vector.memset(w_scale[1][:].bitcast(I32), 0)
-        nc.vector.quantize_mx(out=z_q[:].bitcast(FP8X4), scales=z_s[:], in_=z_bf[:])
         z_ps = take_bank("Z", [P, PACK, P])
         for n in range(WARM):
             nc.tensor.matmul_mx(out=z_ps[:, n % PACK, :], lhsT=z_q[:].bitcast(FP8X4), lhsT_scale=z_s[:], rhs=z_q[:].bitcast(FP8X4), rhs_scale=z_s[:], start=True, stop=True)
@@ -256,10 +256,10 @@ def tile_tensorproductrolefillerwrite_x2_kernel(
         load_ws(0, (nc.scalar, nc.scalar, nc.gpsimd, nc.gpsimd))
         nc.scalar.activation(out=warm[:], in_=warm[:], func=ACT.Tanh)
         load_w(0)
-        load_x(1, 0)
+        load_m(0, 0)
+        nc.scalar.dma_start(out=g_sb[:], in_=g.rearrange("b (h p t) -> p (b h) t", h=2, t=PACK))
         load_x(1, 1)
-        load_ws(1, (nc.sync, nc.sync, nc.gpsimd, nc.gpsimd))
-        nc.gpsimd.dma_start(out=g_sb[:], in_=g.rearrange("b (h p t) -> p (b h) t", h=2, t=PACK))
+        load_ws(1, (nc.gpsimd, nc.gpsimd, nc.gpsimd, nc.gpsimd))
         load_m(0, 1)
         load_w(1)
         load_x(2, 0)

@@ -23,7 +23,7 @@ CH = 128
 NCH = 4
 NG = 8
 BANKS = 8
-WARM = 13
+WARM = 10
 ORDER = """
 T00 T01 D T10 T11 X00v X01 Q00 DC Q01 M00 U00 U01 X10 X11 M01 Q1 M02
 U10 M03 U11 T20 T21 M10 F00 F01 F02 F03 Y0 M11 T30 X20 X21 T31 Q2 M12
@@ -76,19 +76,29 @@ def tile_tensorproductrolefillerwrite_x2_kernel(
         o_q = sbt("o_q", [P, B * R], U32)
         o_s = sbt("o_s", [P, B * R], U8)
 
-        def load_x(i, h):
+        def load_x(i, h, pieces=1):
             role, b, half = group(i)
             src = (xr if role else xf)[b, half * KP:(half + 1) * KP, :].rearrange("(p j) d -> p j d", j=PACK)
             x_raw[i, h] = sbt("xraw%d_%d" % (i, h), [P, 2, D], BF16)
-            nc.sync.dma_start(out=x_raw[i, h][:], in_=src[:, 2 * h:2 * h + 2, :])
+            step = 2 // pieces
+            for j in range(0, 2, step):
+                nc.sync.dma_start(out=x_raw[i, h][:, j:j + step, :], in_=src[:, 2 * h + j:2 * h + j + step, :])
+
+        def load_x_whole(i):
+            role, b, half = group(i)
+            src = (xr if role else xf)[b, half * KP:(half + 1) * KP, :].rearrange("(p j) d -> p j d", j=PACK)
+            whole = sbt("xraw%d" % i, [P, PACK, D], BF16)
+            nc.sync.dma_start(out=whole[:], in_=src)
+            for h in range(2):
+                x_raw[i, h] = whole[:, 2 * h:2 * h + 2, :]
 
         def load_w(o):
             nc.sync.dma_start(out=w_words[o][:].bitcast(I32), in_=(wf_words, wr_words)[o][0].bitcast(I32))
 
-        def load_ws(o, queues):
+        def load_ws(o, quadrants, queue):
             src = (wf_scales, wr_scales)[o][0].bitcast(I32)
-            for q in range(4):
-                queues[q].dma_start(out=w_scale[o][:].bitcast(I32)[32 * q:32 * q + 4, :], in_=src[4 * q:4 * q + 4, :])
+            for q in quadrants:
+                queue.dma_start(out=w_scale[o][:].bitcast(I32)[32 * q:32 * q + 4, :], in_=src[4 * q:4 * q + 4, :])
 
         def load_m(b, h):
             m_raw[b, h] = sbt("m%d_%d" % (b, h), [P, 2, R], BF16)
@@ -236,10 +246,12 @@ def tile_tensorproductrolefillerwrite_x2_kernel(
             else:
                 nc.scalar.copy(out=dst, in_=src)
 
-        nc.scalar.dma_start(out=d_col[:], in_=decay.rearrange("(p j) -> p j", j=PACK))
         load_x(0, 0)
+        nc.scalar.dma_start(out=d_col[:], in_=decay.rearrange("(p j) -> p j", j=PACK))
         load_x(0, 1)
         load_x(1, 0)
+        load_x(1, 1)
+        load_w(0)
         make_identity(nc, ident[:])
         z_bf = sbt("z_bf", [P, KP], BF16)
         z_q = sbt("z_q", [P, P], U32)
@@ -253,17 +265,16 @@ def tile_tensorproductrolefillerwrite_x2_kernel(
         for n in range(WARM):
             nc.tensor.matmul_mx(out=z_ps[:, n % PACK, :], lhsT=z_q[:].bitcast(FP8X4), lhsT_scale=z_s[:], rhs=z_q[:].bitcast(FP8X4), rhs_scale=z_s[:], start=True, stop=True)
         give_bank("Z")
-        load_ws(0, (nc.scalar, nc.scalar, nc.gpsimd, nc.gpsimd))
+        load_ws(0, (0, 1), nc.scalar)
+        load_ws(0, (2, 3), nc.gpsimd)
         nc.scalar.activation(out=warm[:], in_=warm[:], func=ACT.Tanh)
-        load_w(0)
         load_m(0, 0)
-        nc.scalar.dma_start(out=g_sb[:], in_=g.rearrange("b (h p t) -> p (b h) t", h=2, t=PACK))
-        load_x(1, 1)
-        load_ws(1, (nc.gpsimd, nc.gpsimd, nc.gpsimd, nc.gpsimd))
         load_m(0, 1)
         load_w(1)
         load_x(2, 0)
         load_x(2, 1)
+        load_ws(1, range(4), nc.sync)
+        nc.sync.dma_start(out=g_sb[:], in_=g.rearrange("b (h p t) -> p (b h) t", h=2, t=PACK))
         load_m(1, 0)
         load_m(1, 1)
         for i in range(3, NG):

@@ -22,19 +22,7 @@ KP = P * PACK
 CH = 128
 NCH = 4
 NG = 8
-BANKS = 8
-WARM = 10
-ORDER = """
-T00 T01 D T10 T11 X00v X01 Q00 DC Q01 M00 U00 U01 X10 X11 M01 Q1 M02
-U10 M03 U11 T20 T21 M10 F00 F01 F02 F03 Y0 M11 T30 X20 X21 T31 Q2 M12
-H10 M13 M20 M21 H11 M22 X30v X31 G10 Q3 H12 H13 M23 T40 T41 M30 F20 F21v
-M31 T50 G12 F22 X40v F23 X41 H30 T51 H31 Y1 Q4 M32 T60 Y2 X50 M33 X51
-M40 H32 H33 M41 F40 G30 T61 Q5 X60 F41 G32 X61 M42 M43 F42v F43 T70 Y3
-Q6 Y4 M50 M51 H50 H51 A0 M52 M53 S0 H52 H53 M60 T71 X70 X71 F60 M61
-G50 G52 A1 M62 S1 Q7 M63 F61 A2 M70 F62 M71 F63 H70 Y5 A3 M72 S2
-Y6 M73 G70 S3 Y70 H71 H72 B0 R00 H73 G71 G72 Y71 B1 Z0 Y72 G73 Z1
-B2 Y73 B3 R10 Z2 R01 O00 R11 O01 Z3 O10 O11 R12 R13v O12 O13
-"""
+BANKS = 7
 
 
 def tile_tensorproductrolefillerwrite_x2_kernel(
@@ -49,48 +37,40 @@ def tile_tensorproductrolefillerwrite_x2_kernel(
         def sbt(name, shape, dtype, tag=None):
             return sb.tile(shape, dtype, name=name, tag=tag or name, align_bytes=64)
 
-        free_banks = list(range(BANKS))
-        held = {}
+        taken = []
 
-        def take_bank(key, shape):
-            held[key] = free_banks[0]
-            free_banks.remove(held[key])
-            return ps.tile(shape, F32, name="ps_%s" % key, tag="bank%d" % held[key])
-
-        def give_bank(key):
-            free_banks.append(held[key])
+        def next_bank(name, shape):
+            taken.append(name)
+            return ps.tile(shape, F32, name=name, tag="bank%d" % (len(taken) % BANKS))
 
         def group(i):
             return i % 2, i // 4, (i // 2) % 2
 
-        x_raw, x_t, x_q, x_s, y_bf, y_q, y_s, tp, mm, th = {}, {}, {}, {}, {}, {}, {}, {}, {}, {}
+        x_raw, x_t, x_q, x_s, y_bf, y_q, y_s, th = {}, {}, {}, {}, {}, {}, {}, {}
         m_raw, dm, res, res_bf = {}, {}, {}, {}
 
         ident = sbt("ident", [P, P], F32)
         w_words = [sbt("ww%d" % o, [P, 2 * F], U8) for o in range(2)]
         w_scale = [sbt("ws%d" % o, [P, F], U8) for o in range(2)]
-        g_sb = sbt("g_sb", [P, B * 2, PACK], BF16)
+        g_rows = sbt("g_rows", [P, KP], BF16)
         d_col = sbt("d_col", [P, PACK], BF16)
         d_row = sbt("d_row", [P, R], BF16)
         warm = sbt("warm", [P, 1], F32)
         o_q = sbt("o_q", [P, B * R], U32)
         o_s = sbt("o_s", [P, B * R], U8)
+        consts = ps.tile([P, 4, P], F32, name="consts", tag="consts")
 
-        def load_x(i, h, pieces=1):
+        def copy_on(eng, dst, src):
+            if eng is nc.vector:
+                nc.vector.tensor_copy(out=dst, in_=src)
+            else:
+                nc.scalar.copy(out=dst, in_=src)
+
+        def load_x(i, h):
             role, b, half = group(i)
             src = (xr if role else xf)[b, half * KP:(half + 1) * KP, :].rearrange("(p j) d -> p j d", j=PACK)
             x_raw[i, h] = sbt("xraw%d_%d" % (i, h), [P, 2, D], BF16)
-            step = 2 // pieces
-            for j in range(0, 2, step):
-                nc.sync.dma_start(out=x_raw[i, h][:, j:j + step, :], in_=src[:, 2 * h + j:2 * h + j + step, :])
-
-        def load_x_whole(i):
-            role, b, half = group(i)
-            src = (xr if role else xf)[b, half * KP:(half + 1) * KP, :].rearrange("(p j) d -> p j d", j=PACK)
-            whole = sbt("xraw%d" % i, [P, PACK, D], BF16)
-            nc.sync.dma_start(out=whole[:], in_=src)
-            for h in range(2):
-                x_raw[i, h] = whole[:, 2 * h:2 * h + 2, :]
+            nc.sync.dma_start(out=x_raw[i, h][:], in_=src[:, 2 * h:2 * h + 2, :])
 
         def load_w(o):
             nc.sync.dma_start(out=w_words[o][:].bitcast(I32), in_=(wf_words, wr_words)[o][0].bitcast(I32))
@@ -100,127 +80,110 @@ def tile_tensorproductrolefillerwrite_x2_kernel(
             for q in quadrants:
                 queue.dma_start(out=w_scale[o][:].bitcast(I32)[32 * q:32 * q + 4, :], in_=src[4 * q:4 * q + 4, :])
 
-        def load_m(b, h):
-            m_raw[b, h] = sbt("m%d_%d" % (b, h), [P, 2, R], BF16)
-            nc.sync.dma_start(out=m_raw[b, h][:], in_=m0[b].rearrange("(p j) r -> p j r", j=PACK)[:, 2 * h:2 * h + 2, :])
+        def load_m(b, j0, j1):
+            m_raw[b, j0] = sbt("m%d_%d" % (b, j0), [P, j1 - j0, R], BF16)
+            nc.sync.dma_start(out=m_raw[b, j0][:], in_=m0[b].rearrange("(p j) r -> p j r", j=PACK)[:, j0:j1, :])
 
-        def transp(i, h):
-            tp[i, h] = take_bank("T%d%d" % (i, h), [P, 2, 2, P])
+        def turn_x(i, h, eng):
+            bank = next_bank("T%d%d" % (i, h), [P, 2, 2, P])
             words = x_raw[i, h][:].rearrange("p j d -> p (j d)").bitcast(F32)
             for j in range(2):
                 for u in range(2):
-                    nc.tensor.transpose(tp[i, h][:, j, u, :], words[:, 256 * j + u:256 * (j + 1):2], ident[:])
-
-        def xcopy(i, h, on_vector):
-            give_bank("T%d%d" % (i, h))
+                    nc.tensor.transpose(bank[:, j, u, :], words[:, 256 * j + u:256 * (j + 1):2], ident[:])
             if h == 0:
                 x_t[i] = sbt("xt%d" % i, [P, PACK * P * PACK], BF16)
             dst = x_t[i][:].bitcast(F32)[:, 512 * h:512 * (h + 1)].rearrange("p (j m u) -> p j m u", j=2, u=2)
-            src = tp[i, h][:].rearrange("p j u m -> p j m u")
-            if on_vector:
-                nc.vector.tensor_copy(out=dst, in_=src)
-            else:
-                nc.scalar.copy(out=dst, in_=src)
+            copy_on(eng, dst, bank[:].rearrange("p j u m -> p j m u"))
 
-        def xquant(i, h0=0, h1=2):
+        def quant_x(i, h0=0, h1=2):
             if h0 == 0:
                 x_q[i] = sbt("xq%d" % i, [P, KP], U32)
                 x_s[i] = sbt("xs%d" % i, [P, KP], U8)
             nc.vector.quantize_mx(out=x_q[i][:, 256 * h0:256 * h1].bitcast(FP8X4), scales=x_s[i][:, 256 * h0:256 * h1], in_=x_t[i][:, 1024 * h0:1024 * h1])
 
-        def mm1(i, c):
+        def stage1(i, c, eng):
             o = group(i)[0]
-            mm[i, c] = take_bank("M%d%d" % (i, c), [P, PACK, CH])
+            bank = next_bank("M%d%d" % (i, c), [P, PACK, CH])
             for j in range(PACK):
                 nc.tensor.matmul_mx(
-                    out=mm[i, c][:, j, :],
+                    out=bank[:, j, :],
                     lhsT=x_q[i][:, P * j:P * (j + 1)].bitcast(FP8X4), lhsT_scale=x_s[i][:, P * j:P * (j + 1)],
                     rhs=w_words[o][:, 2 * CH * c:2 * CH * (c + 1)].bitcast(FP4X4), rhs_scale=w_scale[o][:, CH * c:CH * (c + 1)],
                     start=True, stop=True)
-
-        def new_y(i):
-            y_bf[i] = sbt("y%d" % i, [P, F * PACK], BF16)
-            y_q[i] = sbt("yq%d" % i, [P, F], U32)
-            y_s[i] = sbt("ys%d" % i, [P, F], U8)
-
-        def fil_out(i, c, on_vector):
-            give_bank("M%d%d" % (i, c))
             if c == 0:
-                new_y(i)
-            dst = y_bf[i][:].rearrange("p (a m t) -> p a m t", a=PACK, t=PACK)[:, :, 32 * c:32 * (c + 1), :]
-            src = mm[i, c][:].rearrange("p t (m a) -> p a m t", a=PACK)
-            if on_vector:
-                nc.vector.tensor_copy(out=dst, in_=src)
+                y_bf[i] = sbt("y%d" % i, [P, F * PACK], BF16)
+                y_q[i] = sbt("yq%d" % i, [P, F], U32)
+                y_s[i] = sbt("ys%d" % i, [P, F], U8)
+            if o == 0:
+                dst = y_bf[i][:].rearrange("p (a m t) -> p a m t", a=PACK, t=PACK)[:, :, 32 * c:32 * (c + 1), :]
+                copy_on(eng, dst, bank[:].rearrange("p t (m a) -> p a m t", a=PACK))
             else:
-                nc.scalar.copy(out=dst, in_=src)
+                if c == 0:
+                    th[i] = sbt("th%d" % i, [P, R, PACK], F32)
+                nc.scalar.activation(out=th[i][:, CH * c:CH * (c + 1), :], in_=bank[:].rearrange("p t n -> p n t"), func=ACT.Tanh)
 
-        def tanh_out(i, c):
-            give_bank("M%d%d" % (i, c))
-            if c == 0:
-                th[i] = sbt("th%d" % i, [P, R, PACK], F32, tag="th%d" % ((i // 2) % 2))
-            nc.scalar.activation(out=th[i][:, CH * c:CH * (c + 1), :], in_=mm[i, c][:].rearrange("p t n -> p n t"), func=ACT.Tanh)
+        def gate(i, c0, c1):
+            dst = y_bf[i][:, CH * PACK * c0:CH * PACK * c1].rearrange("p (n u e) -> p n u e", u=2, e=2)
+            src = th[i][:, CH * c0:CH * c1, :].rearrange("p n (u e) -> p n u e", u=2)
+            strength = consts[:, 2:4, :].bitcast(BF16)[:, :, i - 1:i + 1].unsqueeze(1).to_broadcast([P, CH * (c1 - c0), 2, 2])
+            nc.vector.tensor_tensor(out=dst, in0=src, in1=strength, op=ALU.mult)
 
-        def gmul(i, c0, c1):
-            if c0 == 0:
-                new_y(i)
-            dst = y_bf[i][:, CH * PACK * c0:CH * PACK * c1].rearrange("p (n t) -> p n t", t=PACK)
-            gate = g_sb[:, i // 2, :].unsqueeze(1).to_broadcast([P, CH * (c1 - c0), PACK])
-            nc.vector.tensor_tensor(out=dst, in0=th[i][:, CH * c0:CH * c1, :], in1=gate, op=ALU.mult)
-
-        def yquant(i, c0, c1):
+        def quant_y(i, c0=0, c1=NCH):
             nc.vector.quantize_mx(out=y_q[i][:, CH * c0:CH * c1].bitcast(FP8X4), scales=y_s[i][:, CH * c0:CH * c1],
                                   in_=y_bf[i][:, CH * PACK * c0:CH * PACK * c1])
 
-        def decay_mul(b, h):
-            if h == 0:
-                dm[b] = sbt("dm%d" % b, [P, PACK, R], F32)
-            row = d_row[:].unsqueeze(1).to_broadcast([P, 2, R])
-            nc.vector.tensor_tensor(out=dm[b][:, 2 * h:2 * h + 2, :], in0=m_raw[b, h][:], in1=row, op=ALU.mult)
+        def decay_mul(b, h, eng, tag=None):
+            if b == 0:
+                dm[b, h] = sbt("dm%d_%d" % (b, h), [P, 2, R], F32, tag=tag)
+                eng.tensor_tensor(out=dm[b, h][:], in0=m_raw[b, 2 * h][:], in1=d_row[:].unsqueeze(1).to_broadcast([P, 2, R]), op=ALU.mult)
+            else:
+                cols = slice(256 * h, 256 * (h + 1))
+                dm[b, h] = sbt("dm%d_%d" % (b, h), [P, PACK, 256], F32, tag=tag)
+                eng.tensor_tensor(out=dm[b, h][:], in0=m_raw[b, 0][:, :, cols], in1=d_row[:, cols].unsqueeze(1).to_broadcast([P, PACK, 256]), op=ALU.mult)
 
-        def mm2_pass(out, b, a, half, cols):
+        def stage2_pass(out, b, a, half, cols, start, stop):
             fi = 4 * b + 2 * half
             nc.tensor.matmul_mx(
                 out=out,
                 lhsT=y_q[fi][:, P * a:P * (a + 1)].bitcast(FP8X4), lhsT_scale=y_s[fi][:, P * a:P * (a + 1)],
                 rhs=y_q[fi + 1][:, cols].bitcast(FP8X4), rhs_scale=y_s[fi + 1][:, cols],
-                start=(half == 0), stop=(half == 1))
+                start=start, stop=stop)
 
-        def mm2_rows(b, a):
-            mm["o", b, a] = take_bank("A%d" % a, [P, R])
+        acc = {}
+
+        def bind_rows(a):
+            acc[0, a] = next_bank("A%d" % a, [P, R])
             for half in range(2):
-                mm2_pass(mm["o", b, a][:], b, a, half, slice(0, R))
+                stage2_pass(acc[0, a][:], 0, a, half, slice(0, R), half == 0, half == 1)
 
-        def finish_rows(b, a):
-            give_bank("A%d" % a)
+        def finish_rows(a):
             if a == 0:
-                res[b] = sbt("res%d" % b, [P, PACK, R], F32)
-            nc.vector.scalar_tensor_tensor(out=res[b][:, a, :], in0=mm["o", b, a][:], scalar=1.0 / 32.0, in1=dm[b][:, a, :], op0=ALU.mult, op1=ALU.add)
+                res[0] = sbt("res0", [P, PACK, R], F32)
+            nc.vector.scalar_tensor_tensor(out=res[0][:, a, :], in0=acc[0, a][:], scalar=1.0 / 32.0, in1=dm[0, a // 2][:, a % 2, :], op0=ALU.mult, op1=ALU.add)
             if a == PACK - 1:
-                nc.sync.dma_start(out=out_0[b].rearrange("(p a) r -> p a r", a=PACK), in_=res[b][:])
+                nc.sync.dma_start(out=out_0[0].rearrange("(p a) r -> p a r", a=PACK), in_=res[0][:])
 
-        def mm2_cols(b, c):
-            mm["o", b, c] = take_bank("B%d" % c, [P, PACK, CH])
+        def bind_cols(c, half):
+            if half == 0:
+                acc[1, c] = next_bank("B%d" % c, [P, PACK, CH])
             for a in range(PACK):
-                for half in range(2):
-                    mm2_pass(mm["o", b, c][:, a, :], b, a, half, slice(CH * c, CH * (c + 1)))
+                stage2_pass(acc[1, c][:, a, :], 1, a, half, slice(CH * c, CH * (c + 1)), half == 0 and a == 0, half == 1 and a == PACK - 1)
 
-        def finish_cols(b, c):
-            give_bank("B%d" % c)
-            res[b, c] = sbt("res%d_%d" % (b, c), [P, PACK, CH], F32)
-            nc.vector.scalar_tensor_tensor(out=res[b, c][:], in0=mm["o", b, c][:], scalar=1.0 / 32.0, in1=dm[b][:, :, CH * c:CH * (c + 1)],
+        def finish_cols(c):
+            res[1, c] = sbt("res1_%d" % c, [P, PACK, CH], F32)
+            nc.vector.scalar_tensor_tensor(out=res[1, c][:], in0=acc[1, c][:], scalar=1.0 / 32.0, in1=dm[1, c // 2][:, :, CH * (c % 2):CH * (c % 2 + 1)],
                                            op0=ALU.mult, op1=ALU.add)
-            nc.sync.dma_start(out=out_0[b].rearrange("(p a) r -> p a r", a=PACK)[:, :, CH * c:CH * (c + 1)], in_=res[b, c][:])
+            nc.sync.dma_start(out=out_0[1].rearrange("(p a) r -> p a r", a=PACK)[:, :, CH * c:CH * (c + 1)], in_=res[1, c][:])
 
-        def round_out(key, src, on_vector=False):
-            res_bf[key] = sbt("rb%d_%d" % key, [P, src.shape[2] * PACK], BF16)
-            dst = res_bf[key][:].rearrange("p (n i a) -> p n a i", a=PACK, i=4)
-            src = src.rearrange("p a (n i) -> p n a i", i=4)
-            if on_vector:
-                nc.vector.tensor_copy(out=dst, in_=src)
+        def round_out(key, src, eng, tag=None):
+            res_bf[key] = sbt("rb%d_%d" % key, [P, src.shape[2] * PACK], BF16, tag=tag)
+            if eng is nc.gpsimd:
+                nc.gpsimd.tensor_scalar(out=res_bf[key][:].rearrange("p (n a) -> p n a", a=PACK), in0=src.rearrange("p a n -> p n a"),
+                                        scalar1=1.0, scalar2=0.0, op0=ALU.mult, op1=ALU.add)
             else:
-                nc.scalar.copy(out=dst, in_=src)
+                copy_on(eng, res_bf[key][:].rearrange("p (n i a) -> p n a i", a=PACK, i=4), src.rearrange("p a (n i) -> p n a i", i=4))
 
-        def oquant(key, c0, c1):
+        def quant_out(key, c0, c1):
             nc.vector.quantize_mx(out=o_q[:, c0:c1].bitcast(FP8X4), scales=o_s[:, c0:c1], in_=res_bf[key][:])
 
         def store_words(c0, c1):
@@ -233,103 +196,123 @@ def tile_tensorproductrolefillerwrite_x2_kernel(
                 eng.dma_start(out=out_2[0].bitcast(I32)[4 * q:4 * q + 4, :], in_=o_s[:].bitcast(I32)[32 * q:32 * q + 4, :])
 
         def spread_decay():
-            mm["d"] = take_bank("D", [P, 2, P])
             for u in range(2):
-                nc.tensor.transpose(mm["d"][:, u, :], d_col[:].bitcast(F32)[:, u:u + 1].to_broadcast([P, P]), ident[:])
+                nc.tensor.transpose(consts[:, u, :], d_col[:].bitcast(F32)[:, u:u + 1].to_broadcast([P, P]), ident[:])
+            nc.vector.tensor_copy(out=d_row[:].bitcast(F32).rearrange("p (m u) -> p m u", u=2), in_=consts[:, 0:2, :].rearrange("p u m -> p m u"))
 
-        def copy_decay(on_vector):
-            give_bank("D")
-            dst = d_row[:].bitcast(F32).rearrange("p (m u) -> p m u", u=2)
-            src = mm["d"][:].rearrange("p u m -> p m u")
-            if on_vector:
-                nc.vector.tensor_copy(out=dst, in_=src)
-            else:
-                nc.scalar.copy(out=dst, in_=src)
+        def turn_g():
+            for u in range(2):
+                nc.tensor.transpose(consts[:, 2 + u, :], g_rows[:].bitcast(F32)[:, u:2 * P:2], ident[:])
 
-        load_x(0, 0)
-        nc.scalar.dma_start(out=d_col[:], in_=decay.rearrange("(p j) -> p j", j=PACK))
-        load_x(0, 1)
+        V, S, G = nc.vector, nc.scalar, nc.gpsimd
         load_x(1, 0)
+        nc.scalar.dma_start(out=d_col[:], in_=decay.rearrange("(p j) -> p j", j=PACK))
         load_x(1, 1)
-        load_w(0)
-        make_identity(nc, ident[:])
-        z_bf = sbt("z_bf", [P, KP], BF16)
-        z_q = sbt("z_q", [P, P], U32)
-        z_s = sbt("z_s", [P, P], U8)
-        nc.vector.memset(z_bf[:].bitcast(I32), 0)
-        nc.vector.memset(w_scale[0][:].bitcast(I32), 0)
-        nc.vector.quantize_mx(out=z_q[:].bitcast(FP8X4), scales=z_s[:], in_=z_bf[:])
-        nc.vector.memset(warm[:], 0.0)
-        nc.vector.memset(w_scale[1][:].bitcast(I32), 0)
-        z_ps = take_bank("Z", [P, PACK, P])
-        for n in range(WARM):
-            nc.tensor.matmul_mx(out=z_ps[:, n % PACK, :], lhsT=z_q[:].bitcast(FP8X4), lhsT_scale=z_s[:], rhs=z_q[:].bitcast(FP8X4), rhs_scale=z_s[:], start=True, stop=True)
-        give_bank("Z")
-        load_ws(0, (0, 1), nc.scalar)
-        load_ws(0, (2, 3), nc.gpsimd)
-        nc.scalar.activation(out=warm[:], in_=warm[:], func=ACT.Tanh)
-        load_m(0, 0)
-        load_m(0, 1)
+        load_x(0, 0)
+        load_x(0, 1)
         load_w(1)
+        make_identity(nc, ident[:])
+        nc.vector.memset(w_scale[1][:].bitcast(I32), 0)
+        nc.vector.memset(warm[:], 0.0)
+        nc.vector.memset(g_rows[:].bitcast(I32), 0)
+        nc.vector.memset(w_scale[0][:].bitcast(I32), 0)
+        load_ws(1, (0, 1), nc.scalar)
+        load_ws(1, (2, 3), nc.gpsimd)
+        nc.scalar.activation(out=warm[:], in_=warm[:], func=ACT.Tanh)
+        load_x(3, 0)
+        load_x(3, 1)
+        load_w(0)
+        nc.sync.dma_start(out=g_rows[0:4, :], in_=g.rearrange("b (h k) -> (b h) k", h=2))
+        load_m(0, 0, 2)
+        load_ws(0, range(4), nc.sync)
         load_x(2, 0)
         load_x(2, 1)
-        load_ws(1, range(4), nc.sync)
-        nc.sync.dma_start(out=g_sb[:], in_=g.rearrange("b (h p t) -> p (b h) t", h=2, t=PACK))
-        load_m(1, 0)
-        load_m(1, 1)
-        for i in range(3, NG):
+        load_m(0, 2, 4)
+        load_x(5, 0)
+        load_x(5, 1)
+        load_m(1, 0, 4)
+        for i in (4, 7, 6):
             load_x(i, 0)
             load_x(i, 1)
 
-        for step in ORDER.split():
-            vec = step[-1] == "v"
-            name = step[:-1] if vec else step
-            kind = name[0]
-            n = [int(ch) for ch in name[1:]] if name != "DC" else []
-            if name == "D":
-                spread_decay()
-            elif name == "DC":
-                copy_decay(vec)
-            elif kind == "T":
-                transp(*n)
-            elif kind == "X":
-                xcopy(n[0], n[1], vec)
-            elif kind == "Q":
-                if len(n) == 2:
-                    xquant(n[0], n[1], n[1] + 1)
-                else:
-                    xquant(n[0])
-            elif kind == "M":
-                mm1(*n)
-            elif kind == "F":
-                fil_out(n[0], n[1], vec)
-            elif kind == "H":
-                tanh_out(*n)
-            elif kind == "G":
-                gmul(n[0], n[1], n[1] + (1 if n[0] == NG - 1 else 2))
-            elif kind == "Y":
-                if len(n) == 2:
-                    yquant(n[0], n[1], n[1] + 1)
-                else:
-                    yquant(n[0], 0, NCH)
-            elif kind == "U":
-                decay_mul(*n)
-            elif kind == "A":
-                mm2_rows(0, n[0])
-            elif kind == "S":
-                finish_rows(0, n[0])
-            elif kind == "B":
-                mm2_cols(1, n[0])
-            elif kind == "Z":
-                finish_cols(1, n[0])
-            elif kind == "R":
-                round_out(tuple(n), res[0][:, :, 256 * n[1]:256 * (n[1] + 1)] if n[0] == 0 else res[1, n[1]][:], vec)
+        last = NG - 1
+        turn_x(1, 0, V)
+        turn_x(1, 1, S)
+        quant_x(1, 0, 1)
+        quant_x(1, 1, 2)
+        turn_x(0, 0, V)
+        turn_x(0, 1, S)
+        spread_decay()
+        quant_x(0)
+        for k in range(3):
+            role, fil = 2 * k + 1, 2 * k
+            turn_x(role + 2, 0, V)
+            turn_x(role + 2, 1, S)
+            if k > 0:
+                quant_y(fil - 2)
+            quant_x(role + 2)
+            if k == 0:
+                decay_mul(0, 0, V)
             else:
-                width = 256 if n[0] == 0 else CH
-                oquant(tuple(n), R * n[0] + width * n[1], R * n[0] + width * (n[1] + 1))
-                if n == [0, 1]:
-                    store_words(0, R)
-                if n == [1, 2]:
-                    store_words(R, R + 3 * CH)
-        store_words(R + 3 * CH, 2 * R)
+                decay_mul(k // 2, k % 2, G, "xt%d" % (role + 2))
+            stage1(role, 0, S)
+            stage1(role, 1, S)
+            if k > 0:
+                gate(role, 0, 2)
+            stage1(role, 2, S)
+            stage1(role, 3, S)
+            if k == 0:
+                turn_g()
+                gate(role, 0, 2)
+            turn_x(fil + 2, 0, S)
+            turn_x(fil + 2, 1, S)
+            gate(role, 2, 4)
+            if k < 2:
+                for c in range(NCH):
+                    stage1(fil, c, V if c == 0 else S)
+            else:
+                bind_rows(0)
+                for c in range(NCH - 1):
+                    stage1(fil, c, S)
+                finish_rows(0)
+                bind_rows(1)
+                stage1(fil, NCH - 1, S)
+            quant_y(role)
+            quant_x(fil + 2)
+        decay_mul(1, 1, G, "xt%d" % (last - 1))
+        finish_rows(1)
+        for c in range(2):
+            stage1(last, c, S)
+            bind_rows(2 + c)
+        for c in range(2):
+            finish_rows(2 + c)
+        for c in range(2):
+            gate(last, c, c + 1)
+        quant_y(last - 3)
+        quant_y(last, 0, 2)
+        for c in range(NCH):
+            stage1(last - 1, c, S)
+        quant_y(last - 1)
+        for c in range(2, NCH):
+            stage1(last, c, S)
+        for c in range(NCH):
+            bind_cols(c, 0)
+        for c in range(2):
+            bind_cols(c, 1)
+            gate(last, 2 + c, 3 + c)
+        for c in range(2):
+            quant_y(last, 2 + c, 3 + c)
+            bind_cols(2 + c, 1)
+            finish_cols(c)
+            round_out((0, c), res[0][:, :, 256 * c:256 * (c + 1)], S)
+        for c in range(2):
+            finish_cols(2 + c)
+            quant_out((0, c), 256 * c, 256 * (c + 1))
+            round_out((1, c), res[1, c][:], S)
+        store_words(0, R)
+        round_out((1, 2), res[1, 2][:], S)
+        round_out((1, 3), res[1, 3][:], V)
+        for c in (0, 1, 3, 2):
+            quant_out((1, c), R + CH * c, R + CH * (c + 1))
+        store_words(R, 2 * R)
         store_scales()

@@ -23,6 +23,7 @@ CH = 128
 NCH = 4
 NG = 8
 BANKS = 7
+YT = {5: "xt6", 7: "y4"}
 
 
 def tile_tensorproductrolefillerwrite_x2_kernel(
@@ -59,6 +60,7 @@ def tile_tensorproductrolefillerwrite_x2_kernel(
         o_q = sbt("o_q", [P, B * R], U32)
         o_s = sbt("o_s", [P, B * R], U8)
         consts = ps.tile([P, 4, P], F32, name="consts", tag="consts")
+        g_sb = sbt("g_sb", [P, B * 2, PACK], BF16)
 
         def copy_on(eng, dst, src):
             if eng is nc.vector:
@@ -84,6 +86,10 @@ def tile_tensorproductrolefillerwrite_x2_kernel(
             m_raw[b, j0] = sbt("m%d_%d" % (b, j0), [P, j1 - j0, R], BF16)
             nc.sync.dma_start(out=m_raw[b, j0][:], in_=m0[b].rearrange("(p j) r -> p j r", j=PACK)[:, j0:j1, :])
 
+        def load_m_cols(h):
+            m_raw[1, h] = sbt("m1_%d" % h, [P, PACK, 256], BF16)
+            nc.sync.dma_start(out=m_raw[1, h][:], in_=m0[1].rearrange("(p j) r -> p j r", j=PACK)[:, :, 256 * h:256 * (h + 1)])
+
         def turn_x(i, h, eng):
             bank = next_bank("T%d%d" % (i, h), [P, 2, 2, P])
             words = x_raw[i, h][:].rearrange("p j d -> p (j d)").bitcast(F32)
@@ -94,6 +100,10 @@ def tile_tensorproductrolefillerwrite_x2_kernel(
                 x_t[i] = sbt("xt%d" % i, [P, PACK * P * PACK], BF16)
             dst = x_t[i][:].bitcast(F32)[:, 512 * h:512 * (h + 1)].rearrange("p (j m u) -> p j m u", j=2, u=2)
             copy_on(eng, dst, bank[:].rearrange("p j u m -> p j m u"))
+
+        def turn_both(i):
+            turn_x(i, 0, S)
+            turn_x(i, 1, S)
 
         def quant_x(i, h0=0, h1=2):
             if h0 == 0:
@@ -111,7 +121,8 @@ def tile_tensorproductrolefillerwrite_x2_kernel(
                     rhs=w_words[o][:, 2 * CH * c:2 * CH * (c + 1)].bitcast(FP4X4), rhs_scale=w_scale[o][:, CH * c:CH * (c + 1)],
                     start=True, stop=True)
             if c == 0:
-                y_bf[i] = sbt("y%d" % i, [P, F * PACK], BF16)
+                if o == 0:
+                    y_bf[i] = sbt("y%d" % i, [P, F * PACK], BF16)
                 y_q[i] = sbt("yq%d" % i, [P, F], U32)
                 y_s[i] = sbt("ys%d" % i, [P, F], U8)
             if o == 0:
@@ -122,11 +133,16 @@ def tile_tensorproductrolefillerwrite_x2_kernel(
                     th[i] = sbt("th%d" % i, [P, R, PACK], F32)
                 nc.scalar.activation(out=th[i][:, CH * c:CH * (c + 1), :], in_=bank[:].rearrange("p t n -> p n t"), func=ACT.Tanh)
 
-        def gate(i, c0, c1):
+        def gate(i, c0, c1, eng=None):
+            if i not in y_bf:
+                y_bf[i] = sbt("y%d" % i, [P, F * PACK], BF16, tag=YT.get(i))
             dst = y_bf[i][:, CH * PACK * c0:CH * PACK * c1].rearrange("p (n u e) -> p n u e", u=2, e=2)
             src = th[i][:, CH * c0:CH * c1, :].rearrange("p n (u e) -> p n u e", u=2)
             strength = consts[:, 2:4, :].bitcast(BF16)[:, :, i - 1:i + 1].unsqueeze(1).to_broadcast([P, CH * (c1 - c0), 2, 2])
-            nc.vector.tensor_tensor(out=dst, in0=src, in1=strength, op=ALU.mult)
+            if eng is nc.gpsimd:
+                nc.gpsimd.tensor_tensor(out=dst.rearrange("p n u e -> p n (u e)"), in0=th[i][:, CH * c0:CH * c1, :], in1=g_sb[:, i // 2, :].unsqueeze(1).to_broadcast([P, CH * (c1 - c0), PACK]), op=ALU.mult)
+            else:
+                nc.vector.tensor_tensor(out=dst, in0=src, in1=strength, op=ALU.mult)
 
         def quant_y(i, c0=0, c1=NCH):
             nc.vector.quantize_mx(out=y_q[i][:, CH * c0:CH * c1].bitcast(FP8X4), scales=y_s[i][:, CH * c0:CH * c1],
@@ -139,7 +155,7 @@ def tile_tensorproductrolefillerwrite_x2_kernel(
             else:
                 cols = slice(256 * h, 256 * (h + 1))
                 dm[b, h] = sbt("dm%d_%d" % (b, h), [P, PACK, 256], F32, tag=tag)
-                eng.tensor_tensor(out=dm[b, h][:], in0=m_raw[b, 0][:, :, cols], in1=d_row[:, cols].unsqueeze(1).to_broadcast([P, PACK, 256]), op=ALU.mult)
+                eng.tensor_tensor(out=dm[b, h][:], in0=m_raw[b, h][:], in1=d_row[:, cols].unsqueeze(1).to_broadcast([P, PACK, 256]), op=ALU.mult)
 
         def stage2_pass(out, b, a, half, cols, start, stop):
             fi = 4 * b + 2 * half
@@ -204,92 +220,117 @@ def tile_tensorproductrolefillerwrite_x2_kernel(
             for u in range(2):
                 nc.tensor.transpose(consts[:, 2 + u, :], g_rows[:].bitcast(F32)[:, u:2 * P:2], ident[:])
 
+        def copy_g():
+            nc.scalar.copy(out=g_sb[:].rearrange("p q t -> p (q t)").bitcast(F32).rearrange("p (q u) -> p q u", u=2), in_=consts[:, 2:4, 0:4].rearrange("p u q -> p q u"))
+
         V, S, G = nc.vector, nc.scalar, nc.gpsimd
         load_x(1, 0)
         nc.scalar.dma_start(out=d_col[:], in_=decay.rearrange("(p j) -> p j", j=PACK))
         load_x(1, 1)
         load_x(0, 0)
         load_x(0, 1)
-        load_w(1)
+        load_m(0, 0, 2)
         make_identity(nc, ident[:])
+        nc.vector.memset(g_rows[:].bitcast(I32), 0)
         nc.vector.memset(w_scale[1][:].bitcast(I32), 0)
         nc.vector.memset(warm[:], 0.0)
-        nc.vector.memset(g_rows[:].bitcast(I32), 0)
         nc.vector.memset(w_scale[0][:].bitcast(I32), 0)
-        load_ws(1, (0, 1), nc.scalar)
-        load_ws(1, (2, 3), nc.gpsimd)
+        nc.scalar.dma_start(out=g_rows[0:4, :], in_=g.rearrange("b (h k) -> (b h) k", h=2))
+        load_ws(1, (0,), nc.scalar)
+        load_ws(1, (1, 2, 3), nc.gpsimd)
         nc.scalar.activation(out=warm[:], in_=warm[:], func=ACT.Tanh)
         load_x(3, 0)
         load_x(3, 1)
+        load_w(1)
+        load_m(0, 2, 4)
         load_w(0)
-        nc.sync.dma_start(out=g_rows[0:4, :], in_=g.rearrange("b (h k) -> (b h) k", h=2))
-        load_m(0, 0, 2)
         load_ws(0, range(4), nc.sync)
+        load_m_cols(0)
         load_x(2, 0)
         load_x(2, 1)
-        load_m(0, 2, 4)
         load_x(5, 0)
         load_x(5, 1)
-        load_m(1, 0, 4)
+        load_m_cols(1)
         for i in (4, 7, 6):
             load_x(i, 0)
             load_x(i, 1)
 
-        last = NG - 1
         turn_x(1, 0, V)
         turn_x(1, 1, S)
         quant_x(1, 0, 1)
-        quant_x(1, 1, 2)
-        turn_x(0, 0, V)
-        turn_x(0, 1, S)
         spread_decay()
+        quant_x(1, 1, 2)
+        decay_mul(0, 0, V)
+        turn_x(0, 0, S)
+        turn_x(0, 1, S)
+        turn_g()
         quant_x(0)
-        for k in range(3):
-            role, fil = 2 * k + 1, 2 * k
-            turn_x(role + 2, 0, V)
-            turn_x(role + 2, 1, S)
-            if k > 0:
-                quant_y(fil - 2)
-            quant_x(role + 2)
-            if k == 0:
-                decay_mul(0, 0, V)
-            else:
-                decay_mul(k // 2, k % 2, G, "xt%d" % (role + 2))
-            stage1(role, 0, S)
-            stage1(role, 1, S)
-            if k > 0:
-                gate(role, 0, 2)
-            stage1(role, 2, S)
-            stage1(role, 3, S)
-            if k == 0:
-                turn_g()
-                gate(role, 0, 2)
-            turn_x(fil + 2, 0, S)
-            turn_x(fil + 2, 1, S)
-            gate(role, 2, 4)
-            if k < 2:
-                for c in range(NCH):
-                    stage1(fil, c, V if c == 0 else S)
-            else:
-                bind_rows(0)
-                for c in range(NCH - 1):
-                    stage1(fil, c, S)
-                finish_rows(0)
-                bind_rows(1)
-                stage1(fil, NCH - 1, S)
-            quant_y(role)
-            quant_x(fil + 2)
-        decay_mul(1, 1, G, "xt%d" % (last - 1))
+        decay_mul(0, 1, V)
+        turn_x(3, 0, S)
+        turn_x(3, 1, S)
+        copy_g()
+        quant_x(3)
+        decay_mul(1, 0, G, "xt3")
+        for c in range(NCH):
+            stage1(1, c, S)
+        gate(1, 0, 1)
+        gate(1, 1, 2)
+        for c in range(2):
+            stage1(0, c, V)
+            gate(1, 2 + c, 3 + c)
+        stage1(0, 2, S)
+        turn_both(2)
+        stage1(0, 3, S)
+        turn_both(5)
+        quant_x(2)
+        quant_y(1)
+        quant_y(0)
+        quant_x(5)
+        decay_mul(1, 1, G, "xt5")
+        for c in range(NCH):
+            stage1(3, c, S)
+        for c in range(2):
+            stage1(2, c, V)
+        gate(3, 0, 2)
+        gate(3, 2, 4)
+        stage1(2, 2, S)
+        turn_both(4)
+        stage1(2, 3, S)
+        turn_both(7)
+        stage1(5, 0, S)
+        quant_x(4)
+        quant_y(3)
+        quant_y(2)
+        turn_x(6, 0, V)
+        turn_x(6, 1, S)
+        quant_x(7)
+        quant_x(6)
+        gate(5, 0, 1, G)
+        stage1(5, 1, S)
+        stage1(5, 2, S)
+        gate(5, 1, 2, G)
+        stage1(5, 3, S)
+        bind_rows(0)
+        gate(5, 2, 3)
+        stage1(4, 0, S)
+        stage1(4, 1, S)
+        bind_rows(1)
+        stage1(4, 2, S)
+        stage1(4, 3, S)
+        finish_rows(0)
+        gate(5, 3, 4)
         finish_rows(1)
         for c in range(2):
-            stage1(last, c, S)
+            stage1(7, c, S)
             bind_rows(2 + c)
-        for c in range(2):
-            finish_rows(2 + c)
-        for c in range(2):
-            gate(last, c, c + 1)
-        quant_y(last - 3)
-        quant_y(last, 0, 2)
+        finish_rows(2)
+        quant_y(5)
+        quant_y(4)
+        gate(7, 0, 1, G)
+        finish_rows(3)
+        gate(7, 1, 2)
+        quant_y(7, 0, 2)
+        last = NG - 1
         for c in range(NCH):
             stage1(last - 1, c, S)
         quant_y(last - 1)

@@ -23,7 +23,10 @@ CH = 128
 NCH = 4
 NG = 8
 BANKS = 7
-YT = {5: "xt6", 7: "y4"}
+YT = {4: "xtp"}
+XP = (7, 6)
+Y7P = [(0, 2, "xtp"), (2, 4, None)]
+RT = {}
 
 
 def tile_tensorproductrolefillerwrite_x2_kernel(
@@ -48,7 +51,7 @@ def tile_tensorproductrolefillerwrite_x2_kernel(
             return i % 2, i // 4, (i // 2) % 2
 
         x_raw, x_t, x_q, x_s, y_bf, y_q, y_s, th = {}, {}, {}, {}, {}, {}, {}, {}
-        m_raw, dm, res, res_bf = {}, {}, {}, {}
+        m_raw, dm, res, res_bf, y_pair, x_pair, y_last, g_sb = {}, {}, {}, {}, {}, {}, {}, {}
 
         ident = sbt("ident", [P, P], F32)
         w_words = [sbt("ww%d" % o, [P, 2 * F], U8) for o in range(2)]
@@ -60,7 +63,6 @@ def tile_tensorproductrolefillerwrite_x2_kernel(
         o_q = sbt("o_q", [P, B * R], U32)
         o_s = sbt("o_s", [P, B * R], U8)
         consts = ps.tile([P, 4, P], F32, name="consts", tag="consts")
-        g_sb = sbt("g_sb", [P, B * 2, PACK], BF16)
 
         def copy_on(eng, dst, src):
             if eng is nc.vector:
@@ -73,6 +75,13 @@ def tile_tensorproductrolefillerwrite_x2_kernel(
             src = (xr if role else xf)[b, half * KP:(half + 1) * KP, :].rearrange("(p j) d -> p j d", j=PACK)
             x_raw[i, h] = sbt("xraw%d_%d" % (i, h), [P, 2, D], BF16)
             nc.sync.dma_start(out=x_raw[i, h][:], in_=src[:, 2 * h:2 * h + 2, :])
+
+        def load_x_whole(i):
+            role, b, half = group(i)
+            whole = sbt("xraw%d" % i, [P, PACK, D], BF16)
+            nc.sync.dma_start(out=whole[:], in_=(xr if role else xf)[b, half * KP:(half + 1) * KP, :].rearrange("(p j) d -> p j d", j=PACK))
+            for h in range(2):
+                x_raw[i, h] = whole[:, 2 * h:2 * h + 2, :]
 
         def load_w(o):
             nc.sync.dma_start(out=w_words[o][:].bitcast(I32), in_=(wf_words, wr_words)[o][0].bitcast(I32))
@@ -96,20 +105,58 @@ def tile_tensorproductrolefillerwrite_x2_kernel(
             for j in range(2):
                 for u in range(2):
                     nc.tensor.transpose(bank[:, j, u, :], words[:, 256 * j + u:256 * (j + 1):2], ident[:])
-            if h == 0:
+            if i in XP and i not in x_t:
+                x_pair[0] = sbt("xtp", [P, 2 * PACK * P * PACK], BF16)
+                for s in range(2):
+                    x_t[XP[s]] = x_pair[0][:, 2048 * s:2048 * (s + 1)]
+            if i not in x_t:
                 x_t[i] = sbt("xt%d" % i, [P, PACK * P * PACK], BF16)
             dst = x_t[i][:].bitcast(F32)[:, 512 * h:512 * (h + 1)].rearrange("p (j m u) -> p j m u", j=2, u=2)
             copy_on(eng, dst, bank[:].rearrange("p j u m -> p j m u"))
-
-        def turn_both(i):
-            turn_x(i, 0, S)
-            turn_x(i, 1, S)
 
         def quant_x(i, h0=0, h1=2):
             if h0 == 0:
                 x_q[i] = sbt("xq%d" % i, [P, KP], U32)
                 x_s[i] = sbt("xs%d" % i, [P, KP], U8)
             nc.vector.quantize_mx(out=x_q[i][:, 256 * h0:256 * h1].bitcast(FP8X4), scales=x_s[i][:, 256 * h0:256 * h1], in_=x_t[i][:, 1024 * h0:1024 * h1])
+
+        def quant_x_pair():
+            codes = sbt("xqp", [P, 2 * KP], U32)
+            scales = sbt("xsp", [P, 2 * KP], U8)
+            nc.vector.quantize_mx(out=codes[:].bitcast(FP8X4), scales=scales[:], in_=x_pair[0][:])
+            for s in range(2):
+                x_q[XP[s]] = codes[:, KP * s:KP * (s + 1)]
+                x_s[XP[s]] = scales[:, KP * s:KP * (s + 1)]
+
+        def new_y(i):
+            if i in y_bf:
+                return
+            if i >= 6:
+                y_q[i] = sbt("yq%d" % i, [P, F], U32)
+                y_s[i] = sbt("ys%d" % i, [P, F], U8)
+                y_bf[i] = sbt("y6", [P, F * PACK], BF16) if i == 6 else None
+                return
+            fil = i - i % 2
+            both = sbt("y%d" % fil, [P, 2 * F * PACK], BF16, tag=YT.get(fil))
+            codes = sbt("yq%d" % fil, [P, 2 * F], U32)
+            scales = sbt("ys%d" % fil, [P, 2 * F], U8)
+            y_pair[fil] = (both, codes, scales)
+            for s in range(2):
+                y_bf[fil + s] = both[:, F * PACK * s:F * PACK * (s + 1)]
+                y_q[fil + s] = codes[:, F * s:F * (s + 1)]
+                y_s[fil + s] = scales[:, F * s:F * (s + 1)]
+
+        def y_cols(i, c0, c1):
+            if i < 7:
+                return y_bf[i][:, CH * PACK * c0:CH * PACK * c1]
+            p0, p1, tag = [p for p in Y7P if p[0] <= c0 < p[1]][0]
+            if p0 not in y_last:
+                y_last[p0] = sbt("y7_%d" % p0, [P, CH * PACK * (p1 - p0)], BF16, tag=tag)
+            return y_last[p0][:, CH * PACK * (c0 - p0):CH * PACK * (c1 - p0)]
+
+        def quant_pair(fil):
+            both, codes, scales = y_pair[fil]
+            nc.vector.quantize_mx(out=codes[:].bitcast(FP8X4), scales=scales[:], in_=both[:])
 
         def stage1(i, c, eng):
             o = group(i)[0]
@@ -120,11 +167,8 @@ def tile_tensorproductrolefillerwrite_x2_kernel(
                     lhsT=x_q[i][:, P * j:P * (j + 1)].bitcast(FP8X4), lhsT_scale=x_s[i][:, P * j:P * (j + 1)],
                     rhs=w_words[o][:, 2 * CH * c:2 * CH * (c + 1)].bitcast(FP4X4), rhs_scale=w_scale[o][:, CH * c:CH * (c + 1)],
                     start=True, stop=True)
-            if c == 0:
-                if o == 0:
-                    y_bf[i] = sbt("y%d" % i, [P, F * PACK], BF16)
-                y_q[i] = sbt("yq%d" % i, [P, F], U32)
-                y_s[i] = sbt("ys%d" % i, [P, F], U8)
+            if o == 0:
+                new_y(i)
             if o == 0:
                 dst = y_bf[i][:].rearrange("p (a m t) -> p a m t", a=PACK, t=PACK)[:, :, 32 * c:32 * (c + 1), :]
                 copy_on(eng, dst, bank[:].rearrange("p t (m a) -> p a m t", a=PACK))
@@ -134,19 +178,18 @@ def tile_tensorproductrolefillerwrite_x2_kernel(
                 nc.scalar.activation(out=th[i][:, CH * c:CH * (c + 1), :], in_=bank[:].rearrange("p t n -> p n t"), func=ACT.Tanh)
 
         def gate(i, c0, c1, eng=None):
-            if i not in y_bf:
-                y_bf[i] = sbt("y%d" % i, [P, F * PACK], BF16, tag=YT.get(i))
-            dst = y_bf[i][:, CH * PACK * c0:CH * PACK * c1].rearrange("p (n u e) -> p n u e", u=2, e=2)
+            new_y(i)
+            dst = y_cols(i, c0, c1).rearrange("p (n u e) -> p n u e", u=2, e=2)
             src = th[i][:, CH * c0:CH * c1, :].rearrange("p n (u e) -> p n u e", u=2)
             strength = consts[:, 2:4, :].bitcast(BF16)[:, :, i - 1:i + 1].unsqueeze(1).to_broadcast([P, CH * (c1 - c0), 2, 2])
             if eng is nc.gpsimd:
-                nc.gpsimd.tensor_tensor(out=dst.rearrange("p n u e -> p n (u e)"), in0=th[i][:, CH * c0:CH * c1, :], in1=g_sb[:, i // 2, :].unsqueeze(1).to_broadcast([P, CH * (c1 - c0), PACK]), op=ALU.mult)
+                nc.gpsimd.tensor_tensor(out=dst.rearrange("p n u e -> p n (u e)"), in0=th[i][:, CH * c0:CH * c1, :], in1=g_sb[i][:].unsqueeze(1).to_broadcast([P, CH * (c1 - c0), PACK]), op=ALU.mult)
             else:
                 nc.vector.tensor_tensor(out=dst, in0=src, in1=strength, op=ALU.mult)
 
         def quant_y(i, c0=0, c1=NCH):
             nc.vector.quantize_mx(out=y_q[i][:, CH * c0:CH * c1].bitcast(FP8X4), scales=y_s[i][:, CH * c0:CH * c1],
-                                  in_=y_bf[i][:, CH * PACK * c0:CH * PACK * c1])
+                                  in_=y_cols(i, c0, c1))
 
         def decay_mul(b, h, eng, tag=None):
             if b == 0:
@@ -176,8 +219,7 @@ def tile_tensorproductrolefillerwrite_x2_kernel(
             if a == 0:
                 res[0] = sbt("res0", [P, PACK, R], F32)
             nc.vector.scalar_tensor_tensor(out=res[0][:, a, :], in0=acc[0, a][:], scalar=1.0 / 32.0, in1=dm[0, a // 2][:, a % 2, :], op0=ALU.mult, op1=ALU.add)
-            if a == PACK - 1:
-                nc.sync.dma_start(out=out_0[0].rearrange("(p a) r -> p a r", a=PACK), in_=res[0][:])
+            nc.sync.dma_start(out=out_0[0].rearrange("(p a) r -> p a r", a=PACK)[:, a, :], in_=res[0][:, a, :])
 
         def bind_cols(c, half):
             if half == 0:
@@ -191,16 +233,20 @@ def tile_tensorproductrolefillerwrite_x2_kernel(
                                            op0=ALU.mult, op1=ALU.add)
             nc.sync.dma_start(out=out_0[1].rearrange("(p a) r -> p a r", a=PACK)[:, :, CH * c:CH * (c + 1)], in_=res[1, c][:])
 
-        def round_out(key, src, eng, tag=None):
-            res_bf[key] = sbt("rb%d_%d" % key, [P, src.shape[2] * PACK], BF16, tag=tag)
+        def round_out(b, c0, c1, eng):
+            if b not in res_bf:
+                res_bf[b] = sbt("rb%d" % b, [P, R * PACK], BF16, tag=RT.get(b))
+            src = res[0][:, :, CH * c0:CH * c1] if b == 0 else res[1, c0][:]
+            dst = res_bf[b][:, CH * PACK * c0:CH * PACK * c1]
             if eng is nc.gpsimd:
-                nc.gpsimd.tensor_scalar(out=res_bf[key][:].rearrange("p (n a) -> p n a", a=PACK), in0=src.rearrange("p a n -> p n a"),
+                nc.gpsimd.tensor_scalar(out=dst.rearrange("p (n a) -> p n a", a=PACK), in0=src.rearrange("p a n -> p n a"),
                                         scalar1=1.0, scalar2=0.0, op0=ALU.mult, op1=ALU.add)
             else:
-                copy_on(eng, res_bf[key][:].rearrange("p (n i a) -> p n a i", a=PACK, i=4), src.rearrange("p a (n i) -> p n a i", i=4))
+                copy_on(eng, dst.rearrange("p (n i a) -> p n a i", a=PACK, i=4), src.rearrange("p a (n i) -> p n a i", i=4))
 
-        def quant_out(key, c0, c1):
-            nc.vector.quantize_mx(out=o_q[:, c0:c1].bitcast(FP8X4), scales=o_s[:, c0:c1], in_=res_bf[key][:])
+        def quant_out(b, c0, c1):
+            cols = slice(R * b + CH * c0, R * b + CH * c1)
+            nc.vector.quantize_mx(out=o_q[:, cols].bitcast(FP8X4), scales=o_s[:, cols], in_=res_bf[b][:, CH * PACK * c0:CH * PACK * c1])
 
         def store_words(c0, c1):
             dst = out_1[0].rearrange("p m t -> p (m t)").bitcast(I32)
@@ -220,8 +266,9 @@ def tile_tensorproductrolefillerwrite_x2_kernel(
             for u in range(2):
                 nc.tensor.transpose(consts[:, 2 + u, :], g_rows[:].bitcast(F32)[:, u:2 * P:2], ident[:])
 
-        def copy_g():
-            nc.scalar.copy(out=g_sb[:].rearrange("p q t -> p (q t)").bitcast(F32).rearrange("p (q u) -> p q u", u=2), in_=consts[:, 2:4, 0:4].rearrange("p u q -> p q u"))
+        def copy_g(i, eng):
+            g_sb[i] = sbt("g_sb%d" % i, [P, PACK], BF16)
+            copy_on(eng, g_sb[i][:].bitcast(F32), consts[:, 2:4, i // 2])
 
         V, S, G = nc.vector, nc.scalar, nc.gpsimd
         load_x(1, 0)
@@ -248,14 +295,14 @@ def tile_tensorproductrolefillerwrite_x2_kernel(
         load_m_cols(0)
         load_x(2, 0)
         load_x(2, 1)
+        load_m_cols(1)
         load_x(5, 0)
         load_x(5, 1)
-        load_m_cols(1)
         for i in (4, 7, 6):
             load_x(i, 0)
             load_x(i, 1)
 
-        turn_x(1, 0, V)
+        turn_x(1, 0, S)
         turn_x(1, 1, S)
         quant_x(1, 0, 1)
         spread_decay()
@@ -268,92 +315,106 @@ def tile_tensorproductrolefillerwrite_x2_kernel(
         decay_mul(0, 1, V)
         turn_x(3, 0, S)
         turn_x(3, 1, S)
-        copy_g()
+        copy_g(5, S)
+        copy_g(7, S)
         quant_x(3)
         decay_mul(1, 0, G, "xt3")
-        for c in range(NCH):
-            stage1(1, c, S)
-        gate(1, 0, 1)
-        gate(1, 1, 2)
-        for c in range(2):
-            stage1(0, c, V)
-            gate(1, 2 + c, 3 + c)
+        decay_mul(1, 1, G)
+        stage1(1, 0, S)
+        stage1(1, 1, S)
+        gate(1, 0, 2)
+        stage1(1, 2, S)
+        stage1(1, 3, S)
+        stage1(0, 0, V)
+        stage1(0, 1, S)
         stage1(0, 2, S)
-        turn_both(2)
-        stage1(0, 3, S)
-        turn_both(5)
-        quant_x(2)
-        quant_y(1)
-        quant_y(0)
-        quant_x(5)
-        decay_mul(1, 1, G, "xt5")
-        for c in range(NCH):
-            stage1(3, c, S)
-        for c in range(2):
-            stage1(2, c, V)
+        stage1(0, 3, V)
+        gate(1, 2, 4)
+        stage1(3, 0, S)
+        stage1(3, 1, S)
         gate(3, 0, 2)
-        gate(3, 2, 4)
-        stage1(2, 2, S)
-        turn_both(4)
-        stage1(2, 3, S)
-        turn_both(7)
+        turn_x(2, 0, S)
+        turn_x(2, 1, S)
+        stage1(3, 2, S)
+        turn_x(5, 0, V)
+        turn_x(5, 1, S)
+        stage1(3, 3, S)
+        turn_x(4, 0, S)
+        turn_x(4, 1, S)
+        quant_x(2)
+        quant_pair(0)
+        quant_x(5)
+        copy_g(3, V)
+        gate(3, 3, 4, G)
+        gate(3, 2, 3)
+        stage1(2, 0, S)
+        stage1(2, 1, S)
+        stage1(2, 2, V)
+        turn_x(7, 0, S)
+        turn_x(7, 1, S)
+        stage1(2, 3, V)
         stage1(5, 0, S)
-        quant_x(4)
-        quant_y(3)
-        quant_y(2)
-        turn_x(6, 0, V)
+        turn_x(6, 0, S)
         turn_x(6, 1, S)
-        quant_x(7)
-        quant_x(6)
-        gate(5, 0, 1, G)
+        quant_x(4)
+        quant_pair(2)
+        quant_x_pair()
         stage1(5, 1, S)
+        gate(5, 0, 2, G)
         stage1(5, 2, S)
-        gate(5, 1, 2, G)
         stage1(5, 3, S)
-        bind_rows(0)
-        gate(5, 2, 3)
         stage1(4, 0, S)
+        bind_rows(0)
         stage1(4, 1, S)
-        bind_rows(1)
         stage1(4, 2, S)
+        bind_rows(1)
         stage1(4, 3, S)
         finish_rows(0)
-        gate(5, 3, 4)
+        gate(5, 2, 4)
         finish_rows(1)
-        for c in range(2):
-            stage1(7, c, S)
-            bind_rows(2 + c)
+        stage1(7, 0, S)
+        bind_rows(2)
+        stage1(7, 1, S)
+        bind_rows(3)
         finish_rows(2)
-        quant_y(5)
-        quant_y(4)
-        gate(7, 0, 1, G)
+        quant_pair(4)
+        gate(7, 1, 2, G)
+        gate(7, 0, 1)
         finish_rows(3)
-        gate(7, 1, 2)
+        stage1(6, 0, S)
+        stage1(6, 1, S)
+        stage1(6, 2, S)
+        stage1(6, 3, S)
         quant_y(7, 0, 2)
-        last = NG - 1
-        for c in range(NCH):
-            stage1(last - 1, c, S)
-        quant_y(last - 1)
-        for c in range(2, NCH):
-            stage1(last, c, S)
-        for c in range(NCH):
-            bind_cols(c, 0)
-        for c in range(2):
-            bind_cols(c, 1)
-            gate(last, 2 + c, 3 + c)
-        for c in range(2):
-            quant_y(last, 2 + c, 3 + c)
-            bind_cols(2 + c, 1)
-            finish_cols(c)
-            round_out((0, c), res[0][:, :, 256 * c:256 * (c + 1)], S)
-        for c in range(2):
-            finish_cols(2 + c)
-            quant_out((0, c), 256 * c, 256 * (c + 1))
-            round_out((1, c), res[1, c][:], S)
-        store_words(0, R)
-        round_out((1, 2), res[1, 2][:], S)
-        round_out((1, 3), res[1, 3][:], V)
-        for c in (0, 1, 3, 2):
-            quant_out((1, c), R + CH * c, R + CH * (c + 1))
-        store_words(R, 2 * R)
+        quant_y(6)
+        stage1(7, 2, S)
+        stage1(7, 3, S)
+        bind_cols(0, 0)
+        bind_cols(1, 0)
+        bind_cols(2, 0)
+        bind_cols(3, 0)
+        bind_cols(0, 1)
+        bind_cols(1, 1)
+        gate(7, 2, 3)
+        gate(7, 3, 4)
+        quant_y(7, 2, 3)
+        bind_cols(2, 1)
+        finish_cols(0)
+        round_out(0, 0, 2, S)
+        quant_y(7, 3, 4)
+        bind_cols(3, 1)
+        finish_cols(1)
+        round_out(0, 2, 4, S)
+        finish_cols(2)
+        quant_out(0, 0, 2)
+        finish_cols(3)
+        round_out(1, 0, 1, S)
+        round_out(1, 1, 2, S)
+        quant_out(0, 2, 4)
+        store_words(CH * 0, CH * 4)
+        round_out(1, 3, 4, V)
+        quant_out(1, 0, 2)
+        round_out(1, 2, 3, S)
+        quant_out(1, 2, 4)
+        store_words(CH * 4, CH * 8)
         store_scales()

@@ -25,6 +25,7 @@ NG = 8
 BANKS = 7
 YT = {4: "xtp"}
 XP = (7, 6)
+NARROW = ((7, 2), (7, 3))
 Y7P = [(0, 2, "xtp"), (2, 4, None)]
 RT = {}
 
@@ -158,8 +159,24 @@ def tile_tensorproductrolefillerwrite_x2_kernel(
             both, codes, scales = y_pair[fil]
             nc.vector.quantize_mx(out=codes[:].bitcast(FP8X4), scales=scales[:], in_=both[:])
 
+        def stage1_wide(i, c):
+            h, u = divmod(c, 2)
+            bank = next_bank("M%d%d" % (i, c), [P, 2, 2 * CH])
+            for e in range(2):
+                j = 2 * u + e
+                nc.tensor.matmul_mx(
+                    out=bank[:, e, :],
+                    lhsT=x_q[i][:, P * j:P * (j + 1)].bitcast(FP8X4), lhsT_scale=x_s[i][:, P * j:P * (j + 1)],
+                    rhs=w_words[1][:, 4 * CH * h:4 * CH * (h + 1)].bitcast(FP4X4), rhs_scale=w_scale[1][:, 2 * CH * h:2 * CH * (h + 1)],
+                    start=True, stop=True)
+            if c == 0:
+                th[i] = sbt("th%d" % i, [P, 2, R, 2], F32)
+            nc.scalar.activation(out=th[i][:, u, 2 * CH * h:2 * CH * (h + 1), :], in_=bank[:].rearrange("p e n -> p n e"), func=ACT.Tanh)
+
         def stage1(i, c, eng):
             o = group(i)[0]
+            if o == 1 and (i, c) not in NARROW:
+                return stage1_wide(i, c)
             bank = next_bank("M%d%d" % (i, c), [P, PACK, CH])
             for j in range(PACK):
                 nc.tensor.matmul_mx(
@@ -174,16 +191,16 @@ def tile_tensorproductrolefillerwrite_x2_kernel(
                 copy_on(eng, dst, bank[:].rearrange("p t (m a) -> p a m t", a=PACK))
             else:
                 if c == 0:
-                    th[i] = sbt("th%d" % i, [P, R, PACK], F32)
-                nc.scalar.activation(out=th[i][:, CH * c:CH * (c + 1), :], in_=bank[:].rearrange("p t n -> p n t"), func=ACT.Tanh)
+                    th[i] = sbt("th%d" % i, [P, 2, R, 2], F32)
+                nc.scalar.activation(out=th[i][:, :, CH * c:CH * (c + 1), :].rearrange("p u n e -> p n u e"), in_=bank[:].rearrange("p (u e) n -> p n u e", u=2), func=ACT.Tanh)
 
         def gate(i, c0, c1, eng=None):
             new_y(i)
             dst = y_cols(i, c0, c1).rearrange("p (n u e) -> p n u e", u=2, e=2)
-            src = th[i][:, CH * c0:CH * c1, :].rearrange("p n (u e) -> p n u e", u=2)
+            src = th[i][:, :, CH * c0:CH * c1, :].rearrange("p u n e -> p n u e")
             strength = consts[:, 2:4, :].bitcast(BF16)[:, :, i - 1:i + 1].unsqueeze(1).to_broadcast([P, CH * (c1 - c0), 2, 2])
             if eng is nc.gpsimd:
-                nc.gpsimd.tensor_tensor(out=dst.rearrange("p n u e -> p n (u e)"), in0=th[i][:, CH * c0:CH * c1, :], in1=g_sb[i][:].unsqueeze(1).to_broadcast([P, CH * (c1 - c0), PACK]), op=ALU.mult)
+                nc.gpsimd.tensor_tensor(out=dst, in0=src, in1=g_sb[i][:].rearrange("p (u e) -> p u e", u=2).unsqueeze(1).to_broadcast([P, CH * (c1 - c0), 2, 2]), op=ALU.mult)
             else:
                 nc.vector.tensor_tensor(out=dst, in0=src, in1=strength, op=ALU.mult)
 

@@ -319,7 +319,7 @@ def tile_tensorproductrolefillerwrite_x2_kernel(
             load_x(i, 0)
             load_x(i, 1)
 
-        turn_x(1, 0, S)
+        turn_x(1, 0, V)
         turn_x(1, 1, S)
         quant_x(1, 0, 1)
         spread_decay()
@@ -339,52 +339,52 @@ def tile_tensorproductrolefillerwrite_x2_kernel(
         decay_mul(1, 1, G)
         stage1(1, 0, S)
         stage1(1, 1, S)
-        gate(1, 0, 2)
+        stage1(0, 0, V)
         stage1(1, 2, S)
         stage1(1, 3, S)
-        stage1(0, 0, V)
+        gate(1, 0, 2)
         stage1(0, 1, S)
-        stage1(0, 2, S)
-        stage1(0, 3, V)
+        stage1(0, 2, V)
         gate(1, 2, 4)
         stage1(3, 0, S)
-        stage1(3, 1, S)
-        gate(3, 0, 2)
         turn_x(2, 0, S)
-        turn_x(2, 1, S)
-        stage1(3, 2, S)
+        turn_x(2, 1, V)
+        stage1(3, 1, S)
+        stage1(0, 3, S)
         turn_x(5, 0, V)
         turn_x(5, 1, S)
+        stage1(3, 2, S)
         stage1(3, 3, S)
         turn_x(4, 0, S)
         turn_x(4, 1, S)
+        gate(3, 0, 1)
         quant_x(2)
         quant_pair(0)
         quant_x(5)
         copy_g(3, V)
         gate(3, 3, 4, G)
-        gate(3, 2, 3)
+        gate(3, 1, 3)
         stage1(2, 0, S)
-        stage1(2, 1, S)
-        stage1(2, 2, V)
+        stage1(2, 1, V)
         turn_x(7, 0, S)
         turn_x(7, 1, S)
-        stage1(2, 3, V)
-        stage1(5, 0, S)
+        stage1(2, 2, V)
+        stage1(2, 3, S)
         turn_x(6, 0, S)
         turn_x(6, 1, S)
         quant_x(4)
         quant_pair(2)
         quant_x_pair()
+        stage1(5, 0, S)
         stage1(5, 1, S)
         gate(5, 0, 2, G)
         stage1(5, 2, S)
         stage1(5, 3, S)
-        stage1(4, 0, S)
         bind_rows(0)
+        stage1(4, 0, S)
         stage1(4, 1, S)
-        stage1(4, 2, S)
         bind_rows(1)
+        stage1(4, 2, S)
         stage1(4, 3, S)
         finish_rows(0)
         gate(5, 2, 4)
@@ -392,15 +392,15 @@ def tile_tensorproductrolefillerwrite_x2_kernel(
         stage1(7, 0, S)
         bind_rows(2)
         stage1(7, 1, S)
-        bind_rows(3)
         finish_rows(2)
+        stage1(6, 0, S)
+        bind_rows(3)
         quant_pair(4)
         gate(7, 1, 2, G)
         gate(7, 0, 1)
         finish_rows(3)
-        stage1(6, 0, S)
         stage1(6, 1, S)
-        stage1(6, 2, S)
+        stage1(6, 2, V)
         stage1(6, 3, S)
         quant_y(7, 0, 2)
         quant_y(6)

@@ -60,7 +60,6 @@ def tile_tensorproductrolefillerwrite_x2_kernel(
         g_rows = sbt("g_rows", [P, KP], BF16)
         d_col = sbt("d_col", [P, PACK], BF16)
         d_row = sbt("d_row", [P, R], BF16)
-        warm = sbt("warm", [P, 1], F32)
         o_q = sbt("o_q", [P, B * R], U32)
         o_s = sbt("o_s", [P, B * R], U8)
         consts = ps.tile([P, 4, P], F32, name="consts", tag="consts")
@@ -297,12 +296,10 @@ def tile_tensorproductrolefillerwrite_x2_kernel(
         make_identity(nc, ident[:])
         nc.vector.memset(g_rows[:].bitcast(I32), 0)
         nc.vector.memset(w_scale[1][:].bitcast(I32), 0)
-        nc.vector.memset(warm[:], 0.0)
         nc.vector.memset(w_scale[0][:].bitcast(I32), 0)
         nc.scalar.dma_start(out=g_rows[0:4, :], in_=g.rearrange("b (h k) -> (b h) k", h=2))
         load_ws(1, (0,), nc.scalar)
         load_ws(1, (1, 2, 3), nc.gpsimd)
-        nc.scalar.activation(out=warm[:], in_=warm[:], func=ACT.Tanh)
         load_x(3, 0)
         load_x(3, 1)
         load_w(1)

@@ -64,11 +64,28 @@ def tile_tensorproductrolefillerwrite_x2_kernel(
         o_s = sbt("o_s", [P, B * R], U8)
         consts = ps.tile([P, 4, P], F32, name="consts", tag="consts")
 
+        held = []
+
+        def on_scalar(call):
+            if held:
+                held.append(call)
+            else:
+                call()
+
+        def later_first(first, second):
+            held.append(None)
+            first()
+            second()
+            calls = held[1:]
+            held.clear()
+            for call in reversed(calls):
+                call()
+
         def copy_on(eng, dst, src):
             if eng is nc.vector:
                 nc.vector.tensor_copy(out=dst, in_=src)
             else:
-                nc.scalar.copy(out=dst, in_=src)
+                on_scalar(lambda: nc.scalar.copy(out=dst, in_=src))
 
         def load_x(i, h):
             role, b, half = group(i)
@@ -170,7 +187,7 @@ def tile_tensorproductrolefillerwrite_x2_kernel(
                     start=True, stop=True)
             if c == 0:
                 th[i] = sbt("th%d" % i, [P, 2, R, 2], F32)
-            nc.scalar.activation(out=th[i][:, u, 2 * CH * h:2 * CH * (h + 1), :], in_=bank[:].rearrange("p e n -> p n e"), func=ACT.Tanh)
+            on_scalar(lambda: nc.scalar.activation(out=th[i][:, u, 2 * CH * h:2 * CH * (h + 1), :], in_=bank[:].rearrange("p e n -> p n e"), func=ACT.Tanh))
 
         def stage1(i, c, eng):
             o = group(i)[0]
@@ -191,7 +208,7 @@ def tile_tensorproductrolefillerwrite_x2_kernel(
             else:
                 if c == 0:
                     th[i] = sbt("th%d" % i, [P, 2, R, 2], F32)
-                nc.scalar.activation(out=th[i][:, :, CH * c:CH * (c + 1), :].rearrange("p u n e -> p n u e"), in_=bank[:].rearrange("p (u e) n -> p n u e", u=2), func=ACT.Tanh)
+                on_scalar(lambda: nc.scalar.activation(out=th[i][:, :, CH * c:CH * (c + 1), :].rearrange("p u n e -> p n u e"), in_=bank[:].rearrange("p (u e) n -> p n u e", u=2), func=ACT.Tanh))
 
         def gate(i, c0, c1, eng=None):
             new_y(i)
@@ -337,8 +354,7 @@ def tile_tensorproductrolefillerwrite_x2_kernel(
         stage1(1, 0, S)
         stage1(1, 1, S)
         stage1(0, 0, V)
-        stage1(1, 2, S)
-        stage1(1, 3, S)
+        later_first(lambda: stage1(1, 2, S), lambda: stage1(1, 3, S))
         gate(1, 0, 2)
         stage1(0, 1, S)
         stage1(0, 2, V)
@@ -346,14 +362,11 @@ def tile_tensorproductrolefillerwrite_x2_kernel(
         stage1(3, 0, S)
         turn_x(2, 0, S)
         turn_x(2, 1, V)
-        stage1(3, 1, S)
-        stage1(0, 3, S)
+        later_first(lambda: stage1(3, 1, S), lambda: stage1(0, 3, S))
         turn_x(5, 0, V)
         turn_x(5, 1, S)
-        stage1(3, 2, S)
-        stage1(3, 3, S)
-        turn_x(4, 0, S)
-        turn_x(4, 1, S)
+        later_first(lambda: stage1(3, 2, S), lambda: stage1(3, 3, S))
+        later_first(lambda: turn_x(4, 0, S), lambda: turn_x(4, 1, S))
         gate(3, 0, 1)
         quant_x(2)
         quant_pair(0)
@@ -372,17 +385,13 @@ def tile_tensorproductrolefillerwrite_x2_kernel(
         quant_x(4)
         quant_pair(2)
         quant_x_pair()
-        stage1(5, 0, S)
-        stage1(5, 1, S)
+        later_first(lambda: stage1(5, 0, S), lambda: stage1(5, 1, S))
         gate(5, 0, 2, G)
-        stage1(5, 2, S)
-        stage1(5, 3, S)
+        later_first(lambda: stage1(5, 2, S), lambda: stage1(5, 3, S))
         bind_rows(0)
-        stage1(4, 0, S)
-        stage1(4, 1, S)
+        later_first(lambda: stage1(4, 0, S), lambda: stage1(4, 1, S))
         bind_rows(1)
-        stage1(4, 2, S)
-        stage1(4, 3, S)
+        later_first(lambda: stage1(4, 2, S), lambda: stage1(4, 3, S))
         finish_rows(0)
         gate(5, 2, 4)
         finish_rows(1)
@@ -397,12 +406,10 @@ def tile_tensorproductrolefillerwrite_x2_kernel(
         gate(7, 0, 1)
         finish_rows(3)
         stage1(6, 1, S)
-        stage1(6, 2, V)
-        stage1(6, 3, S)
+        later_first(lambda: stage1(6, 2, S), lambda: stage1(6, 3, S))
         quant_y(7, 0, 2)
         quant_y(6)
-        stage1(7, 2, S)
-        stage1(7, 3, S)
+        later_first(lambda: stage1(7, 2, S), lambda: stage1(7, 3, S))
         bind_cols(0, 0)
         bind_cols(1, 0)
         bind_cols(2, 0)

@@ -21,13 +21,10 @@ PACK = 4
 KP = P * PACK
 CH = 128
 NCH = 4
-NG = 8
 BANKS = 7
-YT = {4: "xtp"}
-XP = (7, 6)
-NARROW = ((7, 2), (7, 3))
-Y7P = [(0, 2, "xtp"), (2, 4, None)]
-RT = {}
+FIL, ROL = 0, 1
+Y_TAGS = {"2": "y1"}
+X_PAIRS = (((ROL, 3), (FIL, 3)),)
 
 
 def tile_tensorproductrolefillerwrite_x2_kernel(
@@ -38,21 +35,33 @@ def tile_tensorproductrolefillerwrite_x2_kernel(
         sb = ctx.enter_context(tc.tile_pool(name="sb", bufs=1))
         ps = ctx.enter_context(tc.psum_pool(name="ps", bufs=1))
         ctx.enter_context(tc.manual_schedule())
+        V, S, G = nc.vector, nc.scalar, nc.gpsimd
 
         def sbt(name, shape, dtype, tag=None):
             return sb.tile(shape, dtype, name=name, tag=tag or name, align_bytes=64)
 
-        taken = []
+        free_banks = list(range(BANKS))
+        waiting = {}
+        held = {}
 
         def next_bank(name, shape):
-            taken.append(name)
-            return ps.tile(shape, F32, name=name, tag="bank%d" % (len(taken) % BANKS))
+            n = free_banks.pop(0)
+            return n, ps.tile(shape, F32, name=name, tag="bank%d" % n)
 
-        def group(i):
-            return i % 2, i // 4, (i // 2) % 2
+        def newest_first(count):
+            free_banks[:count] = reversed(free_banks[:count])
+
+        def take(eng, *keys):
+            for key in keys:
+                n, empty = waiting.pop(key)
+                empty(eng)
+                free_banks.append(n)
+
+        def label(o, k):
+            return "%s%d" % ("FR"[o], k)
 
         x_raw, x_t, x_q, x_s, y_bf, y_q, y_s, th = {}, {}, {}, {}, {}, {}, {}, {}
-        m_raw, dm, res, res_bf, y_pair, x_pair, y_last, g_sb = {}, {}, {}, {}, {}, {}, {}, {}
+        m_raw, dm, res, res_bf, y_pair, g_sb, acc, x_pair = {}, {}, {}, {}, {}, {}, {}, {}
 
         ident = sbt("ident", [P, P], F32)
         w_words = [sbt("ww%d" % o, [P, 2 * F], U8) for o in range(2)]
@@ -64,365 +73,408 @@ def tile_tensorproductrolefillerwrite_x2_kernel(
         o_s = sbt("o_s", [P, B * R], U8)
         consts = ps.tile([P, 4, P], F32, name="consts", tag="consts")
 
-        held = []
-
-        def on_scalar(call):
-            if held:
-                held.append(call)
-            else:
-                call()
-
-        def later_first(first, second):
-            held.append(None)
-            first()
-            second()
-            calls = held[1:]
-            held.clear()
-            for call in reversed(calls):
-                call()
-
         def copy_on(eng, dst, src):
-            if eng is nc.vector:
+            if eng is V:
                 nc.vector.tensor_copy(out=dst, in_=src)
             else:
-                on_scalar(lambda: nc.scalar.copy(out=dst, in_=src))
+                nc.scalar.copy(out=dst, in_=src)
 
-        def load_x(i, h):
-            role, b, half = group(i)
-            src = (xr if role else xf)[b, half * KP:(half + 1) * KP, :].rearrange("(p j) d -> p j d", j=PACK)
-            x_raw[i, h] = sbt("xraw%d_%d" % (i, h), [P, 2, D], BF16)
-            nc.sync.dma_start(out=x_raw[i, h][:], in_=src[:, 2 * h:2 * h + 2, :])
+        def x_rows(o, k):
+            b, half = divmod(k, 2)
+            return (xf, xr)[o][b, half * KP:(half + 1) * KP, :].rearrange("(p j) d -> p j d", j=PACK)
 
-        def load_x_whole(i):
-            role, b, half = group(i)
-            whole = sbt("xraw%d" % i, [P, PACK, D], BF16)
-            nc.sync.dma_start(out=whole[:], in_=(xr if role else xf)[b, half * KP:(half + 1) * KP, :].rearrange("(p j) d -> p j d", j=PACK))
+        def load_x_half(o, k, h):
+            x_raw[o, k, h] = sbt("xraw%s_%d" % (label(o, k), h), [P, 2 * D], BF16)
+            nc.sync.dma_start(out=x_raw[o, k, h][:].rearrange("p (j d) -> p j d", j=2), in_=x_rows(o, k)[:, 2 * h:2 * h + 2, :])
+
+        def load_x(o, k):
+            whole = sbt("xraw%s" % label(o, k), [P, PACK * D], BF16)
+            nc.sync.dma_start(out=whole[:].rearrange("p (j d) -> p j d", j=PACK), in_=x_rows(o, k))
             for h in range(2):
-                x_raw[i, h] = whole[:, 2 * h:2 * h + 2, :]
+                x_raw[o, k, h] = whole[:, 2 * D * h:2 * D * (h + 1)]
 
-        def load_w(o):
-            nc.sync.dma_start(out=w_words[o][:].bitcast(I32), in_=(wf_words, wr_words)[o][0].bitcast(I32))
+        def load_w(o, queue):
+            queue.dma_start(out=w_words[o][:].bitcast(I32), in_=(wf_words, wr_words)[o][0].bitcast(I32))
 
         def load_ws(o, quadrants, queue):
             src = (wf_scales, wr_scales)[o][0].bitcast(I32)
             for q in quadrants:
                 queue.dma_start(out=w_scale[o][:].bitcast(I32)[32 * q:32 * q + 4, :], in_=src[4 * q:4 * q + 4, :])
 
-        def load_m(b, j0, j1):
-            m_raw[b, j0] = sbt("m%d_%d" % (b, j0), [P, j1 - j0, R], BF16)
-            nc.sync.dma_start(out=m_raw[b, j0][:], in_=m0[b].rearrange("(p j) r -> p j r", j=PACK)[:, j0:j1, :])
+        def load_m(b, h):
+            m_raw[b, h] = sbt("m%d_%d" % (b, h), [P, 2, R], BF16)
+            nc.sync.dma_start(out=m_raw[b, h][:], in_=m0[b].rearrange("(p j) r -> p j r", j=PACK)[:, 2 * h:2 * h + 2, :])
 
-        def load_m_cols(h):
-            m_raw[1, h] = sbt("m1_%d" % h, [P, PACK, 256], BF16)
-            nc.sync.dma_start(out=m_raw[1, h][:], in_=m0[1].rearrange("(p j) r -> p j r", j=PACK)[:, :, 256 * h:256 * (h + 1)])
+        def load_m_whole(b):
+            whole = sbt("m%d" % b, [P, PACK, R], BF16)
+            nc.sync.dma_start(out=whole[:], in_=m0[b].rearrange("(p j) r -> p j r", j=PACK))
+            m_raw[b] = whole
 
-        def turn_x(i, h, eng):
-            bank = next_bank("T%d%d" % (i, h), [P, 2, 2, P])
-            words = x_raw[i, h][:].rearrange("p j d -> p (j d)").bitcast(F32)
+        def turn_half(o, k, h):
+            n, bank = next_bank("T%s%d" % (label(o, k), h), [P, 2, 2, P])
+            words = x_raw[o, k, h][:].bitcast(F32)
             for j in range(2):
                 for u in range(2):
                     nc.tensor.transpose(bank[:, j, u, :], words[:, 256 * j + u:256 * (j + 1):2], ident[:])
-            if i in XP and i not in x_t:
-                x_pair[0] = sbt("xtp", [P, 2 * PACK * P * PACK], BF16)
-                for s in range(2):
-                    x_t[XP[s]] = x_pair[0][:, 2048 * s:2048 * (s + 1)]
-            if i not in x_t:
-                x_t[i] = sbt("xt%d" % i, [P, PACK * P * PACK], BF16)
-            dst = x_t[i][:].bitcast(F32)[:, 512 * h:512 * (h + 1)].rearrange("p (j m u) -> p j m u", j=2, u=2)
-            copy_on(eng, dst, bank[:].rearrange("p j u m -> p j m u"))
+            for m, pair in enumerate(X_PAIRS):
+                if (o, k) in pair and m not in x_pair:
+                    x_pair[m] = sbt("xtp%d" % m, [P, 2 * KP * PACK], BF16)
+                    for s in range(2):
+                        x_t[pair[s]] = x_pair[m][:, KP * PACK * s:KP * PACK * (s + 1)]
+            if (o, k) not in x_t:
+                x_t[o, k] = sbt("xt" + label(o, k), [P, KP * PACK], BF16)
+            dst = x_t[o, k][:].bitcast(F32)[:, 512 * h:512 * (h + 1)].rearrange("p (j m u) -> p j m u", j=2, u=2)
+            waiting["x%s%d" % (label(o, k), h)] = (n, lambda eng: copy_on(eng, dst, bank[:].rearrange("p j u m -> p j m u")))
 
-        def quant_x(i, h0=0, h1=2):
+        def turn(o, k):
+            for h in range(2):
+                turn_half(o, k, h)
+
+        def quant_x(o, k, h0=0, h1=2):
             if h0 == 0:
-                x_q[i] = sbt("xq%d" % i, [P, KP], U32)
-                x_s[i] = sbt("xs%d" % i, [P, KP], U8)
-            nc.vector.quantize_mx(out=x_q[i][:, 256 * h0:256 * h1].bitcast(FP8X4), scales=x_s[i][:, 256 * h0:256 * h1], in_=x_t[i][:, 1024 * h0:1024 * h1])
+                x_q[o, k] = sbt("xq" + label(o, k), [P, KP], U32)
+                x_s[o, k] = sbt("xs" + label(o, k), [P, KP], U8)
+            cols = slice(256 * h0, 256 * h1)
+            nc.vector.quantize_mx(out=x_q[o, k][:, cols].bitcast(FP8X4), scales=x_s[o, k][:, cols], in_=x_t[o, k][:, 1024 * h0:1024 * h1])
 
-        def quant_x_pair():
-            codes = sbt("xqp", [P, 2 * KP], U32)
-            scales = sbt("xsp", [P, 2 * KP], U8)
-            nc.vector.quantize_mx(out=codes[:].bitcast(FP8X4), scales=scales[:], in_=x_pair[0][:])
+        def quant_x_pair(n):
+            codes = sbt("xqp%d" % n, [P, 2 * KP], U32)
+            scales = sbt("xsp%d" % n, [P, 2 * KP], U8)
+            nc.vector.quantize_mx(out=codes[:].bitcast(FP8X4), scales=scales[:], in_=x_pair[n][:])
             for s in range(2):
-                x_q[XP[s]] = codes[:, KP * s:KP * (s + 1)]
-                x_s[XP[s]] = scales[:, KP * s:KP * (s + 1)]
+                x_q[X_PAIRS[n][s]] = codes[:, KP * s:KP * (s + 1)]
+                x_s[X_PAIRS[n][s]] = scales[:, KP * s:KP * (s + 1)]
 
-        def new_y(i):
-            if i in y_bf:
-                return
-            if i >= 6:
-                y_q[i] = sbt("yq%d" % i, [P, F], U32)
-                y_s[i] = sbt("ys%d" % i, [P, F], U8)
-                y_bf[i] = sbt("y6", [P, F * PACK], BF16) if i == 6 else None
-                return
-            fil = i - i % 2
-            both = sbt("y%d" % fil, [P, 2 * F * PACK], BF16, tag=YT.get(fil))
-            codes = sbt("yq%d" % fil, [P, 2 * F], U32)
-            scales = sbt("ys%d" % fil, [P, 2 * F], U8)
-            y_pair[fil] = (both, codes, scales)
-            for s in range(2):
-                y_bf[fil + s] = both[:, F * PACK * s:F * PACK * (s + 1)]
-                y_q[fil + s] = codes[:, F * s:F * (s + 1)]
-                y_s[fil + s] = scales[:, F * s:F * (s + 1)]
+        def y_tiles(name, groups):
+            width = F * groups
+            y_pair[name] = (sbt("y" + name, [P, width * PACK], BF16, tag=Y_TAGS.get(name)), sbt("yq" + name, [P, width], U32), sbt("ys" + name, [P, width], U8))
 
-        def y_cols(i, c0, c1):
-            if i < 7:
-                return y_bf[i][:, CH * PACK * c0:CH * PACK * c1]
-            p0, p1, tag = [p for p in Y7P if p[0] <= c0 < p[1]][0]
-            if p0 not in y_last:
-                y_last[p0] = sbt("y7_%d" % p0, [P, CH * PACK * (p1 - p0)], BF16, tag=tag)
-            return y_last[p0][:, CH * PACK * (c0 - p0):CH * PACK * (c1 - p0)]
+        def y_at(o, k, c0, c1):
+            name, col = str(k), F * o + int(CH * c0)
+            if name not in y_pair:
+                y_tiles(name, 2)
+            values, codes, scales = y_pair[name]
+            n = int(CH * (c1 - c0))
+            return values[:, PACK * col:PACK * (col + n)], codes[:, col:col + n], scales[:, col:col + n]
 
-        def quant_pair(fil):
-            both, codes, scales = y_pair[fil]
-            nc.vector.quantize_mx(out=codes[:].bitcast(FP8X4), scales=scales[:], in_=both[:])
+        def quant_y(o, k, c0=0, c1=NCH):
+            values, codes, scales = y_at(o, k, c0, c1)
+            nc.vector.quantize_mx(out=codes.bitcast(FP8X4), scales=scales, in_=values)
 
-        def stage1_wide(i, c):
-            h, u = divmod(c, 2)
-            bank = next_bank("M%d%d" % (i, c), [P, 2, 2 * CH])
-            for e in range(2):
-                j = 2 * u + e
-                nc.tensor.matmul_mx(
-                    out=bank[:, e, :],
-                    lhsT=x_q[i][:, P * j:P * (j + 1)].bitcast(FP8X4), lhsT_scale=x_s[i][:, P * j:P * (j + 1)],
-                    rhs=w_words[1][:, 4 * CH * h:4 * CH * (h + 1)].bitcast(FP4X4), rhs_scale=w_scale[1][:, 2 * CH * h:2 * CH * (h + 1)],
-                    start=True, stop=True)
-            if c == 0:
-                th[i] = sbt("th%d" % i, [P, 2, R, 2], F32)
-            on_scalar(lambda: nc.scalar.activation(out=th[i][:, u, 2 * CH * h:2 * CH * (h + 1), :], in_=bank[:].rearrange("p e n -> p n e"), func=ACT.Tanh))
+        def quant_pair(k):
+            quant_y(FIL, k, 0, 2 * NCH)
 
-        def stage1(i, c, eng):
-            o = group(i)[0]
-            if o == 1 and (i, c) not in NARROW:
-                return stage1_wide(i, c)
-            bank = next_bank("M%d%d" % (i, c), [P, PACK, CH])
-            for j in range(PACK):
-                nc.tensor.matmul_mx(
-                    out=bank[:, j, :],
-                    lhsT=x_q[i][:, P * j:P * (j + 1)].bitcast(FP8X4), lhsT_scale=x_s[i][:, P * j:P * (j + 1)],
-                    rhs=w_words[o][:, 2 * CH * c:2 * CH * (c + 1)].bitcast(FP4X4), rhs_scale=w_scale[o][:, CH * c:CH * (c + 1)],
-                    start=True, stop=True)
-            if o == 0:
-                new_y(i)
-            if o == 0:
-                dst = y_bf[i][:].rearrange("p (a m t) -> p a m t", a=PACK, t=PACK)[:, :, 32 * c:32 * (c + 1), :]
-                copy_on(eng, dst, bank[:].rearrange("p t (m a) -> p a m t", a=PACK))
-            else:
-                if c == 0:
-                    th[i] = sbt("th%d" % i, [P, 2, R, 2], F32)
-                on_scalar(lambda: nc.scalar.activation(out=th[i][:, :, CH * c:CH * (c + 1), :].rearrange("p u n e -> p n u e"), in_=bank[:].rearrange("p (u e) n -> p n u e", u=2), func=ACT.Tanh))
-
-        def gate(i, c0, c1, eng=None):
-            new_y(i)
-            dst = y_cols(i, c0, c1).rearrange("p (n u e) -> p n u e", u=2, e=2)
-            src = th[i][:, :, CH * c0:CH * c1, :].rearrange("p u n e -> p n u e")
-            strength = consts[:, 2:4, :].bitcast(BF16)[:, :, i - 1:i + 1].unsqueeze(1).to_broadcast([P, CH * (c1 - c0), 2, 2])
-            if eng is nc.gpsimd:
-                nc.gpsimd.tensor_tensor(out=dst, in0=src, in1=g_sb[i][:].rearrange("p (u e) -> p u e", u=2).unsqueeze(1).to_broadcast([P, CH * (c1 - c0), 2, 2]), op=ALU.mult)
-            else:
-                nc.vector.tensor_tensor(out=dst, in0=src, in1=strength, op=ALU.mult)
-
-        def quant_y(i, c0=0, c1=NCH):
-            nc.vector.quantize_mx(out=y_q[i][:, CH * c0:CH * c1].bitcast(FP8X4), scales=y_s[i][:, CH * c0:CH * c1],
-                                  in_=y_cols(i, c0, c1))
-
-        def decay_mul(b, h, eng, tag=None):
-            if b == 0:
-                dm[b, h] = sbt("dm%d_%d" % (b, h), [P, 2, R], F32, tag=tag)
-                eng.tensor_tensor(out=dm[b, h][:], in0=m_raw[b, 2 * h][:], in1=d_row[:].unsqueeze(1).to_broadcast([P, 2, R]), op=ALU.mult)
-            else:
-                cols = slice(256 * h, 256 * (h + 1))
-                dm[b, h] = sbt("dm%d_%d" % (b, h), [P, PACK, 256], F32, tag=tag)
-                eng.tensor_tensor(out=dm[b, h][:], in0=m_raw[b, h][:], in1=d_row[:, cols].unsqueeze(1).to_broadcast([P, PACK, 256]), op=ALU.mult)
-
-        def stage2_pass(out, b, a, half, cols, start, stop):
-            fi = 4 * b + 2 * half
+        def project(out, o, k, j, c0, c1):
             nc.tensor.matmul_mx(
                 out=out,
-                lhsT=y_q[fi][:, P * a:P * (a + 1)].bitcast(FP8X4), lhsT_scale=y_s[fi][:, P * a:P * (a + 1)],
-                rhs=y_q[fi + 1][:, cols].bitcast(FP8X4), rhs_scale=y_s[fi + 1][:, cols],
-                start=start, stop=stop)
+                lhsT=x_q[o, k][:, P * j:P * (j + 1)].bitcast(FP8X4), lhsT_scale=x_s[o, k][:, P * j:P * (j + 1)],
+                rhs=w_words[o][:, 2 * CH * c0:2 * CH * c1].bitcast(FP4X4), rhs_scale=w_scale[o][:, CH * c0:CH * c1],
+                start=True, stop=True)
 
-        acc = {}
+        def new_th(k):
+            if k not in th:
+                th[k] = sbt("th%d" % k, [P, 2, R, 2], F32)
+
+        def rol_wide(k, i):
+            h, u = divmod(i, 2)
+            n, bank = next_bank("MR%d%d" % (k, i), [P, 2, 2 * CH])
+            for e in range(2):
+                project(bank[:, e, :], ROL, k, 2 * u + e, 2 * h, 2 * h + 2)
+            new_th(k)
+            waiting["R%d%d" % (k, i)] = (n, lambda eng: eng.activation(out=th[k][:, u, 2 * CH * h:2 * CH * (h + 1), :], in_=bank[:].rearrange("p e n -> p n e"), func=ACT.Tanh))
+
+        def rol_narrow(k, c):
+            n, bank = next_bank("MR%d%d" % (k, c), [P, PACK, CH])
+            for j in range(PACK):
+                project(bank[:, j, :], ROL, k, j, c, c + 1)
+            new_th(k)
+            waiting["R%d%d" % (k, c)] = (n, lambda eng: eng.activation(out=th[k][:, :, CH * c:CH * (c + 1), :].rearrange("p u n e -> p n u e"),
+                                                                      in_=bank[:].rearrange("p (u e) n -> p n u e", u=2), func=ACT.Tanh))
+
+        def fil(k, c):
+            n, bank = next_bank("MF%d%d" % (k, c), [P, PACK, CH])
+            for j in range(PACK):
+                project(bank[:, j, :], FIL, k, j, c, c + 1)
+            dst = y_at(FIL, k, 0, NCH)[0].rearrange("p (a m t) -> p a m t", a=PACK, t=PACK)[:, :, 32 * c:32 * (c + 1), :]
+            waiting["F%d%d" % (k, c)] = (n, lambda eng: copy_on(eng, dst, bank[:].rearrange("p t (m a) -> p a m t", a=PACK)))
+
+        def gate(k, c0, c1, eng):
+            n = int(CH * (c1 - c0))
+            dst = y_at(ROL, k, c0, c1)[0].rearrange("p (n u e) -> p n u e", u=2, e=2)
+            src = th[k][:, :, int(CH * c0):int(CH * c1), :].rearrange("p u n e -> p n u e")
+            if eng is G:
+                strength = g_sb[k][:].rearrange("p (u e) -> p u e", u=2)
+            else:
+                strength = consts[:, 2:4, :].bitcast(BF16)[:, :, 2 * k:2 * k + 2]
+            eng.tensor_tensor(out=dst, in0=src, in1=strength.unsqueeze(1).to_broadcast([P, n, 2, 2]), op=ALU.mult)
+
+        def decay_rows(a0, a1, eng, tag=None):
+            part = sbt("dm0_%d" % a0, [P, a1 - a0, R], F32, tag=tag)
+            for a in range(a0, a1):
+                dm[0, a] = part[:, a - a0, :]
+            eng.tensor_tensor(out=part[:], in0=m_raw[0, a0 // 2][:, a0 % 2:a0 % 2 + a1 - a0, :], in1=d_row[:].unsqueeze(1).to_broadcast([P, a1 - a0, R]), op=ALU.mult)
+
+        def bind_pass(out, b, a, half, c0, c1, start, stop):
+            k = 2 * b + half
+            fil_codes, fil_scales = y_at(FIL, k, a, a + 1)[1:]
+            rol_codes, rol_scales = y_at(ROL, k, c0, c1)[1:]
+            nc.tensor.matmul_mx(out=out, lhsT=fil_codes.bitcast(FP8X4), lhsT_scale=fil_scales,
+                                rhs=rol_codes.bitcast(FP8X4), rhs_scale=rol_scales, start=start, stop=stop)
 
         def bind_rows(a):
-            acc[0, a] = next_bank("A%d" % a, [P, R])
+            held[0, a], acc[0, a] = next_bank("A%d" % a, [P, R])
             for half in range(2):
-                stage2_pass(acc[0, a][:], 0, a, half, slice(0, R), half == 0, half == 1)
+                bind_pass(acc[0, a][:], 0, a, half, 0, NCH, half == 0, half == 1)
 
         def finish_rows(a):
-            if a == 0:
+            if 0 not in res:
                 res[0] = sbt("res0", [P, PACK, R], F32)
-            nc.vector.scalar_tensor_tensor(out=res[0][:, a, :], in0=acc[0, a][:], scalar=1.0 / 32.0, in1=dm[0, a // 2][:, a % 2, :], op0=ALU.mult, op1=ALU.add)
+            nc.vector.scalar_tensor_tensor(out=res[0][:, a, :], in0=acc[0, a][:], scalar=1.0 / 32.0, in1=dm[0, a], op0=ALU.mult, op1=ALU.add)
+            free_banks.append(held[0, a])
             nc.sync.dma_start(out=out_0[0].rearrange("(p a) r -> p a r", a=PACK)[:, a, :], in_=res[0][:, a, :])
 
         def bind_cols(c, half):
             if half == 0:
-                acc[1, c] = next_bank("B%d" % c, [P, PACK, CH])
+                held[1, c], acc[1, c] = next_bank("B%d" % c, [P, PACK, CH])
             for a in range(PACK):
-                stage2_pass(acc[1, c][:, a, :], 1, a, half, slice(CH * c, CH * (c + 1)), half == 0 and a == 0, half == 1 and a == PACK - 1)
+                bind_pass(acc[1, c][:, a, :], 1, a, half, c, c + 1, half == 0 and a == 0, half == 1 and a == PACK - 1)
 
         def finish_cols(c):
             res[1, c] = sbt("res1_%d" % c, [P, PACK, CH], F32)
-            nc.vector.scalar_tensor_tensor(out=res[1, c][:], in0=acc[1, c][:], scalar=1.0 / 32.0, in1=dm[1, c // 2][:, :, CH * (c % 2):CH * (c % 2 + 1)],
+            nc.vector.scalar_tensor_tensor(out=res[1, c][:], in0=acc[1, c][:], scalar=1.0 / 32.0, in1=dm[1][:, :, CH * c:CH * (c + 1)],
                                            op0=ALU.mult, op1=ALU.add)
+            free_banks.append(held[1, c])
             nc.sync.dma_start(out=out_0[1].rearrange("(p a) r -> p a r", a=PACK)[:, :, CH * c:CH * (c + 1)], in_=res[1, c][:])
 
+        def bind_wide(h, s, half):
+            if half == 0:
+                held[1, h, s], acc[1, h, s] = next_bank("W%d%d" % (h, s), [P, 2, 2 * CH])
+            for e in range(2):
+                bind_pass(acc[1, h, s][:, e, :], 1, 2 * s + e, half, 2 * h, 2 * h + 2, half == 0 and e == 0, half == 1 and e == 1)
+
+        def finish_wide(h, s):
+            if (1, "wide", h) not in res:
+                res[1, "wide", h] = sbt("res1_w%d" % h, [P, PACK, 2 * CH], F32)
+                for c in range(2):
+                    res[1, 2 * h + c] = res[1, "wide", h][:, :, CH * c:CH * (c + 1)]
+            rows = res[1, "wide", h][:, 2 * s:2 * s + 2, :]
+            nc.vector.scalar_tensor_tensor(out=rows, in0=acc[1, h, s][:], scalar=1.0 / 32.0, in1=dm[1][:, 2 * s:2 * s + 2, 2 * CH * h:2 * CH * (h + 1)],
+                                           op0=ALU.mult, op1=ALU.add)
+            free_banks.append(held[1, h, s])
+            nc.sync.dma_start(out=out_0[1].rearrange("(p a) r -> p a r", a=PACK)[:, 2 * s:2 * s + 2, 2 * CH * h:2 * CH * (h + 1)], in_=rows)
+
         def round_out(b, c0, c1, eng):
-            if b not in res_bf:
-                res_bf[b] = sbt("rb%d" % b, [P, R * PACK], BF16, tag=RT.get(b))
-            src = res[0][:, :, CH * c0:CH * c1] if b == 0 else res[1, c0][:]
-            dst = res_bf[b][:, CH * PACK * c0:CH * PACK * c1]
-            if eng is nc.gpsimd:
-                nc.gpsimd.tensor_scalar(out=dst.rearrange("p (n a) -> p n a", a=PACK), in0=src.rearrange("p a n -> p n a"),
-                                        scalar1=1.0, scalar2=0.0, op0=ALU.mult, op1=ALU.add)
-            else:
-                copy_on(eng, dst.rearrange("p (n i a) -> p n a i", a=PACK, i=4), src.rearrange("p a (n i) -> p n a i", i=4))
+            if (b, c0 // 2) not in res_bf:
+                res_bf[b, c0 // 2] = sbt("rb%d_%d" % (b, c0 // 2), [P, 2 * CH * PACK], BF16)
+            src = res[0][:, :, CH * c0:CH * c1] if b == 0 else (res[1, c0][:] if c1 - c0 == 1 else res[1, "wide", c0 // 2][:])
+            dst = res_bf[b, c0 // 2][:, CH * PACK * (c0 % 2):CH * PACK * (c0 % 2 + c1 - c0)]
+            copy_on(eng, dst.rearrange("p (n i a) -> p n a i", a=PACK, i=4), src.rearrange("p a (n i) -> p n a i", i=4))
 
         def quant_out(b, c0, c1):
             cols = slice(R * b + CH * c0, R * b + CH * c1)
-            nc.vector.quantize_mx(out=o_q[:, cols].bitcast(FP8X4), scales=o_s[:, cols], in_=res_bf[b][:, CH * PACK * c0:CH * PACK * c1])
+            nc.vector.quantize_mx(out=o_q[:, cols].bitcast(FP8X4), scales=o_s[:, cols],
+                                  in_=res_bf[b, c0 // 2][:, CH * PACK * (c0 % 2):CH * PACK * (c0 % 2 + c1 - c0)])
 
         def store_words(c0, c1):
             dst = out_1[0].rearrange("p m t -> p (m t)").bitcast(I32)
-            nc.sync.dma_start(out=dst[:, c0:c1], in_=o_q[:].bitcast(I32)[:, c0:c1])
+            nc.sync.dma_start(out=dst[:, CH * c0:CH * c1], in_=o_q[:].bitcast(I32)[:, CH * c0:CH * c1])
 
         def store_scales():
             for q in range(4):
                 eng = nc.scalar if q % 2 else nc.sync
                 eng.dma_start(out=out_2[0].bitcast(I32)[4 * q:4 * q + 4, :], in_=o_s[:].bitcast(I32)[32 * q:32 * q + 4, :])
 
-        def spread_decay():
+        def turn_decay():
             for u in range(2):
                 nc.tensor.transpose(consts[:, u, :], d_col[:].bitcast(F32)[:, u:u + 1].to_broadcast([P, P]), ident[:])
-            nc.vector.tensor_copy(out=d_row[:].bitcast(F32).rearrange("p (m u) -> p m u", u=2), in_=consts[:, 0:2, :].rearrange("p u m -> p m u"))
+
+        def copy_decay(eng):
+            copy_on(eng, d_row[:].bitcast(F32).rearrange("p (m u) -> p m u", u=2), consts[:, 0:2, :].rearrange("p u m -> p m u"))
 
         def turn_g():
             for u in range(2):
                 nc.tensor.transpose(consts[:, 2 + u, :], g_rows[:].bitcast(F32)[:, u:2 * P:2], ident[:])
 
-        def copy_g(i, eng):
-            g_sb[i] = sbt("g_sb%d" % i, [P, PACK], BF16)
-            copy_on(eng, g_sb[i][:].bitcast(F32), consts[:, 2:4, i // 2])
+        def copy_g(k, eng):
+            g_sb[k] = sbt("g_sb%d" % k, [P, PACK], BF16)
+            copy_on(eng, g_sb[k][:].bitcast(F32), consts[:, 2:4, k])
 
-        V, S, G = nc.vector, nc.scalar, nc.gpsimd
-        load_x(1, 0)
-        nc.scalar.dma_start(out=d_col[:], in_=decay.rearrange("(p j) -> p j", j=PACK))
-        load_x(1, 1)
-        load_x(0, 0)
-        load_x(0, 1)
-        load_m(0, 0, 2)
+        def copy_g_again(k, eng):
+            g_sb[k] = sbt("g_again%d" % k, [P, PACK], BF16)
+            copy_on(eng, g_sb[k][:].bitcast(F32), consts[:, 2:4, k])
+
+        def rol(k):
+            for i in range(4):
+                rol_wide(k, i)
+
+        def load_decay(queue):
+            queue.dma_start(out=d_col[:], in_=decay.rearrange("(p j) -> p j", j=PACK))
+
+        def load_g(queue):
+            queue.dma_start(out=g_rows[0:4, :], in_=g.rearrange("b (h k) -> (b h) k", h=2))
+
+        def decay_last(s, tag=None):
+            if s == 0:
+                dm[1] = sbt("dm1", [P, PACK, R], F32, tag=tag)
+            nc.gpsimd.tensor_tensor(out=dm[1][:, 2 * s:2 * s + 2, :], in0=m_raw[1, s][:], in1=d_row[:].unsqueeze(1).to_broadcast([P, 2, R]), op=ALU.mult)
+
+
+        load_x_half(ROL, 0, 0)
+        load_decay(nc.scalar)
+        load_x_half(ROL, 0, 1)
+        load_x_half(FIL, 0, 0)
+        load_x_half(FIL, 0, 1)
+        load_m(0, 0)
         make_identity(nc, ident[:])
         nc.vector.memset(g_rows[:].bitcast(I32), 0)
         nc.vector.memset(w_scale[1][:].bitcast(I32), 0)
         nc.vector.memset(w_scale[0][:].bitcast(I32), 0)
-        nc.scalar.dma_start(out=g_rows[0:4, :], in_=g.rearrange("b (h k) -> (b h) k", h=2))
-        load_ws(1, (0,), nc.scalar)
-        load_ws(1, (1, 2, 3), nc.gpsimd)
-        load_x(3, 0)
-        load_x(3, 1)
-        load_w(1)
-        load_m(0, 2, 4)
-        load_w(0)
-        load_ws(0, range(4), nc.sync)
-        load_m_cols(0)
-        load_x(2, 0)
-        load_x(2, 1)
-        load_m_cols(1)
-        load_x(5, 0)
-        load_x(5, 1)
-        for i in (4, 7, 6):
-            load_x(i, 0)
-            load_x(i, 1)
+        load_g(nc.scalar)
+        load_ws(ROL, (0,), nc.scalar)
+        load_ws(ROL, (1, 2, 3), nc.gpsimd)
+        load_x_half(ROL, 1, 0)
+        load_x_half(ROL, 1, 1)
+        load_w(ROL, nc.sync)
+        load_m(0, 1)
+        load_w(FIL, nc.sync)
+        load_ws(FIL, range(4), nc.sync)
+        load_m(1, 0)
+        load_x_half(FIL, 1, 0)
+        load_x_half(FIL, 1, 1)
+        load_m(1, 1)
+        for o, k in ((ROL, 2), (FIL, 2), (ROL, 3), (FIL, 3)):
+            load_x(o, k)
 
-        turn_x(1, 0, V)
-        turn_x(1, 1, S)
-        quant_x(1, 0, 1)
-        spread_decay()
-        quant_x(1, 1, 2)
-        decay_mul(0, 0, V)
-        turn_x(0, 0, S)
-        turn_x(0, 1, S)
+        turn(ROL, 0)
+        take(V, "xR00")
+        take(S, "xR01")
+        quant_x(ROL, 0, 0, 1)
+        turn_decay()
         turn_g()
-        quant_x(0)
-        decay_mul(0, 1, V)
-        turn_x(3, 0, S)
-        turn_x(3, 1, S)
-        copy_g(5, S)
-        copy_g(7, S)
-        quant_x(3)
-        decay_mul(1, 0, G, "xt3")
-        decay_mul(1, 1, G)
-        stage1(1, 0, S)
-        stage1(1, 1, S)
-        stage1(0, 0, V)
-        later_first(lambda: stage1(1, 2, S), lambda: stage1(1, 3, S))
-        gate(1, 0, 2)
-        stage1(0, 1, S)
-        stage1(0, 2, V)
-        gate(1, 2, 4)
-        stage1(3, 0, S)
-        turn_x(2, 0, S)
-        turn_x(2, 1, V)
-        later_first(lambda: stage1(3, 1, S), lambda: stage1(0, 3, S))
-        turn_x(5, 0, V)
-        turn_x(5, 1, S)
-        later_first(lambda: stage1(3, 2, S), lambda: stage1(3, 3, S))
-        later_first(lambda: turn_x(4, 0, S), lambda: turn_x(4, 1, S))
-        gate(3, 0, 1)
-        quant_x(2)
+        copy_decay(V)
+        quant_x(ROL, 0, 1, 2)
+        decay_rows(0, 2, V)
+        turn(FIL, 0)
+        take(S, "xF00", "xF01")
+        quant_x(FIL, 0)
+        decay_rows(2, 4, V)
+        turn(ROL, 1)
+        take(S, "xR10", "xR11")
+        copy_g(2, S)
+        quant_x(ROL, 1)
+        decay_last(0, "m0_1")
+        decay_last(1)
+        rol_wide(0, 0)
+        rol_wide(0, 1)
+        take(S, "R00", "R01")
+        fil(0, 0)
+        take(V, "F00")
+        rol_wide(0, 2)
+        rol_wide(0, 3)
+        take(S, "R02", "R03")
+        gate(0, 0, 2, V)
+        fil(0, 1)
+        fil(0, 2)
+        take(V, "F02")
+        rol_wide(1, 0)
+        take(S, "F01", "R10")
+        gate(0, 2, 4, V)
+        newest_first(2)
+        turn(FIL, 1)
+        take(S, "xF10")
+        take(V, "xF11")
+        newest_first(2)
+        rol_wide(1, 1)
+        fil(0, 3)
+        take(S, "R11", "F03")
+        newest_first(2)
+        turn(ROL, 2)
+        take(V, "xR20")
+        take(S, "xR21")
+        newest_first(2)
+        rol_wide(1, 2)
+        rol_wide(1, 3)
+        take(S, "R12", "R13")
+        newest_first(2)
+        turn(FIL, 2)
+        take(S, "xF20", "xF21")
+        gate(1, 0, 1, V)
+        quant_x(FIL, 1)
         quant_pair(0)
-        quant_x(5)
-        copy_g(3, V)
-        gate(3, 3, 4, G)
-        gate(3, 1, 3)
-        stage1(2, 0, S)
-        stage1(2, 1, V)
-        turn_x(7, 0, S)
-        turn_x(7, 1, S)
-        stage1(2, 2, V)
-        stage1(2, 3, S)
-        turn_x(6, 0, S)
-        turn_x(6, 1, S)
-        quant_x(4)
-        quant_pair(2)
-        quant_x_pair()
-        later_first(lambda: stage1(5, 0, S), lambda: stage1(5, 1, S))
-        gate(5, 0, 2, G)
-        later_first(lambda: stage1(5, 2, S), lambda: stage1(5, 3, S))
+        copy_g(1, V)
+        quant_x(ROL, 2)
+        gate(1, 2.5, 4, G)
+        gate(1, 1, 2.5, V)
+        fil(1, 0)
+        take(S, "F10")
+        fil(1, 1)
+        take(V, "F11")
+        newest_first(2)
+        turn(ROL, 3)
+        take(S, "xR30", "xR31")
+        fil(1, 2)
+        take(V, "F12")
+        fil(1, 3)
+        take(S, "F13")
+        newest_first(2)
+        turn(FIL, 3)
+        take(S, "xF30", "xF31")
+        quant_x(FIL, 2)
+        quant_pair(1)
+        quant_x_pair(0)
+        newest_first(2)
+        rol_wide(2, 0)
+        rol_wide(2, 1)
+        take(S, "R20", "R21")
+        gate(2, 0, 2, G)
+        rol_wide(2, 2)
+        rol_wide(2, 3)
+        take(S, "R23", "R22")
         bind_rows(0)
-        later_first(lambda: stage1(4, 0, S), lambda: stage1(4, 1, S))
+        fil(2, 0)
+        fil(2, 1)
+        take(S, "F21", "F20")
         bind_rows(1)
-        later_first(lambda: stage1(4, 2, S), lambda: stage1(4, 3, S))
+        fil(2, 2)
+        fil(2, 3)
+        take(S, "F23", "F22")
         finish_rows(0)
-        gate(5, 2, 4)
+        gate(2, 2, 4, V)
         finish_rows(1)
-        stage1(7, 0, S)
+        rol_wide(3, 0)
         bind_rows(2)
-        stage1(7, 1, S)
+        rol_wide(3, 1)
+        take(S, "R31", "R30")
         finish_rows(2)
-        stage1(6, 0, S)
+        fil(3, 0)
         bind_rows(3)
-        quant_pair(4)
-        gate(7, 1, 2, G)
-        gate(7, 0, 1)
+        copy_g(3, V)
+        quant_pair(2)
+        gate(3, 1, 2, G)
+        gate(3, 0, 1, V)
         finish_rows(3)
-        stage1(6, 1, S)
-        later_first(lambda: stage1(6, 2, S), lambda: stage1(6, 3, S))
-        quant_y(7, 0, 2)
-        quant_y(6)
-        later_first(lambda: stage1(7, 2, S), lambda: stage1(7, 3, S))
-        bind_cols(0, 0)
-        bind_cols(1, 0)
-        bind_cols(2, 0)
-        bind_cols(3, 0)
+        fil(3, 1)
+        take(S, "F30", "F31")
+        fil(3, 2)
+        take(V, "F32")
+        fil(3, 3)
+        take(S, "F33")
+        quant_y(ROL, 3, 0, 2)
+        quant_y(FIL, 3)
+        rol_narrow(3, 2)
+        rol_narrow(3, 3)
+        take(S, "R32", "R33")
+        for c in range(4):
+            bind_cols(c, 0)
         bind_cols(0, 1)
         bind_cols(1, 1)
-        gate(7, 2, 3)
-        gate(7, 3, 4)
-        quant_y(7, 2, 3)
+        gate(3, 2, 3, V)
+        gate(3, 3, 4, V)
+        quant_y(ROL, 3, 2, 3)
         bind_cols(2, 1)
         finish_cols(0)
         round_out(0, 0, 2, S)
-        quant_y(7, 3, 4)
+        quant_y(ROL, 3, 3, 4)
         bind_cols(3, 1)
         finish_cols(1)
         round_out(0, 2, 4, S)
@@ -432,10 +484,10 @@ def tile_tensorproductrolefillerwrite_x2_kernel(
         round_out(1, 0, 1, S)
         round_out(1, 1, 2, S)
         quant_out(0, 2, 4)
-        store_words(CH * 0, CH * 4)
+        store_words(0, 4)
         round_out(1, 3, 4, V)
         quant_out(1, 0, 2)
         round_out(1, 2, 3, S)
         quant_out(1, 2, 4)
-        store_words(CH * 4, CH * 8)
+        store_words(4, 8)
         store_scales()

@@ -264,16 +264,15 @@ def tile_tensorproductrolefillerwrite_x2_kernel(
             nc.sync.dma_start(out=out_0[1].rearrange("(p a) r -> p a r", a=PACK)[:, 2 * s:2 * s + 2, 2 * CH * h:2 * CH * (h + 1)], in_=rows)
 
         def round_out(b, c0, c1, eng):
-            if (b, c0 // 2) not in res_bf:
-                res_bf[b, c0 // 2] = sbt("rb%d_%d" % (b, c0 // 2), [P, 2 * CH * PACK], BF16)
-            src = res[0][:, :, CH * c0:CH * c1] if b == 0 else (res[1, c0][:] if c1 - c0 == 1 else res[1, "wide", c0 // 2][:])
-            dst = res_bf[b, c0 // 2][:, CH * PACK * (c0 % 2):CH * PACK * (c0 % 2 + c1 - c0)]
+            if b not in res_bf:
+                res_bf[b] = sbt("rb%d" % b, [P, R * PACK], BF16)
+            src = res[0][:, :, CH * c0:CH * c1] if b == 0 else res[1, c0][:]
+            dst = res_bf[b][:, CH * PACK * c0:CH * PACK * c1]
             copy_on(eng, dst.rearrange("p (n i a) -> p n a i", a=PACK, i=4), src.rearrange("p a (n i) -> p n a i", i=4))
 
         def quant_out(b, c0, c1):
             cols = slice(R * b + CH * c0, R * b + CH * c1)
-            nc.vector.quantize_mx(out=o_q[:, cols].bitcast(FP8X4), scales=o_s[:, cols],
-                                  in_=res_bf[b, c0 // 2][:, CH * PACK * (c0 % 2):CH * PACK * (c0 % 2 + c1 - c0)])
+            nc.vector.quantize_mx(out=o_q[:, cols].bitcast(FP8X4), scales=o_s[:, cols], in_=res_bf[b][:, CH * PACK * c0:CH * PACK * c1])
 
         def store_words(c0, c1):
             dst = out_1[0].rearrange("p m t -> p (m t)").bitcast(I32)
@@ -369,10 +368,12 @@ def tile_tensorproductrolefillerwrite_x2_kernel(
         take(S, "R00", "R01")
         fil(0, 0)
         take(V, "F00")
+        newest_first(2)
         rol_wide(0, 2)
         rol_wide(0, 3)
         take(S, "R02", "R03")
         gate(0, 0, 2, V)
+        newest_first(2)
         fil(0, 1)
         fil(0, 2)
         take(V, "F02")
@@ -386,11 +387,11 @@ def tile_tensorproductrolefillerwrite_x2_kernel(
         newest_first(2)
         rol_wide(1, 1)
         fil(0, 3)
-        take(S, "R11", "F03")
+        take(S, "R11")
+        take(V, "F03")
         newest_first(2)
         turn(ROL, 2)
-        take(V, "xR20")
-        take(S, "xR21")
+        take(S, "xR20", "xR21")
         newest_first(2)
         rol_wide(1, 2)
         rol_wide(1, 3)
@@ -405,6 +406,7 @@ def tile_tensorproductrolefillerwrite_x2_kernel(
         quant_x(ROL, 2)
         gate(1, 2.5, 4, G)
         gate(1, 1, 2.5, V)
+        newest_first(2)
         fil(1, 0)
         take(S, "F10")
         fil(1, 1)
@@ -412,6 +414,7 @@ def tile_tensorproductrolefillerwrite_x2_kernel(
         newest_first(2)
         turn(ROL, 3)
         take(S, "xR30", "xR31")
+        newest_first(2)
         fil(1, 2)
         take(V, "F12")
         fil(1, 3)
@@ -427,6 +430,7 @@ def tile_tensorproductrolefillerwrite_x2_kernel(
         rol_wide(2, 1)
         take(S, "R20", "R21")
         gate(2, 0, 2, G)
+        newest_first(2)
         rol_wide(2, 2)
         rol_wide(2, 3)
         take(S, "R23", "R22")
@@ -468,26 +472,23 @@ def tile_tensorproductrolefillerwrite_x2_kernel(
             bind_cols(c, 0)
         bind_cols(0, 1)
         bind_cols(1, 1)
-        gate(3, 2, 3, V)
-        gate(3, 3, 4, V)
-        quant_y(ROL, 3, 2, 3)
-        bind_cols(2, 1)
+        gate(3, 2, 4, V)
         finish_cols(0)
-        round_out(0, 0, 2, S)
-        quant_y(ROL, 3, 3, 4)
+        round_out(0, 0, 4, S)
+        quant_y(ROL, 3, 2, 4)
+        bind_cols(2, 1)
         bind_cols(3, 1)
         finish_cols(1)
-        round_out(0, 2, 4, S)
-        finish_cols(2)
-        quant_out(0, 0, 2)
-        finish_cols(3)
         round_out(1, 0, 1, S)
         round_out(1, 1, 2, S)
-        quant_out(0, 2, 4)
+        quant_out(0, 0, 4)
         store_words(0, 4)
-        round_out(1, 3, 4, V)
-        quant_out(1, 0, 2)
+        finish_cols(2)
         round_out(1, 2, 3, S)
-        quant_out(1, 2, 4)
+        finish_cols(3)
+        quant_out(1, 0, 2)
+        round_out(1, 3, 4, V)
+        quant_out(1, 2, 3)
+        quant_out(1, 3, 4)
         store_words(4, 8)
         store_scales()

@@ -360,6 +360,7 @@ def tile_tensorproductrolefillerwrite_x2_kernel(
         turn(ROL, 1)
         take(S, "xR10", "xR11")
         copy_g(2, S)
+        copy_g(3, S)
         quant_x(ROL, 1)
         decay_last(0, "m0_1")
         decay_last(1)
@@ -399,13 +400,12 @@ def tile_tensorproductrolefillerwrite_x2_kernel(
         newest_first(2)
         turn(FIL, 2)
         take(S, "xF20", "xF21")
-        gate(1, 0, 1, V)
         quant_x(FIL, 1)
         quant_pair(0)
         copy_g(1, V)
         quant_x(ROL, 2)
-        gate(1, 2.5, 4, G)
-        gate(1, 1, 2.5, V)
+        gate(1, 2, 4, G)
+        gate(1, 0, 2, V)
         newest_first(2)
         fil(1, 0)
         take(S, "F10")
@@ -452,10 +452,9 @@ def tile_tensorproductrolefillerwrite_x2_kernel(
         finish_rows(2)
         fil(3, 0)
         bind_rows(3)
-        copy_g(3, V)
         quant_pair(2)
-        gate(3, 1, 2, G)
-        gate(3, 0, 1, V)
+        gate(3, 0.75, 2, G)
+        gate(3, 0, 0.75, V)
         finish_rows(3)
         fil(3, 1)
         take(S, "F30", "F31")

@@ -23,8 +23,6 @@ CH = 128
 NCH = 4
 BANKS = 7
 FIL, ROL = 0, 1
-Y_TAGS = {"2": "y1"}
-X_PAIRS = (((ROL, 3), (FIL, 3)),)
 
 
 def tile_tensorproductrolefillerwrite_x2_kernel(
@@ -60,12 +58,12 @@ def tile_tensorproductrolefillerwrite_x2_kernel(
         def label(o, k):
             return "%s%d" % ("FR"[o], k)
 
-        x_raw, x_t, x_q, x_s, y_bf, y_q, y_s, th = {}, {}, {}, {}, {}, {}, {}, {}
-        m_raw, dm, res, res_bf, y_pair, g_sb, acc, x_pair = {}, {}, {}, {}, {}, {}, {}, {}
+        x_raw, x_t, x_q, x_s, y, th = {}, {}, {}, {}, {}, {}
+        m_raw, dm, res, res_bf, g_sb, acc = {}, {}, {}, {}, {}, {}
 
         ident = sbt("ident", [P, P], F32)
         w_words = [sbt("ww%d" % o, [P, 2 * F], U8) for o in range(2)]
-        w_scale = [sbt("ws%d" % o, [P, F], U8) for o in range(2)]
+        w_scale = [sbt("ws%d" % o, [P, 4 * F], U8) for o in range(2)]
         g_rows = sbt("g_rows", [P, KP], BF16)
         d_col = sbt("d_col", [P, PACK], BF16)
         d_row = sbt("d_row", [P, R], BF16)
@@ -96,19 +94,44 @@ def tile_tensorproductrolefillerwrite_x2_kernel(
         def load_w(o, queue):
             queue.dma_start(out=w_words[o][:].bitcast(I32), in_=(wf_words, wr_words)[o][0].bitcast(I32))
 
-        def load_ws(o, quadrants, queue):
-            src = (wf_scales, wr_scales)[o][0].bitcast(I32)
-            for q in quadrants:
-                queue.dma_start(out=w_scale[o][:].bitcast(I32)[32 * q:32 * q + 4, :], in_=src[4 * q:4 * q + 4, :])
+        def load_ws(o, queue):
+            src = (wf_scales, wr_scales)[o][0].bitcast(I32).rearrange("(q r) w -> r q w", r=4)
+            queue.dma_start(out=w_scale[o][:].bitcast(I32)[0:4, :].rearrange("r (q w) -> r q w", q=4), in_=src)
+
+        def spread_ws(o):
+            words = w_scale[o][:].bitcast(I32)
+            for q in range(1, 4):
+                nc.vector.tensor_copy(out=words[32 * q:32 * q + 4, 0:F // 4], in_=words[0:4, q * F // 4:(q + 1) * F // 4])
 
         def load_m(b, h):
             m_raw[b, h] = sbt("m%d_%d" % (b, h), [P, 2, R], BF16)
             nc.sync.dma_start(out=m_raw[b, h][:], in_=m0[b].rearrange("(p j) r -> p j r", j=PACK)[:, 2 * h:2 * h + 2, :])
 
-        def load_m_whole(b):
-            whole = sbt("m%d" % b, [P, PACK, R], BF16)
-            nc.sync.dma_start(out=whole[:], in_=m0[b].rearrange("(p j) r -> p j r", j=PACK))
-            m_raw[b] = whole
+        def load_decay(queue):
+            queue.dma_start(out=d_col[:], in_=decay.rearrange("(p j) -> p j", j=PACK))
+
+        def load_g(queue):
+            queue.dma_start(out=g_rows[0:4, :], in_=g.rearrange("b (h k) -> (b h) k", h=2))
+
+        def turn_decay():
+            for u in range(2):
+                nc.tensor.transpose(consts[:, u, :], d_col[:].bitcast(F32)[:, u:u + 1].to_broadcast([P, P]), ident[:])
+
+        def turn_g():
+            for u in range(2):
+                nc.tensor.transpose(consts[:, 2 + u, :], g_rows[:].bitcast(F32)[:, u:2 * P:2], ident[:])
+
+        def copy_decay(eng):
+            copy_on(eng, d_row[:].bitcast(F32).rearrange("p (m u) -> p m u", u=2), consts[:, 0:2, :].rearrange("p u m -> p m u"))
+
+        def copy_g(k, eng, name="g_sb"):
+            g_sb[k] = sbt("%s%d" % (name, k), [P, PACK], BF16)
+            copy_on(eng, g_sb[k][:].bitcast(F32), consts[:, 2:4, k])
+
+        def x_tile(name, groups, tag=None):
+            tile = sbt("xt" + name, [P, len(groups) * KP * PACK], BF16, tag=tag)
+            for s, group in enumerate(groups):
+                x_t[group] = (tile, s)
 
         def turn_half(o, k, h):
             n, bank = next_bank("T%s%d" % (label(o, k), h), [P, 2, 2, P])
@@ -116,14 +139,10 @@ def tile_tensorproductrolefillerwrite_x2_kernel(
             for j in range(2):
                 for u in range(2):
                     nc.tensor.transpose(bank[:, j, u, :], words[:, 256 * j + u:256 * (j + 1):2], ident[:])
-            for m, pair in enumerate(X_PAIRS):
-                if (o, k) in pair and m not in x_pair:
-                    x_pair[m] = sbt("xtp%d" % m, [P, 2 * KP * PACK], BF16)
-                    for s in range(2):
-                        x_t[pair[s]] = x_pair[m][:, KP * PACK * s:KP * PACK * (s + 1)]
             if (o, k) not in x_t:
-                x_t[o, k] = sbt("xt" + label(o, k), [P, KP * PACK], BF16)
-            dst = x_t[o, k][:].bitcast(F32)[:, 512 * h:512 * (h + 1)].rearrange("p (j m u) -> p j m u", j=2, u=2)
+                x_tile(label(o, k), [(o, k)])
+            tile, s = x_t[o, k]
+            dst = tile[:].bitcast(F32)[:, 1024 * s + 512 * h:1024 * s + 512 * (h + 1)].rearrange("p (j m u) -> p j m u", j=2, u=2)
             waiting["x%s%d" % (label(o, k), h)] = (n, lambda eng: copy_on(eng, dst, bank[:].rearrange("p j u m -> p j m u")))
 
         def turn(o, k):
@@ -134,27 +153,26 @@ def tile_tensorproductrolefillerwrite_x2_kernel(
             if h0 == 0:
                 x_q[o, k] = sbt("xq" + label(o, k), [P, KP], U32)
                 x_s[o, k] = sbt("xs" + label(o, k), [P, KP], U8)
+            tile, s = x_t[o, k]
             cols = slice(256 * h0, 256 * h1)
-            nc.vector.quantize_mx(out=x_q[o, k][:, cols].bitcast(FP8X4), scales=x_s[o, k][:, cols], in_=x_t[o, k][:, 1024 * h0:1024 * h1])
+            nc.vector.quantize_mx(out=x_q[o, k][:, cols].bitcast(FP8X4), scales=x_s[o, k][:, cols], in_=tile[:, 2048 * s + 1024 * h0:2048 * s + 1024 * h1])
 
-        def quant_x_pair(n):
-            codes = sbt("xqp%d" % n, [P, 2 * KP], U32)
-            scales = sbt("xsp%d" % n, [P, 2 * KP], U8)
-            nc.vector.quantize_mx(out=codes[:].bitcast(FP8X4), scales=scales[:], in_=x_pair[n][:])
-            for s in range(2):
-                x_q[X_PAIRS[n][s]] = codes[:, KP * s:KP * (s + 1)]
-                x_s[X_PAIRS[n][s]] = scales[:, KP * s:KP * (s + 1)]
+        def quant_x_pair(first, second):
+            codes = sbt("xq" + label(*first) + label(*second), [P, 2 * KP], U32)
+            scales = sbt("xs" + label(*first) + label(*second), [P, 2 * KP], U8)
+            nc.vector.quantize_mx(out=codes[:].bitcast(FP8X4), scales=scales[:], in_=x_t[first][0][:])
+            for s, group in enumerate((first, second)):
+                x_q[group] = codes[:, KP * s:KP * (s + 1)]
+                x_s[group] = scales[:, KP * s:KP * (s + 1)]
 
-        def y_tiles(name, groups):
-            width = F * groups
-            y_pair[name] = (sbt("y" + name, [P, width * PACK], BF16, tag=Y_TAGS.get(name)), sbt("yq" + name, [P, width], U32), sbt("ys" + name, [P, width], U8))
+        def y_tiles(k, tag=None):
+            y[k] = (sbt("y%d" % k, [P, 2 * F * PACK], BF16, tag=tag), sbt("yq%d" % k, [P, 2 * F], U32), sbt("ys%d" % k, [P, 2 * F], U8))
 
         def y_at(o, k, c0, c1):
-            name, col = str(k), F * o + int(CH * c0)
-            if name not in y_pair:
-                y_tiles(name, 2)
-            values, codes, scales = y_pair[name]
-            n = int(CH * (c1 - c0))
+            if k not in y:
+                y_tiles(k)
+            col, n = F * o + int(CH * c0), int(CH * (c1 - c0))
+            values, codes, scales = y[k]
             return values[:, PACK * col:PACK * (col + n)], codes[:, col:col + n], scales[:, col:col + n]
 
         def quant_y(o, k, c0=0, c1=NCH):
@@ -171,23 +189,28 @@ def tile_tensorproductrolefillerwrite_x2_kernel(
                 rhs=w_words[o][:, 2 * CH * c0:2 * CH * c1].bitcast(FP4X4), rhs_scale=w_scale[o][:, CH * c0:CH * c1],
                 start=True, stop=True)
 
-        def new_th(k):
-            if k not in th:
-                th[k] = sbt("th%d" % k, [P, 2, R, 2], F32)
+        def new_th(k, tag=None):
+            th[k] = sbt("th%d" % k, [P, 2, R, 2], F32, tag=tag)
 
-        def rol_wide(k, i):
-            h, u = divmod(i, 2)
-            n, bank = next_bank("MR%d%d" % (k, i), [P, 2, 2 * CH])
+        def rol_wide(k, h, u):
+            n, bank = next_bank("MR%d%d%d" % (k, h, u), [P, 2, 2 * CH])
             for e in range(2):
                 project(bank[:, e, :], ROL, k, 2 * u + e, 2 * h, 2 * h + 2)
-            new_th(k)
-            waiting["R%d%d" % (k, i)] = (n, lambda eng: eng.activation(out=th[k][:, u, 2 * CH * h:2 * CH * (h + 1), :], in_=bank[:].rearrange("p e n -> p n e"), func=ACT.Tanh))
+            if k not in th:
+                new_th(k)
+            waiting["R%d%d%d" % (k, h, u)] = (n, lambda eng: eng.activation(out=th[k][:, u, 2 * CH * h:2 * CH * (h + 1), :], in_=bank[:].rearrange("p e n -> p n e"), func=ACT.Tanh))
+
+        def rol(k, halves=(0, 1)):
+            for h in halves:
+                for u in range(2):
+                    rol_wide(k, h, u)
 
         def rol_narrow(k, c):
             n, bank = next_bank("MR%d%d" % (k, c), [P, PACK, CH])
             for j in range(PACK):
                 project(bank[:, j, :], ROL, k, j, c, c + 1)
-            new_th(k)
+            if k not in th:
+                new_th(k)
             waiting["R%d%d" % (k, c)] = (n, lambda eng: eng.activation(out=th[k][:, :, CH * c:CH * (c + 1), :].rearrange("p u n e -> p n u e"),
                                                                       in_=bank[:].rearrange("p (u e) n -> p n u e", u=2), func=ACT.Tanh))
 
@@ -208,11 +231,20 @@ def tile_tensorproductrolefillerwrite_x2_kernel(
                 strength = consts[:, 2:4, :].bitcast(BF16)[:, :, 2 * k:2 * k + 2]
             eng.tensor_tensor(out=dst, in0=src, in1=strength.unsqueeze(1).to_broadcast([P, n, 2, 2]), op=ALU.mult)
 
-        def decay_rows(a0, a1, eng, tag=None):
-            part = sbt("dm0_%d" % a0, [P, a1 - a0, R], F32, tag=tag)
+        def decay_rows(b, a0, a1, eng, tag=None):
+            part = sbt("dm%d_%d" % (b, a0), [P, a1 - a0, R], F32, tag=tag)
+            dm[b, "pair", a0 // 2] = part
             for a in range(a0, a1):
-                dm[0, a] = part[:, a - a0, :]
-            eng.tensor_tensor(out=part[:], in0=m_raw[0, a0 // 2][:, a0 % 2:a0 % 2 + a1 - a0, :], in1=d_row[:].unsqueeze(1).to_broadcast([P, a1 - a0, R]), op=ALU.mult)
+                dm[b, a] = part[:, a - a0, :]
+            rows = m_raw[b, a0 // 2][:, a0 % 2:a0 % 2 + a1 - a0, :]
+            eng.tensor_tensor(out=part[:], in0=rows, in1=d_row[:].unsqueeze(1).to_broadcast([P, a1 - a0, R]), op=ALU.mult)
+
+        def decay_row_psum(a):
+            if 1 not in dm:
+                dm[1] = sbt("dm1", [P, PACK, R], F32)
+            row = m_raw[1, a // 2][:, a % 2, :]
+            factor = consts[:, 0:2, :].bitcast(BF16).rearrange("p u (m e) -> p m u e", e=2)
+            nc.vector.tensor_tensor(out=dm[1][:, a, :].rearrange("p (m u e) -> p m u e", u=2, e=2), in0=row.rearrange("p (m u e) -> p m u e", u=2, e=2), in1=factor, op=ALU.mult)
 
         def bind_pass(out, b, a, half, c0, c1, start, stop):
             k = 2 * b + half
@@ -233,6 +265,20 @@ def tile_tensorproductrolefillerwrite_x2_kernel(
             free_banks.append(held[0, a])
             nc.sync.dma_start(out=out_0[0].rearrange("(p a) r -> p a r", a=PACK)[:, a, :], in_=res[0][:, a, :])
 
+        def bind_wide(h, s):
+            held[0, h, s], acc[0, h, s] = next_bank("A%d%d" % (h, s), [P, 2, 2 * CH])
+            for e in range(2):
+                for half in range(2):
+                    bind_pass(acc[0, h, s][:, e, :], 0, 2 * s + e, half, 2 * h, 2 * h + 2, half == 0, half == 1)
+
+        def finish_wide(h, s):
+            if 0 not in res:
+                res[0] = sbt("res0", [P, PACK, R], F32)
+            rows, cols = slice(2 * s, 2 * s + 2), slice(2 * CH * h, 2 * CH * (h + 1))
+            nc.vector.scalar_tensor_tensor(out=res[0][:, rows, cols], in0=acc[0, h, s][:], scalar=1.0 / 32.0, in1=dm[0, "pair", s][:, :, cols], op0=ALU.mult, op1=ALU.add)
+            free_banks.append(held[0, h, s])
+            nc.sync.dma_start(out=out_0[0].rearrange("(p a) r -> p a r", a=PACK)[:, rows, cols], in_=res[0][:, rows, cols])
+
         def bind_cols(c, half):
             if half == 0:
                 held[1, c], acc[1, c] = next_bank("B%d" % c, [P, PACK, CH])
@@ -246,29 +292,21 @@ def tile_tensorproductrolefillerwrite_x2_kernel(
             free_banks.append(held[1, c])
             nc.sync.dma_start(out=out_0[1].rearrange("(p a) r -> p a r", a=PACK)[:, :, CH * c:CH * (c + 1)], in_=res[1, c][:])
 
-        def bind_wide(h, s, half):
-            if half == 0:
-                held[1, h, s], acc[1, h, s] = next_bank("W%d%d" % (h, s), [P, 2, 2 * CH])
-            for e in range(2):
-                bind_pass(acc[1, h, s][:, e, :], 1, 2 * s + e, half, 2 * h, 2 * h + 2, half == 0 and e == 0, half == 1 and e == 1)
-
-        def finish_wide(h, s):
-            if (1, "wide", h) not in res:
-                res[1, "wide", h] = sbt("res1_w%d" % h, [P, PACK, 2 * CH], F32)
-                for c in range(2):
-                    res[1, 2 * h + c] = res[1, "wide", h][:, :, CH * c:CH * (c + 1)]
-            rows = res[1, "wide", h][:, 2 * s:2 * s + 2, :]
-            nc.vector.scalar_tensor_tensor(out=rows, in0=acc[1, h, s][:], scalar=1.0 / 32.0, in1=dm[1][:, 2 * s:2 * s + 2, 2 * CH * h:2 * CH * (h + 1)],
-                                           op0=ALU.mult, op1=ALU.add)
-            free_banks.append(held[1, h, s])
-            nc.sync.dma_start(out=out_0[1].rearrange("(p a) r -> p a r", a=PACK)[:, 2 * s:2 * s + 2, 2 * CH * h:2 * CH * (h + 1)], in_=rows)
+        def decay_last(s, tag=None):
+            if s == 0:
+                dm[1] = sbt("dm1", [P, PACK, R], F32, tag=tag)
+            nc.gpsimd.tensor_tensor(out=dm[1][:, 2 * s:2 * s + 2, :], in0=m_raw[1, s][:], in1=d_row[:].unsqueeze(1).to_broadcast([P, 2, R]), op=ALU.mult)
 
         def round_out(b, c0, c1, eng):
             if b not in res_bf:
                 res_bf[b] = sbt("rb%d" % b, [P, R * PACK], BF16)
             src = res[0][:, :, CH * c0:CH * c1] if b == 0 else res[1, c0][:]
             dst = res_bf[b][:, CH * PACK * c0:CH * PACK * c1]
-            copy_on(eng, dst.rearrange("p (n i a) -> p n a i", a=PACK, i=4), src.rearrange("p a (n i) -> p n a i", i=4))
+            dst, src = dst.rearrange("p (n i a) -> p n a i", a=PACK, i=4), src.rearrange("p a (n i) -> p n a i", i=4)
+            if eng is G:
+                nc.gpsimd.tensor_scalar(out=dst, in0=src, scalar1=1.0, scalar2=0.0, op0=ALU.mult, op1=ALU.add)
+            else:
+                copy_on(eng, dst, src)
 
         def quant_out(b, c0, c1):
             cols = slice(R * b + CH * c0, R * b + CH * c1)
@@ -283,60 +321,22 @@ def tile_tensorproductrolefillerwrite_x2_kernel(
                 eng = nc.scalar if q % 2 else nc.sync
                 eng.dma_start(out=out_2[0].bitcast(I32)[4 * q:4 * q + 4, :], in_=o_s[:].bitcast(I32)[32 * q:32 * q + 4, :])
 
-        def turn_decay():
-            for u in range(2):
-                nc.tensor.transpose(consts[:, u, :], d_col[:].bitcast(F32)[:, u:u + 1].to_broadcast([P, P]), ident[:])
-
-        def copy_decay(eng):
-            copy_on(eng, d_row[:].bitcast(F32).rearrange("p (m u) -> p m u", u=2), consts[:, 0:2, :].rearrange("p u m -> p m u"))
-
-        def turn_g():
-            for u in range(2):
-                nc.tensor.transpose(consts[:, 2 + u, :], g_rows[:].bitcast(F32)[:, u:2 * P:2], ident[:])
-
-        def copy_g(k, eng):
-            g_sb[k] = sbt("g_sb%d" % k, [P, PACK], BF16)
-            copy_on(eng, g_sb[k][:].bitcast(F32), consts[:, 2:4, k])
-
-        def copy_g_again(k, eng):
-            g_sb[k] = sbt("g_again%d" % k, [P, PACK], BF16)
-            copy_on(eng, g_sb[k][:].bitcast(F32), consts[:, 2:4, k])
-
-        def rol(k):
-            for i in range(4):
-                rol_wide(k, i)
-
-        def load_decay(queue):
-            queue.dma_start(out=d_col[:], in_=decay.rearrange("(p j) -> p j", j=PACK))
-
-        def load_g(queue):
-            queue.dma_start(out=g_rows[0:4, :], in_=g.rearrange("b (h k) -> (b h) k", h=2))
-
-        def decay_last(s, tag=None):
-            if s == 0:
-                dm[1] = sbt("dm1", [P, PACK, R], F32, tag=tag)
-            nc.gpsimd.tensor_tensor(out=dm[1][:, 2 * s:2 * s + 2, :], in0=m_raw[1, s][:], in1=d_row[:].unsqueeze(1).to_broadcast([P, 2, R]), op=ALU.mult)
-
-
-        load_x_half(ROL, 0, 0)
         load_decay(nc.scalar)
+        load_ws(ROL, nc.scalar)
+        load_ws(FIL, nc.scalar)
+        load_x_half(ROL, 0, 0)
+        nc.vector.memset(g_rows[:].bitcast(I32), 0)
+        load_g(nc.sync)
         load_x_half(ROL, 0, 1)
         load_x_half(FIL, 0, 0)
         load_x_half(FIL, 0, 1)
         load_m(0, 0)
         make_identity(nc, ident[:])
-        nc.vector.memset(g_rows[:].bitcast(I32), 0)
-        nc.vector.memset(w_scale[1][:].bitcast(I32), 0)
-        nc.vector.memset(w_scale[0][:].bitcast(I32), 0)
-        load_g(nc.scalar)
-        load_ws(ROL, (0,), nc.scalar)
-        load_ws(ROL, (1, 2, 3), nc.gpsimd)
         load_x_half(ROL, 1, 0)
         load_x_half(ROL, 1, 1)
         load_w(ROL, nc.sync)
         load_m(0, 1)
         load_w(FIL, nc.sync)
-        load_ws(FIL, range(4), nc.sync)
         load_m(1, 0)
         load_x_half(FIL, 1, 0)
         load_x_half(FIL, 1, 1)
@@ -344,74 +344,76 @@ def tile_tensorproductrolefillerwrite_x2_kernel(
         for o, k in ((ROL, 2), (FIL, 2), (ROL, 3), (FIL, 3)):
             load_x(o, k)
 
-        turn(ROL, 0)
-        take(V, "xR00")
-        take(S, "xR01")
-        quant_x(ROL, 0, 0, 1)
         turn_decay()
-        turn_g()
+        turn(ROL, 0)
         copy_decay(V)
+        spread_ws(ROL)
+        spread_ws(FIL)
+        take(S, "xR00", "xR01")
+        quant_x(ROL, 0, 0, 1)
+        turn_g()
         quant_x(ROL, 0, 1, 2)
-        decay_rows(0, 2, V)
+        decay_rows(0, 0, 2, V)
         turn(FIL, 0)
         take(S, "xF00", "xF01")
         quant_x(FIL, 0)
-        decay_rows(2, 4, V)
+        decay_rows(0, 2, 4, V)
         turn(ROL, 1)
         take(S, "xR10", "xR11")
         copy_g(2, S)
-        copy_g(3, S)
         quant_x(ROL, 1)
         decay_last(0, "m0_1")
         decay_last(1)
-        rol_wide(0, 0)
-        rol_wide(0, 1)
-        take(S, "R00", "R01")
+        rol_wide(0, 0, 0)
+        rol_wide(0, 0, 1)
+        take(S, "R000", "R001")
         fil(0, 0)
         take(V, "F00")
         newest_first(2)
-        rol_wide(0, 2)
-        rol_wide(0, 3)
-        take(S, "R02", "R03")
+        rol_wide(0, 1, 0)
+        rol_wide(0, 1, 1)
+        take(S, "R010", "R011")
         gate(0, 0, 2, V)
         newest_first(2)
         fil(0, 1)
         fil(0, 2)
         take(V, "F02")
-        rol_wide(1, 0)
-        take(S, "F01", "R10")
+        rol_wide(1, 0, 0)
+        take(S, "F01", "R100")
         gate(0, 2, 4, V)
         newest_first(2)
         turn(FIL, 1)
         take(S, "xF10")
         take(V, "xF11")
         newest_first(2)
-        rol_wide(1, 1)
+        rol_wide(1, 0, 1)
         fil(0, 3)
-        take(S, "R11")
+        take(S, "R101")
         take(V, "F03")
         newest_first(2)
         turn(ROL, 2)
         take(S, "xR20", "xR21")
         newest_first(2)
-        rol_wide(1, 2)
-        rol_wide(1, 3)
-        take(S, "R12", "R13")
+        rol_wide(1, 1, 0)
+        rol_wide(1, 1, 1)
+        take(S, "R110", "R111")
         newest_first(2)
         turn(FIL, 2)
         take(S, "xF20", "xF21")
+        gate(1, 0, 1, V)
         quant_x(FIL, 1)
         quant_pair(0)
         copy_g(1, V)
         quant_x(ROL, 2)
-        gate(1, 2, 4, G)
-        gate(1, 0, 2, V)
+        gate(1, 2.5, 4, G)
+        gate(1, 1, 2.5, V)
         newest_first(2)
         fil(1, 0)
         take(S, "F10")
         fil(1, 1)
         take(V, "F11")
         newest_first(2)
+        x_tile("p3", [(ROL, 3), (FIL, 3)])
         turn(ROL, 3)
         take(S, "xR30", "xR31")
         newest_first(2)
@@ -424,46 +426,49 @@ def tile_tensorproductrolefillerwrite_x2_kernel(
         take(S, "xF30", "xF31")
         quant_x(FIL, 2)
         quant_pair(1)
-        quant_x_pair(0)
+        quant_x_pair((ROL, 3), (FIL, 3))
+        y_tiles(2, "y1")
         newest_first(2)
-        rol_wide(2, 0)
-        rol_wide(2, 1)
-        take(S, "R20", "R21")
+        rol_wide(2, 0, 0)
+        rol_wide(2, 0, 1)
+        take(S, "R200", "R201")
         gate(2, 0, 2, G)
         newest_first(2)
-        rol_wide(2, 2)
-        rol_wide(2, 3)
-        take(S, "R23", "R22")
-        bind_rows(0)
+        rol_wide(2, 1, 0)
+        rol_wide(2, 1, 1)
+        take(S, "R211", "R210")
+        bind_wide(0, 0)
         fil(2, 0)
         fil(2, 1)
         take(S, "F21", "F20")
-        bind_rows(1)
+        bind_wide(0, 1)
         fil(2, 2)
         fil(2, 3)
         take(S, "F23", "F22")
-        finish_rows(0)
+        finish_wide(0, 0)
         gate(2, 2, 4, V)
-        finish_rows(1)
-        rol_wide(3, 0)
-        bind_rows(2)
-        rol_wide(3, 1)
-        take(S, "R31", "R30")
-        finish_rows(2)
+        finish_wide(0, 1)
+        rol_wide(3, 0, 0)
+        bind_wide(1, 0)
+        rol_wide(3, 0, 1)
+        take(S, "R301", "R300")
+        finish_wide(1, 0)
         fil(3, 0)
-        bind_rows(3)
+        bind_wide(1, 1)
+        copy_g(3, V)
         quant_pair(2)
-        gate(3, 0.75, 2, G)
-        gate(3, 0, 0.75, V)
-        finish_rows(3)
+        gate(3, 1, 2, G)
+        gate(3, 0, 1, V)
         fil(3, 1)
         take(S, "F30", "F31")
         fil(3, 2)
-        take(V, "F32")
+        take(S, "F32")
         fil(3, 3)
-        take(S, "F33")
-        quant_y(ROL, 3, 0, 2)
+        take(V, "F33")
         quant_y(FIL, 3)
+        copy_g(3, V, "g_last")
+        quant_y(ROL, 3, 0, 2)
+        finish_wide(1, 1)
         rol_narrow(3, 2)
         rol_narrow(3, 3)
         take(S, "R32", "R33")
@@ -471,9 +476,11 @@ def tile_tensorproductrolefillerwrite_x2_kernel(
             bind_cols(c, 0)
         bind_cols(0, 1)
         bind_cols(1, 1)
-        gate(3, 2, 4, V)
+        gate(3, 2, 3, G)
+        gate(3, 3, 4, V)
         finish_cols(0)
-        round_out(0, 0, 4, S)
+        round_out(0, 0, 2, S)
+        round_out(0, 2, 4, S)
         quant_y(ROL, 3, 2, 4)
         bind_cols(2, 1)
         bind_cols(3, 1)

@@ -39,6 +39,7 @@ def tile_tensorproductrolefillerwrite_x2_kernel(
             return sb.tile(shape, dtype, name=name, tag=tag or name, align_bytes=64)
 
         free_banks = list(range(BANKS))
+        freed_by = {}
         waiting = {}
         held = {}
 
@@ -46,14 +47,19 @@ def tile_tensorproductrolefillerwrite_x2_kernel(
             n = free_banks.pop(0)
             return n, ps.tile(shape, F32, name=name, tag="bank%d" % n)
 
-        def newest_first(count):
-            free_banks[:count] = reversed(free_banks[:count])
+        def newest_first(count, eng=None):
+            picked = [n for n in free_banks if eng is None or freed_by.get(n) is eng][:count]
+            free_banks[:] = picked[::-1] + [n for n in free_banks if n not in picked]
+
+        def release(n, eng):
+            freed_by[n] = eng
+            free_banks.append(n)
 
         def take(eng, *keys):
             for key in keys:
                 n, empty = waiting.pop(key)
                 empty(eng)
-                free_banks.append(n)
+                release(n, eng)
 
         def label(o, k):
             return "%s%d" % ("FR"[o], k)
@@ -240,11 +246,12 @@ def tile_tensorproductrolefillerwrite_x2_kernel(
             eng.tensor_tensor(out=part[:], in0=rows, in1=d_row[:].unsqueeze(1).to_broadcast([P, a1 - a0, R]), op=ALU.mult)
 
         def decay_row_psum(a):
-            if 1 not in dm:
-                dm[1] = sbt("dm1", [P, PACK, R], F32)
-            row = m_raw[1, a // 2][:, a % 2, :]
+            if a % 2 == 0:
+                dm[0, "pair", a // 2] = sbt("dm0_%d" % a, [P, 2, R], F32)
+            row = m_raw[0, a // 2][:, a % 2, :]
             factor = consts[:, 0:2, :].bitcast(BF16).rearrange("p u (m e) -> p m u e", e=2)
-            nc.vector.tensor_tensor(out=dm[1][:, a, :].rearrange("p (m u e) -> p m u e", u=2, e=2), in0=row.rearrange("p (m u e) -> p m u e", u=2, e=2), in1=factor, op=ALU.mult)
+            nc.vector.tensor_tensor(out=dm[0, "pair", a // 2][:, a % 2, :].rearrange("p (m u e) -> p m u e", u=2, e=2),
+                                    in0=row.rearrange("p (m u e) -> p m u e", u=2, e=2), in1=factor, op=ALU.mult)
 
         def bind_pass(out, b, a, half, c0, c1, start, stop):
             k = 2 * b + half
@@ -262,7 +269,7 @@ def tile_tensorproductrolefillerwrite_x2_kernel(
             if 0 not in res:
                 res[0] = sbt("res0", [P, PACK, R], F32)
             nc.vector.scalar_tensor_tensor(out=res[0][:, a, :], in0=acc[0, a][:], scalar=1.0 / 32.0, in1=dm[0, a], op0=ALU.mult, op1=ALU.add)
-            free_banks.append(held[0, a])
+            release(held[0, a], V)
             nc.sync.dma_start(out=out_0[0].rearrange("(p a) r -> p a r", a=PACK)[:, a, :], in_=res[0][:, a, :])
 
         def bind_wide(h, s):
@@ -276,7 +283,7 @@ def tile_tensorproductrolefillerwrite_x2_kernel(
                 res[0] = sbt("res0", [P, PACK, R], F32)
             rows, cols = slice(2 * s, 2 * s + 2), slice(2 * CH * h, 2 * CH * (h + 1))
             nc.vector.scalar_tensor_tensor(out=res[0][:, rows, cols], in0=acc[0, h, s][:], scalar=1.0 / 32.0, in1=dm[0, "pair", s][:, :, cols], op0=ALU.mult, op1=ALU.add)
-            free_banks.append(held[0, h, s])
+            release(held[0, h, s], V)
             nc.sync.dma_start(out=out_0[0].rearrange("(p a) r -> p a r", a=PACK)[:, rows, cols], in_=res[0][:, rows, cols])
 
         def bind_cols(c, half):
@@ -289,18 +296,38 @@ def tile_tensorproductrolefillerwrite_x2_kernel(
             res[1, c] = sbt("res1_%d" % c, [P, PACK, CH], F32)
             nc.vector.scalar_tensor_tensor(out=res[1, c][:], in0=acc[1, c][:], scalar=1.0 / 32.0, in1=dm[1][:, :, CH * c:CH * (c + 1)],
                                            op0=ALU.mult, op1=ALU.add)
-            free_banks.append(held[1, c])
+            release(held[1, c], V)
             nc.sync.dma_start(out=out_0[1].rearrange("(p a) r -> p a r", a=PACK)[:, :, CH * c:CH * (c + 1)], in_=res[1, c][:])
 
-        def decay_last(s, tag=None):
+        def bind_late(h, s, half):
+            if half == 0:
+                held[1, h, s], acc[1, h, s] = next_bank("W%d%d" % (h, s), [P, 2, 2 * CH])
+            for e in range(2):
+                bind_pass(acc[1, h, s][:, e, :], 1, 2 * s + e, half, 2 * h, 2 * h + 2, half == 0 and e == 0, half == 1 and e == 1)
+
+        def finish_late(h, s):
             if s == 0:
+                res[1, "pair", h] = sbt("res1_pair%d" % h, [P, PACK, 2 * CH], F32)
+            rows, cols = slice(2 * s, 2 * s + 2), slice(2 * CH * h, 2 * CH * (h + 1))
+            nc.vector.scalar_tensor_tensor(out=res[1, "pair", h][:, rows, :], in0=acc[1, h, s][:], scalar=1.0 / 32.0, in1=dm[1][:, rows, cols], op0=ALU.mult, op1=ALU.add)
+            release(held[1, h, s], V)
+            nc.sync.dma_start(out=out_0[1].rearrange("(p a) r -> p a r", a=PACK)[:, rows, cols], in_=res[1, "pair", h][:, rows, :])
+
+        def decay_last(a0, a1, eng, tag=None):
+            if a0 == 0:
                 dm[1] = sbt("dm1", [P, PACK, R], F32, tag=tag)
-            nc.gpsimd.tensor_tensor(out=dm[1][:, 2 * s:2 * s + 2, :], in0=m_raw[1, s][:], in1=d_row[:].unsqueeze(1).to_broadcast([P, 2, R]), op=ALU.mult)
+            rows = m_raw[1, a0 // 2][:, a0 % 2:a0 % 2 + a1 - a0, :]
+            eng.tensor_tensor(out=dm[1][:, a0:a1, :], in0=rows, in1=d_row[:].unsqueeze(1).to_broadcast([P, a1 - a0, R]), op=ALU.mult)
 
         def round_out(b, c0, c1, eng):
             if b not in res_bf:
                 res_bf[b] = sbt("rb%d" % b, [P, R * PACK], BF16)
-            src = res[0][:, :, CH * c0:CH * c1] if b == 0 else res[1, c0][:]
+            if b == 0:
+                src = res[0][:, :, CH * c0:CH * c1]
+            elif (1, c0) in res:
+                src = res[1, c0][:]
+            else:
+                src = res[1, "pair", c0 // 2][:, :, CH * (c0 % 2):CH * (c0 % 2 + c1 - c0)]
             dst = res_bf[b][:, CH * PACK * c0:CH * PACK * c1]
             dst, src = dst.rearrange("p (n i a) -> p n a i", a=PACK, i=4), src.rearrange("p a (n i) -> p n a i", i=4)
             if eng is G:
@@ -362,8 +389,8 @@ def tile_tensorproductrolefillerwrite_x2_kernel(
         take(S, "xR10", "xR11")
         copy_g(2, S)
         quant_x(ROL, 1)
-        decay_last(0, "m0_1")
-        decay_last(1)
+        decay_last(0, 2, G, "m0_1")
+        decay_last(2, 4, G)
         rol_wide(0, 0, 0)
         rol_wide(0, 0, 1)
         take(S, "R000", "R001")
@@ -428,24 +455,26 @@ def tile_tensorproductrolefillerwrite_x2_kernel(
         quant_pair(1)
         quant_x_pair((ROL, 3), (FIL, 3))
         y_tiles(2, "y1")
-        newest_first(2)
+        newest_first(2, S)
         rol_wide(2, 0, 0)
         rol_wide(2, 0, 1)
         take(S, "R200", "R201")
         gate(2, 0, 2, G)
-        newest_first(2)
+        newest_first(2, V)
         rol_wide(2, 1, 0)
         rol_wide(2, 1, 1)
         take(S, "R211", "R210")
-        bind_wide(0, 0)
+        newest_first(3, S)
         fil(2, 0)
         fil(2, 1)
+        bind_wide(0, 0)
         take(S, "F21", "F20")
-        bind_wide(0, 1)
+        finish_wide(0, 0)
+        newest_first(2, S)
         fil(2, 2)
         fil(2, 3)
+        bind_wide(0, 1)
         take(S, "F23", "F22")
-        finish_wide(0, 0)
         gate(2, 2, 4, V)
         finish_wide(0, 1)
         rol_wide(3, 0, 0)
@@ -454,39 +483,43 @@ def tile_tensorproductrolefillerwrite_x2_kernel(
         take(S, "R301", "R300")
         finish_wide(1, 0)
         fil(3, 0)
-        bind_wide(1, 1)
         copy_g(3, V)
         quant_pair(2)
         gate(3, 1, 2, G)
-        gate(3, 0, 1, V)
+        newest_first(2, S)
         fil(3, 1)
         take(S, "F30", "F31")
         fil(3, 2)
         take(S, "F32")
         fil(3, 3)
         take(V, "F33")
+        gate(3, 0, 1, V)
         quant_y(FIL, 3)
         copy_g(3, V, "g_last")
         quant_y(ROL, 3, 0, 2)
-        finish_wide(1, 1)
+        newest_first(2, S)
         rol_narrow(3, 2)
         rol_narrow(3, 3)
+        bind_wide(1, 1)
+        finish_wide(1, 1)
         take(S, "R32", "R33")
-        for c in range(4):
-            bind_cols(c, 0)
-        bind_cols(0, 1)
-        bind_cols(1, 1)
+        newest_first(2, S)
+        bind_late(0, 0, 0)
+        bind_late(0, 1, 0)
+        bind_cols(2, 0)
+        bind_late(0, 0, 1)
+        bind_late(0, 1, 1)
+        bind_cols(3, 0)
         gate(3, 2, 3, G)
         gate(3, 3, 4, V)
-        finish_cols(0)
+        finish_late(0, 0)
         round_out(0, 0, 2, S)
         round_out(0, 2, 4, S)
         quant_y(ROL, 3, 2, 4)
         bind_cols(2, 1)
         bind_cols(3, 1)
-        finish_cols(1)
-        round_out(1, 0, 1, S)
-        round_out(1, 1, 2, S)
+        finish_late(0, 1)
+        round_out(1, 0, 2, S)
         quant_out(0, 0, 4)
         store_words(0, 4)
         finish_cols(2)

from contextlib import ExitStack

import concourse.mybir as mybir
from concourse.masks import make_identity

B, T, D, F, R = 2, 1024, 512, 512, 512
FLOPS = 2 * B * T * D * (F + R) + 2 * B * T * F * R

F32 = mybir.dt.float32
BF16 = mybir.dt.bfloat16
U32 = mybir.dt.uint32
I32 = mybir.dt.int32
U8 = mybir.dt.uint8
FP8X4 = mybir.dt.float8_e4m3fn_x4
FP4X4 = mybir.dt.float4_e2m1fn_x4
ACT = mybir.ActivationFunctionType
ALU = mybir.AluOpType

P = 128
PACK = 4
KP = P * PACK
CH = 128
NCH = 4
BANKS = 7
FIL, ROL = 0, 1


def tile_tensorproductrolefillerwrite_x2_kernel(
    tc, xf, xr, wf_words, wf_scales, wr_words, wr_scales, g, m0, decay, out_0, out_1, out_2
):
    nc = tc.nc
    with ExitStack() as ctx:
        sb = ctx.enter_context(tc.tile_pool(name="sb", bufs=1))
        ps = ctx.enter_context(tc.psum_pool(name="ps", bufs=1))
        ctx.enter_context(tc.manual_schedule())
        V, S, G = nc.vector, nc.scalar, nc.gpsimd

        def sbt(name, shape, dtype, tag=None):
            return sb.tile(shape, dtype, name=name, tag=tag or name, align_bytes=64)

        free_banks = list(range(BANKS))
        freed_by = {}
        waiting = {}
        held = {}

        def next_bank(name, shape):
            n = free_banks.pop(0)
            return n, ps.tile(shape, F32, name=name, tag="bank%d" % n)

        def newest_first(count, eng=None):
            picked = [n for n in free_banks if eng is None or freed_by.get(n) is eng][:count]
            free_banks[:] = picked[::-1] + [n for n in free_banks if n not in picked]

        def release(n, eng):
            freed_by[n] = eng
            free_banks.append(n)

        def take(eng, *keys):
            for key in keys:
                n, empty = waiting.pop(key)
                empty(eng)
                release(n, eng)

        def label(o, k):
            return "%s%d" % ("FR"[o], k)

        x_raw, x_t, x_q, x_s, y, th = {}, {}, {}, {}, {}, {}
        m_raw, dm, res, res_bf, g_sb, acc = {}, {}, {}, {}, {}, {}

        ident = sbt("ident", [P, P], F32)
        w_words = [sbt("ww%d" % o, [P, 2 * F], U8) for o in range(2)]
        w_scale = [sbt("ws%d" % o, [P, 4 * F], U8) for o in range(2)]
        g_rows = sbt("g_rows", [P, KP], BF16)
        d_col = sbt("d_col", [P, PACK], BF16)
        d_row = sbt("d_row", [P, R], BF16)
        o_q = sbt("o_q", [P, B * R], U32)
        o_s = sbt("o_s", [P, B * R], U8)
        consts = ps.tile([P, 4, P], F32, name="consts", tag="consts")

        def copy_on(eng, dst, src):
            if eng is V:
                nc.vector.tensor_copy(out=dst, in_=src)
            else:
                nc.scalar.copy(out=dst, in_=src)

        def x_rows(o, k):
            b, half = divmod(k, 2)
            return (xf, xr)[o][b, half * KP:(half + 1) * KP, :].rearrange("(p j) d -> p j d", j=PACK)

        def load_x_half(o, k, h):
            x_raw[o, k, h] = sbt("xraw%s_%d" % (label(o, k), h), [P, 2 * D], BF16)
            nc.sync.dma_start(out=x_raw[o, k, h][:].rearrange("p (j d) -> p j d", j=2), in_=x_rows(o, k)[:, 2 * h:2 * h + 2, :])

        def load_x(o, k):
            whole = sbt("xraw%s" % label(o, k), [P, PACK * D], BF16)
            nc.sync.dma_start(out=whole[:].rearrange("p (j d) -> p j d", j=PACK), in_=x_rows(o, k))
            for h in range(2):
                x_raw[o, k, h] = whole[:, 2 * D * h:2 * D * (h + 1)]

        def load_w(o, queue):
            queue.dma_start(out=w_words[o][:].bitcast(I32), in_=(wf_words, wr_words)[o][0].bitcast(I32))

        def load_ws(o, queue):
            src = (wf_scales, wr_scales)[o][0].bitcast(I32).rearrange("(q r) w -> r q w", r=4)
            queue.dma_start(out=w_scale[o][:].bitcast(I32)[0:4, :].rearrange("r (q w) -> r q w", q=4), in_=src)

        def spread_ws(o):
            words = w_scale[o][:].bitcast(I32)
            for q in range(1, 4):
                nc.vector.tensor_copy(out=words[32 * q:32 * q + 4, 0:F // 4], in_=words[0:4, q * F // 4:(q + 1) * F // 4])

        def load_m(b, h):
            m_raw[b, h] = sbt("m%d_%d" % (b, h), [P, 2, R], BF16)
            nc.sync.dma_start(out=m_raw[b, h][:], in_=m0[b].rearrange("(p j) r -> p j r", j=PACK)[:, 2 * h:2 * h + 2, :])

        def load_decay(queue):
            queue.dma_start(out=d_col[:], in_=decay.rearrange("(p j) -> p j", j=PACK))

        def load_g(queue):
            queue.dma_start(out=g_rows[0:4, :], in_=g.rearrange("b (h k) -> (b h) k", h=2))

        def turn_decay():
            for u in range(2):
                nc.tensor.transpose(consts[:, u, :], d_col[:].bitcast(F32)[:, u:u + 1].to_broadcast([P, P]), ident[:])

        def turn_g():
            for u in range(2):
                nc.tensor.transpose(consts[:, 2 + u, :], g_rows[:].bitcast(F32)[:, u:2 * P:2], ident[:])

        def copy_decay(eng):
            copy_on(eng, d_row[:].bitcast(F32).rearrange("p (m u) -> p m u", u=2), consts[:, 0:2, :].rearrange("p u m -> p m u"))

        def copy_g(k, eng, name="g_sb"):
            g_sb[k] = sbt("%s%d" % (name, k), [P, PACK], BF16)
            copy_on(eng, g_sb[k][:].bitcast(F32), consts[:, 2:4, k])

        def x_tile(name, groups, tag=None):
            tile = sbt("xt" + name, [P, len(groups) * KP * PACK], BF16, tag=tag)
            for s, group in enumerate(groups):
                x_t[group] = (tile, s)

        def turn_half(o, k, h):
            n, bank = next_bank("T%s%d" % (label(o, k), h), [P, 2, 2, P])
            words = x_raw[o, k, h][:].bitcast(F32)
            for j in range(2):
                for u in range(2):
                    nc.tensor.transpose(bank[:, j, u, :], words[:, 256 * j + u:256 * (j + 1):2], ident[:])
            if (o, k) not in x_t:
                x_tile(label(o, k), [(o, k)])
            tile, s = x_t[o, k]
            dst = tile[:].bitcast(F32)[:, 1024 * s + 512 * h:1024 * s + 512 * (h + 1)].rearrange("p (j m u) -> p j m u", j=2, u=2)
            waiting["x%s%d" % (label(o, k), h)] = (n, lambda eng: copy_on(eng, dst, bank[:].rearrange("p j u m -> p j m u")))

        def turn(o, k):
            for h in range(2):
                turn_half(o, k, h)

        def quant_x(o, k, h0=0, h1=2):
            if h0 == 0:
                x_q[o, k] = sbt("xq" + label(o, k), [P, KP], U32)
                x_s[o, k] = sbt("xs" + label(o, k), [P, KP], U8)
            tile, s = x_t[o, k]
            cols = slice(256 * h0, 256 * h1)
            nc.vector.quantize_mx(out=x_q[o, k][:, cols].bitcast(FP8X4), scales=x_s[o, k][:, cols], in_=tile[:, 2048 * s + 1024 * h0:2048 * s + 1024 * h1])

        def quant_x_pair(first, second):
            codes = sbt("xq" + label(*first) + label(*second), [P, 2 * KP], U32)
            scales = sbt("xs" + label(*first) + label(*second), [P, 2 * KP], U8)
            nc.vector.quantize_mx(out=codes[:].bitcast(FP8X4), scales=scales[:], in_=x_t[first][0][:])
            for s, group in enumerate((first, second)):
                x_q[group] = codes[:, KP * s:KP * (s + 1)]
                x_s[group] = scales[:, KP * s:KP * (s + 1)]

        def y_tiles(k, tag=None):
            y[k] = (sbt("y%d" % k, [P, 2 * F * PACK], BF16, tag=tag), sbt("yq%d" % k, [P, 2 * F], U32), sbt("ys%d" % k, [P, 2 * F], U8))

        def y_at(o, k, c0, c1):
            if k not in y:
                y_tiles(k)
            col, n = F * o + int(CH * c0), int(CH * (c1 - c0))
            values, codes, scales = y[k]
            return values[:, PACK * col:PACK * (col + n)], codes[:, col:col + n], scales[:, col:col + n]

        def quant_y(o, k, c0=0, c1=NCH):
            values, codes, scales = y_at(o, k, c0, c1)
            nc.vector.quantize_mx(out=codes.bitcast(FP8X4), scales=scales, in_=values)

        def quant_pair(k):
            quant_y(FIL, k, 0, 2 * NCH)

        def project(out, o, k, j, c0, c1):
            nc.tensor.matmul_mx(
                out=out,
                lhsT=x_q[o, k][:, P * j:P * (j + 1)].bitcast(FP8X4), lhsT_scale=x_s[o, k][:, P * j:P * (j + 1)],
                rhs=w_words[o][:, 2 * CH * c0:2 * CH * c1].bitcast(FP4X4), rhs_scale=w_scale[o][:, CH * c0:CH * c1],
                start=True, stop=True)

        def new_th(k, tag=None):
            th[k] = sbt("th%d" % k, [P, 2, R, 2], F32, tag=tag)

        def rol_wide(k, h, u):
            n, bank = next_bank("MR%d%d%d" % (k, h, u), [P, 2, 2 * CH])
            for e in range(2):
                project(bank[:, e, :], ROL, k, 2 * u + e, 2 * h, 2 * h + 2)
            if k not in th:
                new_th(k)
            waiting["R%d%d%d" % (k, h, u)] = (n, lambda eng: eng.activation(out=th[k][:, u, 2 * CH * h:2 * CH * (h + 1), :], in_=bank[:].rearrange("p e n -> p n e"), func=ACT.Tanh))

        def rol(k, halves=(0, 1)):
            for h in halves:
                for u in range(2):
                    rol_wide(k, h, u)

        def rol_narrow(k, c):
            n, bank = next_bank("MR%d%d" % (k, c), [P, PACK, CH])
            for j in range(PACK):
                project(bank[:, j, :], ROL, k, j, c, c + 1)
            if k not in th:
                new_th(k)
            waiting["R%d%d" % (k, c)] = (n, lambda eng: eng.activation(out=th[k][:, :, CH * c:CH * (c + 1), :].rearrange("p u n e -> p n u e"),
                                                                      in_=bank[:].rearrange("p (u e) n -> p n u e", u=2), func=ACT.Tanh))

        def fil(k, c):
            n, bank = next_bank("MF%d%d" % (k, c), [P, PACK, CH])
            for j in range(PACK):
                project(bank[:, j, :], FIL, k, j, c, c + 1)
            dst = y_at(FIL, k, 0, NCH)[0].rearrange("p (a m t) -> p a m t", a=PACK, t=PACK)[:, :, 32 * c:32 * (c + 1), :]
            waiting["F%d%d" % (k, c)] = (n, lambda eng: copy_on(eng, dst, bank[:].rearrange("p t (m a) -> p a m t", a=PACK)))

        def gate(k, c0, c1, eng):
            n = int(CH * (c1 - c0))
            dst = y_at(ROL, k, c0, c1)[0].rearrange("p (n u e) -> p n u e", u=2, e=2)
            src = th[k][:, :, int(CH * c0):int(CH * c1), :].rearrange("p u n e -> p n u e")
            if eng is G:
                strength = g_sb[k][:].rearrange("p (u e) -> p u e", u=2)
            else:
                strength = consts[:, 2:4, :].bitcast(BF16)[:, :, 2 * k:2 * k + 2]
            eng.tensor_tensor(out=dst, in0=src, in1=strength.unsqueeze(1).to_broadcast([P, n, 2, 2]), op=ALU.mult)

        def decay_rows(b, a0, a1, eng, tag=None):
            part = sbt("dm%d_%d" % (b, a0), [P, a1 - a0, R], F32, tag=tag)
            dm[b, "pair", a0 // 2] = part
            for a in range(a0, a1):
                dm[b, a] = part[:, a - a0, :]
            rows = m_raw[b, a0 // 2][:, a0 % 2:a0 % 2 + a1 - a0, :]
            eng.tensor_tensor(out=part[:], in0=rows, in1=d_row[:].unsqueeze(1).to_broadcast([P, a1 - a0, R]), op=ALU.mult)

        def decay_row_psum(a):
            if a % 2 == 0:
                dm[0, "pair", a // 2] = sbt("dm0_%d" % a, [P, 2, R], F32)
            row = m_raw[0, a // 2][:, a % 2, :]
            factor = consts[:, 0:2, :].bitcast(BF16).rearrange("p u (m e) -> p m u e", e=2)
            nc.vector.tensor_tensor(out=dm[0, "pair", a // 2][:, a % 2, :].rearrange("p (m u e) -> p m u e", u=2, e=2),
                                    in0=row.rearrange("p (m u e) -> p m u e", u=2, e=2), in1=factor, op=ALU.mult)

        def bind_pass(out, b, a, half, c0, c1, start, stop):
            k = 2 * b + half
            fil_codes, fil_scales = y_at(FIL, k, a, a + 1)[1:]
            rol_codes, rol_scales = y_at(ROL, k, c0, c1)[1:]
            nc.tensor.matmul_mx(out=out, lhsT=fil_codes.bitcast(FP8X4), lhsT_scale=fil_scales,
                                rhs=rol_codes.bitcast(FP8X4), rhs_scale=rol_scales, start=start, stop=stop)

        def bind_rows(a):
            held[0, a], acc[0, a] = next_bank("A%d" % a, [P, R])
            for half in range(2):
                bind_pass(acc[0, a][:], 0, a, half, 0, NCH, half == 0, half == 1)

        def finish_rows(a):
            if 0 not in res:
                res[0] = sbt("res0", [P, PACK, R], F32)
            nc.vector.scalar_tensor_tensor(out=res[0][:, a, :], in0=acc[0, a][:], scalar=1.0 / 32.0, in1=dm[0, a], op0=ALU.mult, op1=ALU.add)
            release(held[0, a], V)
            nc.sync.dma_start(out=out_0[0].rearrange("(p a) r -> p a r", a=PACK)[:, a, :], in_=res[0][:, a, :])

        def bind_wide(h, s):
            held[0, h, s], acc[0, h, s] = next_bank("A%d%d" % (h, s), [P, 2, 2 * CH])
            for e in range(2):
                for half in range(2):
                    bind_pass(acc[0, h, s][:, e, :], 0, 2 * s + e, half, 2 * h, 2 * h + 2, half == 0, half == 1)

        def finish_wide(h, s):
            if 0 not in res:
                res[0] = sbt("res0", [P, PACK, R], F32)
            rows, cols = slice(2 * s, 2 * s + 2), slice(2 * CH * h, 2 * CH * (h + 1))
            nc.vector.scalar_tensor_tensor(out=res[0][:, rows, cols], in0=acc[0, h, s][:], scalar=1.0 / 32.0, in1=dm[0, "pair", s][:, :, cols], op0=ALU.mult, op1=ALU.add)
            release(held[0, h, s], V)
            nc.sync.dma_start(out=out_0[0].rearrange("(p a) r -> p a r", a=PACK)[:, rows, cols], in_=res[0][:, rows, cols])

        def bind_cols(c, half):
            if half == 0:
                held[1, c], acc[1, c] = next_bank("B%d" % c, [P, PACK, CH])
            for a in range(PACK):
                bind_pass(acc[1, c][:, a, :], 1, a, half, c, c + 1, half == 0 and a == 0, half == 1 and a == PACK - 1)

        def finish_cols(c):
            res[1, c] = sbt("res1_%d" % c, [P, PACK, CH], F32)
            nc.vector.scalar_tensor_tensor(out=res[1, c][:], in0=acc[1, c][:], scalar=1.0 / 32.0, in1=dm[1][:, :, CH * c:CH * (c + 1)],
                                           op0=ALU.mult, op1=ALU.add)
            release(held[1, c], V)
            nc.sync.dma_start(out=out_0[1].rearrange("(p a) r -> p a r", a=PACK)[:, :, CH * c:CH * (c + 1)], in_=res[1, c][:])

        def bind_late(h, s, half):
            if half == 0:
                held[1, h, s], acc[1, h, s] = next_bank("W%d%d" % (h, s), [P, 2, 2 * CH])
            for e in range(2):
                bind_pass(acc[1, h, s][:, e, :], 1, 2 * s + e, half, 2 * h, 2 * h + 2, half == 0 and e == 0, half == 1 and e == 1)

        def finish_late(h, s):
            if s == 0:
                res[1, "pair", h] = sbt("res1_pair%d" % h, [P, PACK, 2 * CH], F32)
            rows, cols = slice(2 * s, 2 * s + 2), slice(2 * CH * h, 2 * CH * (h + 1))
            nc.vector.scalar_tensor_tensor(out=res[1, "pair", h][:, rows, :], in0=acc[1, h, s][:], scalar=1.0 / 32.0, in1=dm[1][:, rows, cols], op0=ALU.mult, op1=ALU.add)
            release(held[1, h, s], V)
            nc.sync.dma_start(out=out_0[1].rearrange("(p a) r -> p a r", a=PACK)[:, rows, cols], in_=res[1, "pair", h][:, rows, :])

        def decay_last(a0, a1, eng, tag=None):
            if a0 == 0:
                dm[1] = sbt("dm1", [P, PACK, R], F32, tag=tag)
            rows = m_raw[1, a0 // 2][:, a0 % 2:a0 % 2 + a1 - a0, :]
            eng.tensor_tensor(out=dm[1][:, a0:a1, :], in0=rows, in1=d_row[:].unsqueeze(1).to_broadcast([P, a1 - a0, R]), op=ALU.mult)

        def round_out(b, c0, c1, eng):
            if b not in res_bf:
                res_bf[b] = sbt("rb%d" % b, [P, R * PACK], BF16)
            if b == 0:
                src = res[0][:, :, CH * c0:CH * c1]
            elif (1, c0) in res:
                src = res[1, c0][:]
            else:
                src = res[1, "pair", c0 // 2][:, :, CH * (c0 % 2):CH * (c0 % 2 + c1 - c0)]
            dst = res_bf[b][:, CH * PACK * c0:CH * PACK * c1]
            dst, src = dst.rearrange("p (n i a) -> p n a i", a=PACK, i=4), src.rearrange("p a (n i) -> p n a i", i=4)
            if eng is G:
                nc.gpsimd.tensor_scalar(out=dst, in0=src, scalar1=1.0, scalar2=0.0, op0=ALU.mult, op1=ALU.add)
            else:
                copy_on(eng, dst, src)

        def quant_out(b, c0, c1):
            cols = slice(R * b + CH * c0, R * b + CH * c1)
            nc.vector.quantize_mx(out=o_q[:, cols].bitcast(FP8X4), scales=o_s[:, cols], in_=res_bf[b][:, CH * PACK * c0:CH * PACK * c1])

        def store_words(c0, c1):
            dst = out_1[0].rearrange("p m t -> p (m t)").bitcast(I32)
            nc.sync.dma_start(out=dst[:, CH * c0:CH * c1], in_=o_q[:].bitcast(I32)[:, CH * c0:CH * c1])

        def store_scales():
            for q in range(4):
                eng = nc.scalar if q % 2 else nc.sync
                eng.dma_start(out=out_2[0].bitcast(I32)[4 * q:4 * q + 4, :], in_=o_s[:].bitcast(I32)[32 * q:32 * q + 4, :])

        load_decay(nc.scalar)
        load_ws(ROL, nc.scalar)
        load_ws(FIL, nc.scalar)
        load_x_half(ROL, 0, 0)
        nc.vector.memset(g_rows[:].bitcast(I32), 0)
        load_g(nc.sync)
        load_x_half(ROL, 0, 1)
        load_x_half(FIL, 0, 0)
        load_x_half(FIL, 0, 1)
        load_m(0, 0)
        make_identity(nc, ident[:])
        load_x_half(ROL, 1, 0)
        load_x_half(ROL, 1, 1)
        load_w(ROL, nc.sync)
        load_m(0, 1)
        load_w(FIL, nc.sync)
        load_m(1, 0)
        load_x_half(FIL, 1, 0)
        load_x_half(FIL, 1, 1)
        load_m(1, 1)
        for o, k in ((ROL, 2), (FIL, 2), (ROL, 3), (FIL, 3)):
            load_x(o, k)

        turn_decay()
        turn(ROL, 0)
        copy_decay(V)
        spread_ws(ROL)
        spread_ws(FIL)
        take(S, "xR00", "xR01")
        quant_x(ROL, 0, 0, 1)
        turn_g()
        quant_x(ROL, 0, 1, 2)
        decay_rows(0, 0, 2, V)
        turn(FIL, 0)
        take(S, "xF00", "xF01")
        quant_x(FIL, 0)
        decay_rows(0, 2, 4, V)
        turn(ROL, 1)
        take(S, "xR10", "xR11")
        copy_g(2, S)
        quant_x(ROL, 1)
        decay_last(0, 2, G, "m0_1")
        decay_last(2, 4, G)
        rol_wide(0, 0, 0)
        rol_wide(0, 0, 1)
        take(S, "R000", "R001")
        fil(0, 0)
        take(V, "F00")
        newest_first(2)
        rol_wide(0, 1, 0)
        rol_wide(0, 1, 1)
        take(S, "R010", "R011")
        gate(0, 0, 2, V)
        newest_first(2)
        fil(0, 1)
        fil(0, 2)
        take(V, "F02")
        rol_wide(1, 0, 0)
        take(S, "F01", "R100")
        gate(0, 2, 4, V)
        newest_first(2)
        turn(FIL, 1)
        take(S, "xF10")
        take(V, "xF11")
        newest_first(2)
        rol_wide(1, 0, 1)
        fil(0, 3)
        take(S, "R101")
        take(V, "F03")
        newest_first(2)
        turn(ROL, 2)
        take(S, "xR20", "xR21")
        newest_first(2)
        rol_wide(1, 1, 0)
        rol_wide(1, 1, 1)
        take(S, "R110", "R111")
        newest_first(2)
        turn(FIL, 2)
        take(S, "xF20", "xF21")
        gate(1, 0, 1, V)
        quant_x(FIL, 1)
        quant_pair(0)
        copy_g(1, V)
        quant_x(ROL, 2)
        gate(1, 2.5, 4, G)
        gate(1, 1, 2.5, V)
        newest_first(2)
        fil(1, 0)
        take(S, "F10")
        fil(1, 1)
        take(V, "F11")
        newest_first(2)
        x_tile("p3", [(ROL, 3), (FIL, 3)])
        turn(ROL, 3)
        take(S, "xR30", "xR31")
        newest_first(2)
        fil(1, 2)
        take(V, "F12")
        fil(1, 3)
        take(S, "F13")
        newest_first(2)
        turn(FIL, 3)
        take(S, "xF30", "xF31")
        quant_x(FIL, 2)
        quant_pair(1)
        quant_x_pair((ROL, 3), (FIL, 3))
        y_tiles(2, "y1")
        newest_first(2, S)
        rol_wide(2, 0, 0)
        rol_wide(2, 0, 1)
        take(S, "R200", "R201")
        gate(2, 0, 2, G)
        newest_first(2, V)
        rol_wide(2, 1, 0)
        rol_wide(2, 1, 1)
        take(S, "R211", "R210")
        newest_first(3, S)
        fil(2, 0)
        fil(2, 1)
        bind_wide(0, 0)
        take(S, "F21", "F20")
        finish_wide(0, 0)
        newest_first(2, S)
        fil(2, 2)
        fil(2, 3)
        bind_wide(0, 1)
        take(S, "F23", "F22")
        gate(2, 2, 4, V)
        finish_wide(0, 1)
        rol_wide(3, 0, 0)
        bind_wide(1, 0)
        rol_wide(3, 0, 1)
        take(S, "R301", "R300")
        finish_wide(1, 0)
        fil(3, 0)
        copy_g(3, V)
        quant_pair(2)
        gate(3, 1, 2, G)
        newest_first(2, S)
        fil(3, 1)
        take(S, "F30", "F31")
        fil(3, 2)
        take(S, "F32")
        fil(3, 3)
        take(V, "F33")
        gate(3, 0, 1, V)
        quant_y(FIL, 3)
        copy_g(3, V, "g_last")
        quant_y(ROL, 3, 0, 2)
        newest_first(2, S)
        rol_narrow(3, 2)
        rol_narrow(3, 3)
        bind_wide(1, 1)
        finish_wide(1, 1)
        take(S, "R32", "R33")
        newest_first(2, S)
        bind_late(0, 0, 0)
        bind_late(0, 1, 0)
        bind_cols(2, 0)
        bind_late(0, 0, 1)
        bind_late(0, 1, 1)
        bind_cols(3, 0)
        gate(3, 2, 3, G)
        gate(3, 3, 4, V)
        finish_late(0, 0)
        round_out(0, 0, 2, S)
        round_out(0, 2, 4, S)
        quant_y(ROL, 3, 2, 4)
        bind_cols(2, 1)
        bind_cols(3, 1)
        finish_late(0, 1)
        round_out(1, 0, 2, S)
        quant_out(0, 0, 4)
        store_words(0, 4)
        finish_cols(2)
        round_out(1, 2, 3, S)
        finish_cols(3)
        quant_out(1, 0, 2)
        round_out(1, 3, 4, V)
        quant_out(1, 2, 3)
        quant_out(1, 3, 4)
        store_words(4, 8)
        store_scales()
